import numpy as np
import ml_dtypes


def mxq(x, axis, fmt="e4m3"):
    dtype, down = {"e4m3": (ml_dtypes.float8_e4m3fn, 7), "e5m2": (ml_dtypes.float8_e5m2, 14)}[fmt]
    v = np.moveaxis(np.asarray(x, np.float32).astype(ml_dtypes.bfloat16).astype(np.float64), axis, -1)
    blocks = v.reshape(v.shape[:-1] + (-1, 32))
    amax = np.abs(blocks).max(-1, keepdims=True)
    byte = np.maximum(np.where(amax > 0, np.frexp(amax)[1] - 1 + 127, 0) - down, 1)
    scale = np.exp2(byte - 127.0)
    codes = (blocks / scale).astype(np.float32).astype(dtype).astype(np.float64)
    return np.moveaxis((codes * scale).reshape(v.shape), -1, axis)


WIDE = False


def mx_kscale(k):
    if not WIDE:
        return np.ones(k)
    levels = np.array([10, -10, 5, -5, 0])
    if k % 512:
        return np.exp2(np.random.permutation(np.resize(levels, k // 32))).repeat(32)
    a = np.empty((k // 512, 16))
    for p in range(k // 512):
        a[p, :8] = np.random.permutation(np.resize(levels, 8))
        for g in range(8):
            far = levels[np.abs(levels - a[p, g]) >= 10]
            a[p, g + 8] = far[np.random.randint(len(far))]
    return np.exp2(a.ravel()).repeat(32)


def f64(x):
    return np.asarray(x).astype(np.float64)


def striped(idx):
    return np.tile(idx.reshape(-1, 16).T, (8, 1)).astype(np.uint16)


def unstriped(offs):
    return offs[:16].T.reshape(-1).astype(np.int64)


E2M1 = np.array([0.0, 0.5, 1.0, 1.5, 2.0, 3.0, 4.0, 6.0, -0.0, -0.5, -1.0, -1.5, -2.0, -3.0, -4.0, -6.0])


def pack_weight(w, fmt):
    k, n = w.shape
    w = f64(np.asarray(w, np.float32).astype(ml_dtypes.bfloat16)).reshape(k // 32, 32, n)
    amax = np.abs(w).max(1)
    if fmt == "e4m3":
        byte = np.frexp(amax)[1] - 1 + 127 - 7
    else:
        mant, ex = np.frexp(amax / 6.0)
        byte = np.where(mant > 0.5, ex, ex - 1) + 127
    byte = np.clip(np.where(amax > 0, byte, 1), 1, 254)
    scaled = (w * np.exp2(127.0 - byte)[:, None, :]).reshape(k, n).astype(np.float32)
    by_word = np.ascontiguousarray(scaled.reshape(k // 512, 128, 4, n).transpose(0, 1, 3, 2))
    if fmt == "e4m3":
        words = by_word.astype(ml_dtypes.float8_e4m3fn).view(np.uint8)
    else:
        c = by_word.astype(ml_dtypes.float4_e2m1fn).view(np.uint8) & 0xF
        words = (c[..., 0::2] | (c[..., 1::2] << 4)).reshape(k // 512, 128, 2 * n)
    return np.ascontiguousarray(words), np.ascontiguousarray(byte.astype(np.uint8).reshape(k // 512, 16, n))


def unpack_weight(words, scales, fmt):
    g, _, n = scales.shape
    words = np.ascontiguousarray(words).reshape(g, 128, n, -1)
    if fmt == "e4m3":
        vals = words.view(ml_dtypes.float8_e4m3fn).astype(np.float64)
    else:
        nib = np.empty((g, 128, n, 4), np.uint8)
        nib[..., 0::2] = words & 0xF
        nib[..., 1::2] = words >> 4
        vals = E2M1[nib]
    vals = vals * np.repeat(np.exp2(scales.astype(np.float64) - 127.0), 8, axis=1)[..., None]
    return vals.transpose(0, 1, 3, 2).reshape(g * 512, n)


def gelu(v):
    return 0.5 * v * (1.0 + np.tanh(np.sqrt(2.0 / np.pi) * (v + 0.044715 * v**3)))


K, T, S, T2, P, H, N = 512, 4096, 1024, 2048, 1024, 1024, 512


def setup_inputs():
    n = np.random.standard_normal
    s = mx_kscale(K)[:, None]
    u = mx_kscale(H)[:, None]
    tab_words, tab_scales = pack_weight(n((K, T)) * s, "e4m3")
    wa_words, wa_scales = pack_weight(n((K, H)) / np.sqrt(K) / s, "e2m1")
    wc_words, wc_scales = pack_weight(n((K, H)) / np.sqrt(K) / s, "e4m3")
    return {
        "tab_words": tab_words, "tab_scales": tab_scales,
        "wa_words": wa_words, "wa_scales": wa_scales,
        "wb": (n((K, H)) / np.sqrt(K) / s).astype(np.float32),
        "wc_words": wc_words, "wc_scales": wc_scales,
        "wgs": np.exp(0.3 * n((128, S))).astype(np.float32),
        "stiff": (np.exp(0.4 * n((H, P))) * u).astype(np.float32),
        "wd": (n((H, N)) / np.sqrt(H) / u).astype(np.float32),
        "offs": striped(np.random.permutation(T)[:S]),
        "offs2": striped(np.random.permutation(T2)[:S]),
        "offs3": striped(np.random.permutation(T2)[:P]),
        "offs4": striped(np.random.permutation(T2)[:P]),
    }


def reference(tab_words, tab_scales, wa_words, wa_scales, wb, wc_words, wc_scales,
              wgs, stiff, wd, offs, offs2, offs3, offs4):
    v = unpack_weight(tab_words, tab_scales, "e4m3")[:, unstriped(offs)]
    wa = unpack_weight(wa_words, wa_scales, "e2m1")
    wc = unpack_weight(wc_words, wc_scales, "e4m3")
    a = wa.T @ v
    b = mxq(f64(wb), 0, "e4m3").T @ v
    c = wc.T @ v
    h = a * (1.0 / (1.0 + np.exp(-b))) + c
    page = np.zeros((H, T2))
    page[:, unstriped(offs2)] = np.tile(f64(wgs), (H // 128, 1)) * h
    x1 = page[:, unstriped(offs3)]
    x2 = page[:, unstriped(offs4)]
    z = (1.0 + x1 - x2) * f64(stiff)
    return mxq(f64(wd), 0, "e4m3").T @ mxq(z, 0, "e4m3")

@@ -1,0 +1,282 @@
+from contextlib import ExitStack
+
+import concourse.mybir as mybir
+from concourse.masks import make_identity
+
+K, T, S, T2, F, H, N = 512, 4096, 1024, 2048, 1024, 1024, 512
+FLOPS = 2 * (3 * K * H * S + H * N * F)
+
+F32 = mybir.dt.float32
+BF16 = mybir.dt.bfloat16
+I32 = mybir.dt.int32
+U32 = mybir.dt.uint32
+U16 = mybir.dt.uint16
+U8 = mybir.dt.uint8
+FP8X4 = mybir.dt.float8_e4m3fn_x4
+FP4X4 = mybir.dt.float4_e2m1fn_x4
+MULT = mybir.AluOpType.mult
+ADD = mybir.AluOpType.add
+SIGMOID = mybir.ActivationFunctionType.Sigmoid
+
+P = 128
+HALF = 512
+BLOCKS = HALF // P
+SLICES = H // P
+PER_PASS = 4
+WB_CHUNKS = ((0, 128), (128, 256), (256, 512), (512, 1024))
+
+
+def tile_list_bone_face_features_kernel(
+    tc, tab_words, tab_scales, wa_words, wa_scales, wb, wc_words, wc_scales,
+    wgs, stiff, wd, offs, offs2, offs3, offs4, out,
+):
+    nc = tc.nc
+    with ExitStack() as ctx:
+        lists = ctx.enter_context(tc.tile_pool(name="lists", bufs=1))
+        sb = ctx.enter_context(tc.tile_pool(name="sb", bufs=1))
+        ps = ctx.enter_context(tc.psum_pool(name="ps", bufs=1))
+
+        def tiles(name, count, shape, dtype):
+            return [sb.tile(shape, dtype, name="%s%d" % (name, i), align_bytes=64) for i in range(count)]
+
+        def one(name, shape, dtype):
+            return sb.tile(shape, dtype, name=name, align_bytes=64)
+
+        idx1 = lists.tile([P, S // 16], U16, name="idx1")
+        idx2 = lists.tile([P, S // 16], U16, name="idx2")
+        idx3 = lists.tile([P, F // 16], U16, name="idx3")
+        idx4 = lists.tile([P, F // 16], U16, name="idx4")
+
+        def half_of(idx, h):
+            return idx[:, h * (HALF // 16) : (h + 1) * (HALF // 16)]
+
+        banks = [ps.tile([P, HALF], F32, name="bank%d" % i) for i in range(8)]
+        bank_a, bank_b0, bank_b1, bank_c, bank_d0, bank_d1, bank_o0, bank_o1 = banks
+        bank_d = (bank_d0, bank_d1)
+
+        ident = one("ident", [P, P], F32)
+        tab_w = one("tab_w", [P, T], U32)
+        tab_s = one("tab_s", [P, T], U8)
+        v_w = tiles("v_w", 2, [P, HALF], U32)
+        v_s = one("v_s", [P, S], U8)
+        wa_w = one("wa_w", [P, 2 * H], U8)
+        wc_w = one("wc_w", [P, H], U32)
+        wa_s = one("wa_s", [P, H], U8)
+        wc_s = one("wc_s", [P, H], U8)
+        wb_raw = [one("wb_raw%d" % i, [P, 4, c1 - c0], F32) for i, (c0, c1) in enumerate(WB_CHUNKS)]
+        w_bf = one("w_bf", [P, 4 * H], BF16)
+        wb_w = one("wb_w", [P, H], U32)
+        wb_s = one("wb_s", [P, H], U8)
+        wd_w = one("wd_w", [P, 2 * N], U32)
+        wd_s = one("wd_s", [P, 2 * N], U8)
+        wgs_sb = one("wgs_sb", [P, S], F32)
+        pages = tiles("page", PER_PASS, [P, T2], F32)
+        gate = tiles("gate", 2, [P, HALF], F32)
+        resp = tiles("resp", 2, [P, HALF], F32)
+        plain = tiles("plain", 2, [P, HALF], F32)
+        h_sb = tiles("h_sb", 2, [P, HALF], F32)
+        put = tiles("put", 2, [P, S], F32)
+        inner = tiles("inner", 2, [P, HALF], F32)
+        outer = tiles("outer", 2, [P, HALF], F32)
+        jump = tiles("jump", 2, [P, HALF], F32)
+        stiff_sb = tiles("stiff_sb", 2, [P, F], F32)
+        stiff_t = tiles("stiff_t", PER_PASS, [P, F], F32)
+        z_t = tiles("z_t", 2, [P, BLOCKS * HALF], BF16)
+        z_bf = one("z_bf", [P, 4 * F], BF16)
+        z_w = tiles("z_w", 2, [P, F], U32)
+        z_s = tiles("z_s", 2, [P, F], U8)
+        staged = tiles("staged", 4, [P, HALF], F32)
+
+        nc.vector.memset(tab_s[:].bitcast(I32), 0)
+        nc.gpsimd.memset(wa_s[:].bitcast(I32), 0)
+        nc.vector.memset(wc_s[:].bitcast(I32), 0)
+        nc.sync.dma_start(idx1[:], offs)
+        nc.sync.dma_start(out=tab_w[:].bitcast(I32), in_=tab_words[0].rearrange("p n t -> p (n t)").bitcast(I32))
+        for q in range(4):
+            nc.scalar.dma_start(out=tab_s[32 * q : 32 * q + 4, :].bitcast(I32),
+                                in_=tab_scales[0][4 * q : 4 * q + 4, :].bitcast(I32))
+        for q in range(4):
+            nc.gpsimd.dma_start(out=wa_s[32 * q : 32 * q + 4, :].bitcast(I32),
+                                in_=wa_scales[0][4 * q : 4 * q + 4, :].bitcast(I32))
+        wb_rows = wb.rearrange("(p j) c -> p j c", j=4)
+
+        def load_wb(i):
+            c0, c1 = WB_CHUNKS[i]
+            nc.sync.dma_start(out=wb_raw[i][:], in_=wb_rows[:, :, c0:c1])
+
+        def interleave(dst, raw):
+            nc.scalar.copy(out=dst.rearrange("p (c i t) -> p c t i", i=4, t=4),
+                           in_=raw.rearrange("p t (c i) -> p c t i", i=4))
+
+        def quantise_wb(i):
+            c0, c1 = WB_CHUNKS[i]
+            interleave(w_bf[:, 4 * c0 : 4 * c1], wb_raw[i][:])
+            nc.vector.quantize_mx(out=wb_w[:, c0:c1].bitcast(FP8X4), scales=wb_s[:, c0:c1],
+                                  in_=w_bf[:, 4 * c0 : 4 * c1])
+
+        load_wb(0)
+        nc.sync.dma_start(out=wa_w[:].bitcast(I32), in_=wa_words[0].bitcast(I32))
+        nc.sync.dma_start(out=wc_w[:].bitcast(I32), in_=wc_words[0].rearrange("p n t -> p (n t)").bitcast(I32))
+        for q in range(4):
+            nc.sync.dma_start(out=wc_s[32 * q : 32 * q + 4, :].bitcast(I32),
+                              in_=wc_scales[0][4 * q : 4 * q + 4, :].bitcast(I32))
+        nc.sync.dma_start(idx2[:], offs2)
+        nc.sync.dma_start(out=wgs_sb[:], in_=wgs)
+        load_wb(1)
+        nc.sync.dma_start(idx3[:], offs3)
+        nc.sync.dma_start(idx4[:], offs4)
+        load_wb(2)
+        load_wb(3)
+
+        make_identity(nc, ident[:])
+        nc.vector.memset(pages[0][:], 0.0)
+        nc.gpsimd.memset(pages[1][:], 0.0)
+        nc.gpsimd.memset(pages[2][:], 0.0)
+        nc.gpsimd.memset(pages[3][:], 0.0)
+
+        nc.vector.tensor_copy(v_s[:], tab_s[:].indirect(idx1[:]))
+        nc.vector.tensor_copy(v_w[0][:], tab_w[:].indirect(half_of(idx1, 0)))
+        quantise_wb(0)
+        nc.vector.tensor_copy(v_w[1][:], tab_w[:].indirect(half_of(idx1, 1)))
+
+        def block(i):
+            return slice(i * P, (i + 1) * P)
+
+        def add_transposed(bank, x, y):
+            for i in range(BLOCKS):
+                nc.tensor.matmul(bank[:, block(i)], x[:, block(i)], ident[:], start=True, stop=False, is_transpose=True)
+                nc.tensor.matmul(bank[:, block(i)], y[:, block(i)], ident[:], start=False, stop=True, is_transpose=True)
+
+        def respond(s, h, direct):
+            k = h
+            bank_b = (bank_b0, bank_b1)[h]
+            bank_h = bank_d[h]
+            for bank, codes, scales in (
+                (bank_b, wb_w[:, block(s)].bitcast(FP8X4), wb_s[:, block(s)]),
+                (bank_a, wa_w[:, 2 * P * s : 2 * P * (s + 1)].bitcast(FP4X4), wa_s[:, block(s)]),
+                (bank_c, wc_w[:, block(s)].bitcast(FP8X4), wc_s[:, block(s)]),
+            ):
+                for i in range(BLOCKS):
+                    nc.tensor.matmul_mx(out=bank[:, block(i)], lhsT=v_w[h][:, block(i)].bitcast(FP8X4),
+                                        lhsT_scale=v_s[:, block(BLOCKS * h + i)], rhs=codes, rhs_scale=scales,
+                                        start=True, stop=True)
+            cols = slice(h * HALF, (h + 1) * HALF)
+            nc.scalar.activation(gate[k][:], bank_b[:], SIGMOID)
+            if direct:
+                nc.vector.tensor_tensor(resp[k][:], bank_a[:], gate[k][:], MULT)
+                nc.scalar.copy(plain[k][:], bank_c[:])
+                add_transposed(bank_h, resp[k], plain[k])
+                nc.scalar.copy(put[s % 2][:, cols], bank_h[:])
+            else:
+                nc.scalar.copy(resp[k][:], bank_a[:])
+                nc.scalar.copy(plain[k][:], bank_c[:])
+                nc.gpsimd.tensor_tensor(gate[k][:], resp[k][:], gate[k][:], MULT)
+                add_transposed(bank_h, gate[k], plain[k])
+                nc.scalar.copy(h_sb[k][:], bank_h[:])
+                nc.gpsimd.tensor_tensor(put[s % 2][:, cols], h_sb[k][:], wgs_sb[:, cols], MULT)
+
+        def turn_stiff(s):
+            nc.sync.dma_start(out=stiff_sb[s % 2][:], in_=stiff[block(s), :])
+            for h in range(2):
+                for i in range(BLOCKS):
+                    nc.tensor.transpose(bank_d[h][:, block(i)], stiff_sb[s % 2][:, block(BLOCKS * h + i)], ident[:])
+                nc.scalar.copy(stiff_t[s % PER_PASS][:, h * HALF : (h + 1) * HALF], bank_d[h][:])
+
+        def fetch(s, h, x1, x2):
+            page = pages[s % PER_PASS]
+            nc.vector.tensor_scalar(x2, page[:].indirect(half_of(idx4, h)), -1.0, 1.0, MULT, ADD)
+            nc.vector.tensor_copy(x1, page[:].indirect(half_of(idx3, h)))
+
+        def combine(s, h, x1, x2, k, direct):
+            add_transposed(bank_d[k], x2, x1)
+            dst = z_t[h][:].rearrange("p (b r) -> p b r", b=BLOCKS)[:, :, block(s % PER_PASS)]
+            factor = stiff_t[s % PER_PASS][:, h * HALF : (h + 1) * HALF].rearrange("p (b r) -> p b r", b=BLOCKS)
+            if direct:
+                nc.vector.tensor_tensor(dst, bank_d[k][:].rearrange("p (b r) -> p b r", b=BLOCKS), factor, MULT)
+            else:
+                nc.scalar.copy(jump[k][:], bank_d[k][:])
+                nc.gpsimd.tensor_tensor(dst, jump[k][:].rearrange("p (b r) -> p b r", b=BLOCKS), factor, MULT)
+
+        def turn_back(h, pair_banks):
+            words = z_t[h][:].bitcast(F32)
+            z_words = z_bf[:].bitcast(F32)
+            for pair in range(2):
+                bank = pair_banks[pair]
+                for b in range(2):
+                    base = (2 * pair + b) * 256
+                    for u in range(2):
+                        nc.tensor.transpose(bank[:, block(2 * b + u)], words[:, base + u : base + 256 : 2], ident[:])
+                first = 2 * (h * HALF + pair * 256)
+                nc.scalar.copy(out=z_words[:, first : first + 512].rearrange("p (b m u) -> p b m u", b=2, u=2),
+                               in_=bank[:].rearrange("p (b u m) -> p b m u", b=2, u=2))
+
+        def quantise_z(g, m0, m1):
+            nc.vector.quantize_mx(out=z_w[g][:, m0:m1].bitcast(FP8X4), scales=z_s[g][:, m0:m1],
+                                  in_=z_bf[:, 4 * m0 : 4 * m1])
+
+        def features(h, out_banks, last):
+            cols = slice(h * HALF, (h + 1) * HALF)
+            for nb in range(N // P):
+                bank = out_banks[nb % len(out_banks)]
+                for g in range(2):
+                    w_cols = slice(g * N + nb * P, g * N + (nb + 1) * P)
+                    nc.tensor.matmul_mx(out=bank[:], lhsT=wd_w[:, w_cols].bitcast(FP8X4), lhsT_scale=wd_s[:, w_cols],
+                                        rhs=z_w[g][:, cols].bitcast(FP8X4), rhs_scale=z_s[g][:, cols],
+                                        start=(g == 0), stop=(g == 1))
+                if last and nb % 2 == 1:
+                    nc.vector.tensor_copy(staged[nb][:], bank[:])
+                else:
+                    nc.scalar.copy(staged[nb][:], bank[:])
+                nc.sync.dma_start(out=out[block(nb), cols], in_=staged[nb][:])
+
+        def load_wd(g):
+            nc.sync.dma_start(out=wb_raw[3][:], in_=wd[g * K : (g + 1) * K, :].rearrange("(p j) c -> p j c", j=4))
+            interleave(w_bf[:, 4 * g * N : 4 * (g + 1) * N], wb_raw[3][:])
+
+        for h in range(2):
+            respond(0, h, True)
+            cols = slice(h * HALF, (h + 1) * HALF)
+            nc.vector.tensor_tensor(pages[0][:].indirect(half_of(idx2, h)), put[0][:, cols], wgs_sb[:, cols], MULT)
+        quantise_wb(1)
+        respond(1, 0, False)
+        respond(1, 1, False)
+        quantise_wb(2)
+        turn_stiff(0)
+
+        for s in range(SLICES):
+            if s > 0:
+                nc.vector.tensor_copy(pages[s % PER_PASS][:].indirect(idx2[:]), put[s % 2][:])
+            halves = range(2) if s < PER_PASS else range(1)
+            for h in halves:
+                k = h if s < PER_PASS else s % 2
+                fetch(s, h, inner[k][:], outer[k][:])
+            if s == 0:
+                quantise_wb(3)
+            if s + 2 < SLICES:
+                respond(s + 2, 0, False)
+                respond(s + 2, 1, False)
+            if s + 1 < SLICES:
+                turn_stiff(s + 1)
+            for h in halves:
+                k = h if s < PER_PASS else s % 2
+                combine(s, h, inner[k][:], outer[k][:], k, False)
+            if s in (1, 2):
+                load_wd(s - 1)
+            if s == PER_PASS - 1:
+                nc.vector.quantize_mx(out=wd_w[:].bitcast(FP8X4), scales=wd_s[:], in_=w_bf[:])
+                for h in range(2):
+                    turn_back(h, bank_d)
+            if s == PER_PASS:
+                quantise_z(0, 0, F)
+
+        turn_back(0, (bank_b0, bank_c))
+        for s in range(PER_PASS, SLICES):
+            x1, x2 = put[s % 2][:, 0:HALF], put[s % 2][:, HALF:S]
+            fetch(s, 1, x1, x2)
+            if s == PER_PASS:
+                quantise_z(1, 0, HALF)
+                features(0, (bank_o0, bank_o1), False)
+            combine(s, 1, x1, x2, s % 2, s == SLICES - 1)
+        turn_back(1, (bank_b0, bank_c))
+        quantise_z(1, HALF, F)
+        features(1, (bank_a, bank_b1, bank_o1, bank_o0), True)

@@ -53,12 +53,13 @@ def tile_list_bone_face_features_kernel(
         banks = [ps.tile([P, HALF], F32, name="bank%d" % i) for i in range(8)]
         bank_a, bank_b0, bank_b1, bank_c, bank_d0, bank_d1, bank_o0, bank_o1 = banks
         bank_d = (bank_d0, bank_d1)
+        bank_o = (bank_o0, bank_o1)
 
         ident = one("ident", [P, P], F32)
         tab_w = one("tab_w", [P, T], U32)
         tab_s = one("tab_s", [P, T], U8)
         v_w = tiles("v_w", 2, [P, HALF], U32)
-        v_s = one("v_s", [P, S], U8)
+        v_s = tiles("v_s", 2, [P, HALF], U8)
         wa_w = one("wa_w", [P, 2 * H], U8)
         wc_w = one("wc_w", [P, H], U32)
         wa_s = one("wa_s", [P, H], U8)
@@ -70,7 +71,8 @@ def tile_list_bone_face_features_kernel(
         wd_w = one("wd_w", [P, 2 * N], U32)
         wd_s = one("wd_s", [P, 2 * N], U8)
         wgs_sb = one("wgs_sb", [P, S], F32)
-        pages = tiles("page", PER_PASS, [P, T2], F32)
+        pages = tiles("page", 3, [P, T2], F32)
+        page_of = [pages[i] for i in (0, 1, 0, 1, 0, 1, 2, 1)]
         gate = tiles("gate", 2, [P, HALF], F32)
         resp = tiles("resp", 2, [P, HALF], F32)
         plain = tiles("plain", 2, [P, HALF], F32)
@@ -78,205 +80,247 @@ def tile_list_bone_face_features_kernel(
         put = tiles("put", 2, [P, S], F32)
         inner = tiles("inner", 2, [P, HALF], F32)
         outer = tiles("outer", 2, [P, HALF], F32)
-        jump = tiles("jump", 2, [P, HALF], F32)
+        jump = tiles("jump", 3, [P, HALF], F32)
         stiff_sb = tiles("stiff_sb", 2, [P, F], F32)
-        stiff_t = tiles("stiff_t", PER_PASS, [P, F], F32)
+        stiff_t = tiles("stiff_t", SLICES, [P, F], F32)
         z_t = tiles("z_t", 2, [P, BLOCKS * HALF], BF16)
-        z_bf = one("z_bf", [P, 4 * F], BF16)
+        z_words = one("z_words", [P, 2 * F], F32)
         z_w = tiles("z_w", 2, [P, F], U32)
         z_s = tiles("z_s", 2, [P, F], U8)
-        staged = tiles("staged", 4, [P, HALF], F32)
+        staged = tiles("staged", 4, [P, F], F32)
 
-        nc.vector.memset(tab_s[:].bitcast(I32), 0)
+        nc.vector.memset(tab_s[:, 0 : T // 2].bitcast(I32), 0)
+        nc.gpsimd.memset(tab_s[:, T // 2 : T].bitcast(I32), 0)
         nc.gpsimd.memset(wa_s[:].bitcast(I32), 0)
         nc.vector.memset(wc_s[:].bitcast(I32), 0)
-        nc.sync.dma_start(idx1[:], offs)
-        nc.sync.dma_start(out=tab_w[:].bitcast(I32), in_=tab_words[0].rearrange("p n t -> p (n t)").bitcast(I32))
-        for q in range(4):
-            nc.scalar.dma_start(out=tab_s[32 * q : 32 * q + 4, :].bitcast(I32),
-                                in_=tab_scales[0][4 * q : 4 * q + 4, :].bitcast(I32))
-        for q in range(4):
-            nc.gpsimd.dma_start(out=wa_s[32 * q : 32 * q + 4, :].bitcast(I32),
-                                in_=wa_scales[0][4 * q : 4 * q + 4, :].bitcast(I32))
         wb_rows = wb.rearrange("(p j) c -> p j c", j=4)
 
         def load_wb(i):
             c0, c1 = WB_CHUNKS[i]
             nc.sync.dma_start(out=wb_raw[i][:], in_=wb_rows[:, :, c0:c1])
 
-        def interleave(dst, raw):
-            nc.scalar.copy(out=dst.rearrange("p (c i t) -> p c t i", i=4, t=4),
-                           in_=raw.rearrange("p t (c i) -> p c t i", i=4))
+        nc.sync.dma_start(idx1[:], offs)
+        load_wb(0)
+        for q in range(4):
+            nc.sync.dma_start(out=tab_s[32 * q : 32 * q + 4, :].bitcast(I32),
+                              in_=tab_scales[0][4 * q : 4 * q + 4, :].bitcast(I32))
+        nc.sync.dma_start(out=tab_w[:].bitcast(I32), in_=tab_words[0].rearrange("p n t -> p (n t)").bitcast(I32))
+        for q in range(4):
+            nc.gpsimd.dma_start(out=wa_s[32 * q : 32 * q + 4, :].bitcast(I32),
+                                in_=wa_scales[0][4 * q : 4 * q + 4, :].bitcast(I32))
+
+        def interleave(dst, raw, copy):
+            copy(out=dst.rearrange("p (c i t) -> p c t i", i=4, t=4), in_=raw.rearrange("p t (c i) -> p c t i", i=4))
 
         def quantise_wb(i):
             c0, c1 = WB_CHUNKS[i]
-            interleave(w_bf[:, 4 * c0 : 4 * c1], wb_raw[i][:])
+            interleave(w_bf[:, 4 * c0 : 4 * c1], wb_raw[i][:], nc.vector.tensor_copy if i == 0 else nc.scalar.copy)
             nc.vector.quantize_mx(out=wb_w[:, c0:c1].bitcast(FP8X4), scales=wb_s[:, c0:c1],
                                   in_=w_bf[:, 4 * c0 : 4 * c1])
 
-        load_wb(0)
         nc.sync.dma_start(out=wa_w[:].bitcast(I32), in_=wa_words[0].bitcast(I32))
         nc.sync.dma_start(out=wc_w[:].bitcast(I32), in_=wc_words[0].rearrange("p n t -> p (n t)").bitcast(I32))
         for q in range(4):
             nc.sync.dma_start(out=wc_s[32 * q : 32 * q + 4, :].bitcast(I32),
                               in_=wc_scales[0][4 * q : 4 * q + 4, :].bitcast(I32))
+        load_wb(1)
         nc.sync.dma_start(idx2[:], offs2)
         nc.sync.dma_start(out=wgs_sb[:], in_=wgs)
-        load_wb(1)
+        load_wb(2)
         nc.sync.dma_start(idx3[:], offs3)
         nc.sync.dma_start(idx4[:], offs4)
-        load_wb(2)
         load_wb(3)
 
         make_identity(nc, ident[:])
-        nc.vector.memset(pages[0][:], 0.0)
-        nc.gpsimd.memset(pages[1][:], 0.0)
-        nc.gpsimd.memset(pages[2][:], 0.0)
-        nc.gpsimd.memset(pages[3][:], 0.0)
+        for page in pages[:2]:
+            nc.vector.memset(page[:], 0.0)
+        for page in pages[2:]:
+            nc.gpsimd.memset(page[:], 0.0)
 
-        nc.vector.tensor_copy(v_s[:], tab_s[:].indirect(idx1[:]))
-        nc.vector.tensor_copy(v_w[0][:], tab_w[:].indirect(half_of(idx1, 0)))
         quantise_wb(0)
-        nc.vector.tensor_copy(v_w[1][:], tab_w[:].indirect(half_of(idx1, 1)))
+        for h in range(2):
+            nc.vector.tensor_copy(v_s[h][:], tab_s[:].indirect(half_of(idx1, h)))
+            nc.vector.tensor_copy(v_w[h][:], tab_w[:].indirect(half_of(idx1, h)))
 
         def block(i):
             return slice(i * P, (i + 1) * P)
 
-        def add_transposed(bank, x, y):
-            for i in range(BLOCKS):
+        def add_transposed(bank, x, y, b0, b1):
+            for i in range(b0, b1):
                 nc.tensor.matmul(bank[:, block(i)], x[:, block(i)], ident[:], start=True, stop=False, is_transpose=True)
                 nc.tensor.matmul(bank[:, block(i)], y[:, block(i)], ident[:], start=False, stop=True, is_transpose=True)
 
-        def respond(s, h, direct):
-            k = h
-            bank_b = (bank_b0, bank_b1)[h]
-            bank_h = bank_d[h]
-            for bank, codes, scales in (
-                (bank_b, wb_w[:, block(s)].bitcast(FP8X4), wb_s[:, block(s)]),
-                (bank_a, wa_w[:, 2 * P * s : 2 * P * (s + 1)].bitcast(FP4X4), wa_s[:, block(s)]),
-                (bank_c, wc_w[:, block(s)].bitcast(FP8X4), wc_s[:, block(s)]),
-            ):
+        def weights(s):
+            return (
+                (wb_w[:, block(s)].bitcast(FP8X4), wb_s[:, block(s)]),
+                (wa_w[:, 2 * P * s : 2 * P * (s + 1)].bitcast(FP4X4), wa_s[:, block(s)]),
+                (wc_w[:, block(s)].bitcast(FP8X4), wc_s[:, block(s)]),
+            )
+
+        def respond_first(h):
+            cols = slice(h * HALF, (h + 1) * HALF)
+            first_b, first_a, first_c = ((bank_b0, bank_a, bank_c), (bank_b1, bank_o0, bank_o1))[h]
+            for bank, (codes, scales) in zip((first_b, first_a, first_c), weights(0)):
+                nc.tensor.matmul_mx(out=bank[:], lhsT=codes, lhsT_scale=scales, rhs=v_w[h][:].bitcast(FP8X4),
+                                    rhs_scale=v_s[h][:], start=True, stop=True)
+            nc.scalar.activation(jump[h][:], first_b[:], SIGMOID)
+            nc.vector.tensor_tensor(inner[h][:], first_a[:], jump[h][:], MULT)
+            nc.vector.tensor_tensor(put[0][:, cols], first_c[:], inner[h][:], ADD)
+            nc.vector.tensor_tensor(pages[0][:].indirect(half_of(idx2, h)), put[0][:, cols], wgs_sb[:, cols], MULT)
+
+        def respond(s, h):
+            for bank, (codes, scales) in zip(((bank_b0, bank_b1)[h], bank_a, bank_c), weights(s)):
                 for i in range(BLOCKS):
                     nc.tensor.matmul_mx(out=bank[:, block(i)], lhsT=v_w[h][:, block(i)].bitcast(FP8X4),
-                                        lhsT_scale=v_s[:, block(BLOCKS * h + i)], rhs=codes, rhs_scale=scales,
+                                        lhsT_scale=v_s[h][:, block(i)], rhs=codes, rhs_scale=scales,
                                         start=True, stop=True)
             cols = slice(h * HALF, (h + 1) * HALF)
-            nc.scalar.activation(gate[k][:], bank_b[:], SIGMOID)
-            if direct:
-                nc.vector.tensor_tensor(resp[k][:], bank_a[:], gate[k][:], MULT)
-                nc.scalar.copy(plain[k][:], bank_c[:])
-                add_transposed(bank_h, resp[k], plain[k])
-                nc.scalar.copy(put[s % 2][:, cols], bank_h[:])
-            else:
-                nc.scalar.copy(resp[k][:], bank_a[:])
-                nc.scalar.copy(plain[k][:], bank_c[:])
-                nc.gpsimd.tensor_tensor(gate[k][:], resp[k][:], gate[k][:], MULT)
-                add_transposed(bank_h, gate[k], plain[k])
-                nc.scalar.copy(h_sb[k][:], bank_h[:])
-                nc.gpsimd.tensor_tensor(put[s % 2][:, cols], h_sb[k][:], wgs_sb[:, cols], MULT)
+            nc.scalar.activation(gate[h][:], (bank_b0, bank_b1)[h][:], SIGMOID)
+            nc.scalar.copy(resp[h][:], bank_a[:])
+            nc.scalar.copy(plain[h][:], bank_c[:])
+            nc.gpsimd.tensor_tensor(gate[h][:], resp[h][:], gate[h][:], MULT)
+            add_transposed(bank_d[h], gate[h][:], plain[h][:], 0, BLOCKS)
+            nc.scalar.copy(h_sb[h][:], bank_d[h][:])
+            nc.gpsimd.tensor_tensor(put[s % 2][:, cols], h_sb[h][:], wgs_sb[:, cols], MULT)
 
         def turn_stiff(s):
             nc.sync.dma_start(out=stiff_sb[s % 2][:], in_=stiff[block(s), :])
             for h in range(2):
                 for i in range(BLOCKS):
-                    nc.tensor.transpose(bank_d[h][:, block(i)], stiff_sb[s % 2][:, block(BLOCKS * h + i)], ident[:])
-                nc.scalar.copy(stiff_t[s % PER_PASS][:, h * HALF : (h + 1) * HALF], bank_d[h][:])
+                    nc.tensor.transpose(bank_o[h][:, block(i)], stiff_sb[s % 2][:, block(BLOCKS * h + i)], ident[:])
+                nc.scalar.copy(stiff_t[s][:, h * HALF : (h + 1) * HALF], bank_o[h][:])
+
+        def fetch_outer(s, h, x2):
+            nc.vector.tensor_scalar(x2, page_of[s][:].indirect(half_of(idx4, h)), -1.0, 1.0, MULT, ADD)
+
+        def fetch_inner(s, m0, m1, x1):
+            nc.vector.tensor_copy(x1, page_of[s][:].indirect(idx3[:, m0 // 16 : m1 // 16]))
 
         def fetch(s, h, x1, x2):
-            page = pages[s % PER_PASS]
-            nc.vector.tensor_scalar(x2, page[:].indirect(half_of(idx4, h)), -1.0, 1.0, MULT, ADD)
-            nc.vector.tensor_copy(x1, page[:].indirect(half_of(idx3, h)))
+            fetch_outer(s, h, x2)
+            fetch_inner(s, h * HALF, (h + 1) * HALF, x1)
 
-        def combine(s, h, x1, x2, k, direct):
-            add_transposed(bank_d[k], x2, x1)
-            dst = z_t[h][:].rearrange("p (b r) -> p b r", b=BLOCKS)[:, :, block(s % PER_PASS)]
-            factor = stiff_t[s % PER_PASS][:, h * HALF : (h + 1) * HALF].rearrange("p (b r) -> p b r", b=BLOCKS)
+        def by_block(ap):
+            return ap.rearrange("p (b r) -> p b r", r=P)
+
+        def combine(s, h, x1, x2, bank, k, b0, b1, direct):
+            add_transposed(bank, x2, x1, b0, b1)
+            dst = z_t[h][:].rearrange("p (b r) -> p b r", b=BLOCKS)[:, b0:b1, block(s % PER_PASS)]
+            factor = by_block(stiff_t[s][:, h * HALF + b0 * P : h * HALF + b1 * P])
+            cols = slice(b0 * P, b1 * P)
             if direct:
-                nc.vector.tensor_tensor(dst, bank_d[k][:].rearrange("p (b r) -> p b r", b=BLOCKS), factor, MULT)
+                nc.vector.tensor_tensor(dst, by_block(bank[:, cols]), factor, MULT)
             else:
-                nc.scalar.copy(jump[k][:], bank_d[k][:])
-                nc.gpsimd.tensor_tensor(dst, jump[k][:].rearrange("p (b r) -> p b r", b=BLOCKS), factor, MULT)
+                nc.scalar.copy(jump[k][:, cols], bank[:, cols])
+                nc.gpsimd.tensor_tensor(dst, by_block(jump[k][:, cols]), factor, MULT)
 
-        def turn_back(h, pair_banks):
+        def turn_back(h, pair, bank, copy):
             words = z_t[h][:].bitcast(F32)
-            z_words = z_bf[:].bitcast(F32)
-            for pair in range(2):
-                bank = pair_banks[pair]
-                for b in range(2):
-                    base = (2 * pair + b) * 256
-                    for u in range(2):
-                        nc.tensor.transpose(bank[:, block(2 * b + u)], words[:, base + u : base + 256 : 2], ident[:])
-                first = 2 * (h * HALF + pair * 256)
-                nc.scalar.copy(out=z_words[:, first : first + 512].rearrange("p (b m u) -> p b m u", b=2, u=2),
-                               in_=bank[:].rearrange("p (b u m) -> p b m u", b=2, u=2))
+            for b in range(2):
+                base = (2 * pair + b) * 256
+                for u in range(2):
+                    nc.tensor.transpose(bank[:, block(2 * b + u)], words[:, base + u : base + 256 : 2], ident[:])
+            first = 2 * (h * HALF + pair * 256)
+            copy(out=z_words[:, first : first + 512].rearrange("p (b m u) -> p b m u", b=2, u=2),
+                 in_=bank[:].rearrange("p (b u m) -> p b m u", b=2, u=2))
 
         def quantise_z(g, m0, m1):
             nc.vector.quantize_mx(out=z_w[g][:, m0:m1].bitcast(FP8X4), scales=z_s[g][:, m0:m1],
-                                  in_=z_bf[:, 4 * m0 : 4 * m1])
+                                  in_=z_words[:, 2 * m0 : 2 * m1].bitcast(BF16))
 
-        def features(h, out_banks, last):
-            cols = slice(h * HALF, (h + 1) * HALF)
+        def features(m0, m1, targets, shared, order):
+            cols = slice(m0, m1)
             for nb in range(N // P):
-                bank = out_banks[nb % len(out_banks)]
-                for g in range(2):
+                acc = targets[nb]
+                for g in order:
                     w_cols = slice(g * N + nb * P, g * N + (nb + 1) * P)
-                    nc.tensor.matmul_mx(out=bank[:], lhsT=wd_w[:, w_cols].bitcast(FP8X4), lhsT_scale=wd_s[:, w_cols],
+                    nc.tensor.matmul_mx(out=acc, lhsT=wd_w[:, w_cols].bitcast(FP8X4), lhsT_scale=wd_s[:, w_cols],
                                         rhs=z_w[g][:, cols].bitcast(FP8X4), rhs_scale=z_s[g][:, cols],
-                                        start=(g == 0), stop=(g == 1))
-                if last and nb % 2 == 1:
-                    nc.vector.tensor_copy(staged[nb][:], bank[:])
+                                        start=(g == order[0]), stop=(g == order[1]))
+                if shared and nb % 2 == 1:
+                    nc.vector.tensor_copy(staged[nb][:, cols], acc)
                 else:
-                    nc.scalar.copy(staged[nb][:], bank[:])
-                nc.sync.dma_start(out=out[block(nb), cols], in_=staged[nb][:])
+                    nc.scalar.copy(staged[nb][:, cols], acc)
+                nc.sync.dma_start(out=out[block(nb), cols], in_=staged[nb][:, cols])
 
         def load_wd(g):
             nc.sync.dma_start(out=wb_raw[3][:], in_=wd[g * K : (g + 1) * K, :].rearrange("(p j) c -> p j c", j=4))
-            interleave(w_bf[:, 4 * g * N : 4 * (g + 1) * N], wb_raw[3][:])
+            interleave(w_bf[:, 4 * g * N : 4 * (g + 1) * N], wb_raw[3][:], nc.scalar.copy)
 
-        for h in range(2):
-            respond(0, h, True)
-            cols = slice(h * HALF, (h + 1) * HALF)
-            nc.vector.tensor_tensor(pages[0][:].indirect(half_of(idx2, h)), put[0][:, cols], wgs_sb[:, cols], MULT)
+        def early(s, h):
+            if s >= PER_PASS:
+                return inner[s % 2][:], outer[s % 2][:]
+            if s % 2 == 0:
+                return inner[h][:], outer[h][:]
+            return staged[h][:, 0:HALF], staged[h][:, HALF:F]
+
+        respond_first(0)
         quantise_wb(1)
-        respond(1, 0, False)
-        respond(1, 1, False)
+        respond_first(1)
+        respond(1, 0)
+        respond(1, 1)
         quantise_wb(2)
         turn_stiff(0)
 
         for s in range(SLICES):
             if s > 0:
-                nc.vector.tensor_copy(pages[s % PER_PASS][:].indirect(idx2[:]), put[s % 2][:])
+                nc.vector.tensor_copy(page_of[s][:].indirect(idx2[:]), put[s % 2][:])
             halves = range(2) if s < PER_PASS else range(1)
             for h in halves:
-                k = h if s < PER_PASS else s % 2
-                fetch(s, h, inner[k][:], outer[k][:])
+                fetch(s, h, *early(s, h))
+            if s == SLICES - 2:
+                fetch(s - 1, 1, gate[1][:], plain[1][:])
             if s == 0:
                 quantise_wb(3)
             if s + 2 < SLICES:
-                respond(s + 2, 0, False)
-                respond(s + 2, 1, False)
+                respond(s + 2, 0)
+                respond(s + 2, 1)
             if s + 1 < SLICES:
                 turn_stiff(s + 1)
             for h in halves:
                 k = h if s < PER_PASS else s % 2
-                combine(s, h, inner[k][:], outer[k][:], k, False)
+                if s < SLICES - 1:
+                    combine(s, h, *early(s, h), bank_d[h if s < PER_PASS else 1], k, 0, BLOCKS, False)
+                else:
+                    for pair in range(2):
+                        combine(s, h, *early(s, h), bank_d[pair], k, 2 * pair, 2 * pair + 2, False)
+                    for pair in range(2):
+                        turn_back(0, pair, bank_d[pair], nc.scalar.copy)
+            if s == SLICES - 2:
+                combine(s - 1, 1, gate[1][:], plain[1][:], bank_d0, 2, 0, BLOCKS, False)
             if s in (1, 2):
                 load_wd(s - 1)
             if s == PER_PASS - 1:
                 nc.vector.quantize_mx(out=wd_w[:].bitcast(FP8X4), scales=wd_s[:], in_=w_bf[:])
                 for h in range(2):
-                    turn_back(h, bank_d)
+                    for pair in range(2):
+                        turn_back(h, pair, bank_o[pair], nc.scalar.copy)
             if s == PER_PASS:
                 quantise_z(0, 0, F)
 
-        turn_back(0, (bank_b0, bank_c))
-        for s in range(PER_PASS, SLICES):
-            x1, x2 = put[s % 2][:, 0:HALF], put[s % 2][:, HALF:S]
-            fetch(s, 1, x1, x2)
-            if s == PER_PASS:
-                quantise_z(1, 0, HALF)
-                features(0, (bank_o0, bank_o1), False)
-            combine(s, 1, x1, x2, s % 2, s == SLICES - 1)
-        turn_back(1, (bank_b0, bank_c))
-        quantise_z(1, HALF, F)
-        features(1, (bank_a, bank_b1, bank_o1, bank_o0), True)
+        quarter = HALF // 2
+        late = {
+            4: (put[1][:, 0:HALF], put[1][:, HALF:S]),
+            6: (inner[1][:], outer[1][:]),
+            7: (z_words[:, 0:HALF], z_words[:, HALF : 2 * HALF]),
+        }
+        for k, s in enumerate((4, 6)):
+            fetch(s, 1, *late[s])
+            combine(s, 1, *late[s], bank_d[k], 2 * k, 0, BLOCKS, False)
+        quantise_z(1, 0, HALF)
+        wide = (bank_a, bank_b0, bank_b1, bank_c)
+        features(0, HALF, [bank[:] for bank in wide], False, (1, 0))
+        s = SLICES - 1
+        x1, x2 = late[s]
+        fetch_outer(s, 1, x2)
+        for pair in range(2):
+            fetch_inner(s, HALF + pair * quarter, HALF + (pair + 1) * quarter, x1[:, pair * quarter : (pair + 1) * quarter])
+        for pair in range(2):
+            combine(s, 1, x1, x2, bank_d[pair], pair, 2 * pair, 2 * pair + 2, True)
+        for pair in range(2):
+            turn_back(1, pair, bank_d[pair], (nc.scalar.copy, nc.vector.tensor_copy)[pair])
+            quantise_z(1, HALF + pair * quarter, HALF + (pair + 1) * quarter)
+        features(HALF, HALF + quarter,
+                 [bank_o0[:, 0:quarter], bank_o1[:, 0:quarter], bank_o0[:, quarter:HALF], bank_o1[:, quarter:HALF]],
+                 True, (1, 0))
+        features(HALF + quarter, F, [bank[:, 0:quarter] for bank in wide], True, (0, 1))

@@ -23,7 +23,7 @@ HALF = 512
 BLOCKS = HALF // P
 SLICES = H // P
 PER_PASS = 4
-WB_CHUNKS = ((0, 128), (128, 256), (256, 512), (512, 1024))
+WB_CHUNKS = ((0, 128), (128, 512), (512, 1024))
 
 
 def tile_list_bone_face_features_kernel(
@@ -76,7 +76,6 @@ def tile_list_bone_face_features_kernel(
         gate = tiles("gate", 2, [P, HALF], F32)
         resp = tiles("resp", 2, [P, HALF], F32)
         plain = tiles("plain", 2, [P, HALF], F32)
-        h_sb = tiles("h_sb", 2, [P, HALF], F32)
         put = tiles("put", 2, [P, S], F32)
         inner = tiles("inner", 2, [P, HALF], F32)
         outer = tiles("outer", 2, [P, HALF], F32)
@@ -85,14 +84,15 @@ def tile_list_bone_face_features_kernel(
         stiff_t = tiles("stiff_t", SLICES, [P, F], F32)
         z_t = tiles("z_t", 2, [P, BLOCKS * HALF], BF16)
         z_words = one("z_words", [P, 2 * F], F32)
+        h_sb = (z_words[:, 3 * HALF : 4 * HALF], one("h_sb", [P, HALF], F32)[:])
         z_w = tiles("z_w", 2, [P, F], U32)
         z_s = tiles("z_s", 2, [P, F], U8)
         staged = tiles("staged", 4, [P, F], F32)
 
         nc.vector.memset(tab_s[:, 0 : T // 2].bitcast(I32), 0)
         nc.gpsimd.memset(tab_s[:, T // 2 : T].bitcast(I32), 0)
-        nc.gpsimd.memset(wa_s[:].bitcast(I32), 0)
-        nc.vector.memset(wc_s[:].bitcast(I32), 0)
+        nc.gpsimd.memset(wc_s[:].bitcast(I32), 0)
+        nc.vector.memset(wa_s[:].bitcast(I32), 0)
         wb_rows = wb.rearrange("(p j) c -> p j c", j=4)
 
         def load_wb(i):
@@ -106,30 +106,31 @@ def tile_list_bone_face_features_kernel(
                               in_=tab_scales[0][4 * q : 4 * q + 4, :].bitcast(I32))
         nc.sync.dma_start(out=tab_w[:].bitcast(I32), in_=tab_words[0].rearrange("p n t -> p (n t)").bitcast(I32))
         for q in range(4):
-            nc.gpsimd.dma_start(out=wa_s[32 * q : 32 * q + 4, :].bitcast(I32),
-                                in_=wa_scales[0][4 * q : 4 * q + 4, :].bitcast(I32))
+            nc.gpsimd.dma_start(out=wc_s[32 * q : 32 * q + 4, :].bitcast(I32),
+                                in_=wc_scales[0][4 * q : 4 * q + 4, :].bitcast(I32))
 
         def interleave(dst, raw, copy):
             copy(out=dst.rearrange("p (c i t) -> p c t i", i=4, t=4), in_=raw.rearrange("p t (c i) -> p c t i", i=4))
 
-        def quantise_wb(i):
-            c0, c1 = WB_CHUNKS[i]
-            interleave(w_bf[:, 4 * c0 : 4 * c1], wb_raw[i][:], nc.vector.tensor_copy if i == 0 else nc.scalar.copy)
+        def quantise_wb(i, c0, c1, copy):
+            first = WB_CHUNKS[i][0]
+            for a in range(c0, c1, 256):
+                b = min(a + 256, c1)
+                interleave(w_bf[:, 4 * a : 4 * b], wb_raw[i][:, :, a - first : b - first], copy)
             nc.vector.quantize_mx(out=wb_w[:, c0:c1].bitcast(FP8X4), scales=wb_s[:, c0:c1],
                                   in_=w_bf[:, 4 * c0 : 4 * c1])
 
         nc.sync.dma_start(out=wa_w[:].bitcast(I32), in_=wa_words[0].bitcast(I32))
-        nc.sync.dma_start(out=wc_w[:].bitcast(I32), in_=wc_words[0].rearrange("p n t -> p (n t)").bitcast(I32))
         for q in range(4):
-            nc.sync.dma_start(out=wc_s[32 * q : 32 * q + 4, :].bitcast(I32),
-                              in_=wc_scales[0][4 * q : 4 * q + 4, :].bitcast(I32))
+            nc.sync.dma_start(out=wa_s[32 * q : 32 * q + 4, :].bitcast(I32),
+                              in_=wa_scales[0][4 * q : 4 * q + 4, :].bitcast(I32))
+        nc.sync.dma_start(out=wc_w[:].bitcast(I32), in_=wc_words[0].rearrange("p n t -> p (n t)").bitcast(I32))
         load_wb(1)
         nc.sync.dma_start(idx2[:], offs2)
         nc.sync.dma_start(out=wgs_sb[:], in_=wgs)
-        load_wb(2)
         nc.sync.dma_start(idx3[:], offs3)
         nc.sync.dma_start(idx4[:], offs4)
-        load_wb(3)
+        load_wb(2)
 
         make_identity(nc, ident[:])
         for page in pages[:2]:
@@ -137,18 +138,25 @@ def tile_list_bone_face_features_kernel(
         for page in pages[2:]:
             nc.gpsimd.memset(page[:], 0.0)
 
-        quantise_wb(0)
+        quantise_wb(0, 0, 128, nc.vector.tensor_copy)
         for h in range(2):
             nc.vector.tensor_copy(v_s[h][:], tab_s[:].indirect(half_of(idx1, h)))
             nc.vector.tensor_copy(v_w[h][:], tab_w[:].indirect(half_of(idx1, h)))
+        quantise_wb(1, 128, 256, nc.vector.tensor_copy)
+        quantise_wb(1, 256, 512, nc.vector.tensor_copy)
 
         def block(i):
             return slice(i * P, (i + 1) * P)
 
-        def add_transposed(bank, x, y, b0, b1):
-            for i in range(b0, b1):
-                nc.tensor.matmul(bank[:, block(i)], x[:, block(i)], ident[:], start=True, stop=False, is_transpose=True)
-                nc.tensor.matmul(bank[:, block(i)], y[:, block(i)], ident[:], start=False, stop=True, is_transpose=True)
+        def add_transposed(bank, x, y, b0, b1, x_first=False):
+            steps = [(term, i) for i in range(b0, b1) for term in (0, 1)]
+            if x_first:
+                steps = sorted(steps)
+            for n, (term, i) in enumerate(steps):
+                start = n == 0 if x_first else term == 0
+                stop = n == len(steps) - 1 if x_first else term == 1
+                nc.tensor.matmul(bank[:, block(i)], (x, y)[term][:, block(i)], ident[:], start=start, stop=stop,
+                                 is_transpose=True)
 
         def weights(s):
             return (
@@ -165,30 +173,33 @@ def tile_list_bone_face_features_kernel(
                                     rhs_scale=v_s[h][:], start=True, stop=True)
             nc.scalar.activation(jump[h][:], first_b[:], SIGMOID)
             nc.vector.tensor_tensor(inner[h][:], first_a[:], jump[h][:], MULT)
-            nc.vector.tensor_tensor(put[0][:, cols], first_c[:], inner[h][:], ADD)
-            nc.vector.tensor_tensor(pages[0][:].indirect(half_of(idx2, h)), put[0][:, cols], wgs_sb[:, cols], MULT)
+            nc.vector.tensor_tensor(outer[h][:], first_c[:], inner[h][:], ADD)
+            nc.gpsimd.tensor_tensor(put[0][:, cols], outer[h][:], wgs_sb[:, cols], MULT)
+            nc.vector.tensor_copy(pages[0][:].indirect(half_of(idx2, h)), put[0][:, cols])
 
         def respond(s, h):
-            for bank, (codes, scales) in zip(((bank_b0, bank_b1)[h], bank_a, bank_c), weights(s)):
+            bank_b = (bank_b0, bank_b1)[h]
+            for bank, (codes, scales) in zip((bank_b, bank_a, bank_c), weights(s)):
                 for i in range(BLOCKS):
                     nc.tensor.matmul_mx(out=bank[:, block(i)], lhsT=v_w[h][:, block(i)].bitcast(FP8X4),
                                         lhsT_scale=v_s[h][:, block(i)], rhs=codes, rhs_scale=scales,
                                         start=True, stop=True)
             cols = slice(h * HALF, (h + 1) * HALF)
-            nc.scalar.activation(gate[h][:], (bank_b0, bank_b1)[h][:], SIGMOID)
+            nc.scalar.activation(gate[h][:], bank_b[:], SIGMOID)
             nc.scalar.copy(resp[h][:], bank_a[:])
             nc.scalar.copy(plain[h][:], bank_c[:])
             nc.gpsimd.tensor_tensor(gate[h][:], resp[h][:], gate[h][:], MULT)
             add_transposed(bank_d[h], gate[h][:], plain[h][:], 0, BLOCKS)
-            nc.scalar.copy(h_sb[h][:], bank_d[h][:])
-            nc.gpsimd.tensor_tensor(put[s % 2][:, cols], h_sb[h][:], wgs_sb[:, cols], MULT)
+            nc.scalar.copy(h_sb[h], bank_d[h][:])
+            nc.gpsimd.tensor_tensor(put[s % 2][:, cols], h_sb[h], wgs_sb[:, cols], MULT)
 
         def turn_stiff(s):
             nc.sync.dma_start(out=stiff_sb[s % 2][:], in_=stiff[block(s), :])
             for h in range(2):
                 for i in range(BLOCKS):
                     nc.tensor.transpose(bank_o[h][:, block(i)], stiff_sb[s % 2][:, block(BLOCKS * h + i)], ident[:])
-                nc.scalar.copy(stiff_t[s][:, h * HALF : (h + 1) * HALF], bank_o[h][:])
+                nc.scalar.copy(out=stiff_t[s][:, h * HALF : (h + 1) * HALF].rearrange("p (b u q e) -> p b u q e", u=2, q=32, e=2),
+                               in_=bank_o[h][:].rearrange("p (b q u e) -> p b u q e", u=2, q=32, e=2))
 
         def fetch_outer(s, h, x2):
             nc.vector.tensor_scalar(x2, page_of[s][:].indirect(half_of(idx4, h)), -1.0, 1.0, MULT, ADD)
@@ -200,26 +211,27 @@ def tile_list_bone_face_features_kernel(
             fetch_outer(s, h, x2)
             fetch_inner(s, h * HALF, (h + 1) * HALF, x1)
 
-        def by_block(ap):
-            return ap.rearrange("p (b r) -> p b r", r=P)
-
         def combine(s, h, x1, x2, bank, k, b0, b1, direct):
-            add_transposed(bank, x2, x1, b0, b1)
-            dst = z_t[h][:].rearrange("p (b r) -> p b r", b=BLOCKS)[:, b0:b1, block(s % PER_PASS)]
-            factor = by_block(stiff_t[s][:, h * HALF + b0 * P : h * HALF + b1 * P])
-            cols = slice(b0 * P, b1 * P)
+            add_transposed(bank, x2, x1, b0, b1, direct)
+            place = slice(64 * (s % PER_PASS), 64 * (s % PER_PASS + 1))
+            dst = z_t[h][:].rearrange("p (b u r) -> p b u r", b=BLOCKS, u=2)[:, :, :, place]
+            factor = stiff_t[s][:, h * HALF : (h + 1) * HALF]
             if direct:
-                nc.vector.tensor_tensor(dst, by_block(bank[:, cols]), factor, MULT)
+                for b in range(b0, b1):
+                    nc.vector.tensor_tensor(dst[:, b, :, :].rearrange("p u (q e) -> p u q e", e=2),
+                                            bank[:, block(b)].rearrange("p (q u e) -> p u q e", u=2, e=2),
+                                            factor[:, block(b)].rearrange("p (u q e) -> p u q e", u=2, e=2), MULT)
             else:
-                nc.scalar.copy(jump[k][:, cols], bank[:, cols])
-                nc.gpsimd.tensor_tensor(dst, by_block(jump[k][:, cols]), factor, MULT)
+                cols = slice(b0 * P, b1 * P)
+                nc.scalar.copy(out=jump[k][:, cols].rearrange("p (b u q e) -> p b u q e", u=2, q=32, e=2),
+                               in_=bank[:, cols].rearrange("p (b q u e) -> p b u q e", u=2, q=32, e=2))
+                nc.gpsimd.tensor_tensor(dst[:, b0:b1, :, :], jump[k][:, cols].rearrange("p (b u r) -> p b u r", u=2, r=64),
+                                        factor[:, cols].rearrange("p (b u r) -> p b u r", u=2, r=64), MULT)
 
         def turn_back(h, pair, bank, copy):
             words = z_t[h][:].bitcast(F32)
-            for b in range(2):
-                base = (2 * pair + b) * 256
-                for u in range(2):
-                    nc.tensor.transpose(bank[:, block(2 * b + u)], words[:, base + u : base + 256 : 2], ident[:])
+            for i in range(BLOCKS):
+                nc.tensor.transpose(bank[:, block(i)], words[:, block(BLOCKS * pair + i)], ident[:])
             first = 2 * (h * HALF + pair * 256)
             copy(out=z_words[:, first : first + 512].rearrange("p (b m u) -> p b m u", b=2, u=2),
                  in_=bank[:].rearrange("p (b u m) -> p b m u", b=2, u=2))
@@ -228,10 +240,11 @@ def tile_list_bone_face_features_kernel(
             nc.vector.quantize_mx(out=z_w[g][:, m0:m1].bitcast(FP8X4), scales=z_s[g][:, m0:m1],
                                   in_=z_words[:, 2 * m0 : 2 * m1].bitcast(BF16))
 
-        def features(m0, m1, targets, shared, order):
+        def features(m0, m1, targets, shared, orders):
             cols = slice(m0, m1)
             for nb in range(N // P):
                 acc = targets[nb]
+                order = orders[nb]
                 for g in order:
                     w_cols = slice(g * N + nb * P, g * N + (nb + 1) * P)
                     nc.tensor.matmul_mx(out=acc, lhsT=wd_w[:, w_cols].bitcast(FP8X4), lhsT_scale=wd_s[:, w_cols],
@@ -244,8 +257,10 @@ def tile_list_bone_face_features_kernel(
                 nc.sync.dma_start(out=out[block(nb), cols], in_=staged[nb][:, cols])
 
         def load_wd(g):
-            nc.sync.dma_start(out=wb_raw[3][:], in_=wd[g * K : (g + 1) * K, :].rearrange("(p j) c -> p j c", j=4))
-            interleave(w_bf[:, 4 * g * N : 4 * (g + 1) * N], wb_raw[3][:], nc.scalar.copy)
+            nc.sync.dma_start(out=wb_raw[2][:], in_=wd[g * K : (g + 1) * K, :].rearrange("(p j) c -> p j c", j=4))
+            for c0 in (0, N // 2):
+                interleave(w_bf[:, 4 * (g * N + c0) : 4 * (g * N + c0 + N // 2)], wb_raw[2][:, :, c0 : c0 + N // 2],
+                           nc.scalar.copy)
 
         def early(s, h):
             if s >= PER_PASS:
@@ -255,11 +270,9 @@ def tile_list_bone_face_features_kernel(
             return staged[h][:, 0:HALF], staged[h][:, HALF:F]
 
         respond_first(0)
-        quantise_wb(1)
         respond_first(1)
         respond(1, 0)
         respond(1, 1)
-        quantise_wb(2)
         turn_stiff(0)
 
         for s in range(SLICES):
@@ -271,7 +284,7 @@ def tile_list_bone_face_features_kernel(
             if s == SLICES - 2:
                 fetch(s - 1, 1, gate[1][:], plain[1][:])
             if s == 0:
-                quantise_wb(3)
+                quantise_wb(2, 512, 1024, nc.scalar.copy)
             if s + 2 < SLICES:
                 respond(s + 2, 0)
                 respond(s + 2, 1)
@@ -284,32 +297,32 @@ def tile_list_bone_face_features_kernel(
                 else:
                     for pair in range(2):
                         combine(s, h, *early(s, h), bank_d[pair], k, 2 * pair, 2 * pair + 2, False)
-                    for pair in range(2):
-                        turn_back(0, pair, bank_d[pair], nc.scalar.copy)
             if s == SLICES - 2:
                 combine(s - 1, 1, gate[1][:], plain[1][:], bank_d0, 2, 0, BLOCKS, False)
             if s in (1, 2):
                 load_wd(s - 1)
             if s == PER_PASS - 1:
                 nc.vector.quantize_mx(out=wd_w[:].bitcast(FP8X4), scales=wd_s[:], in_=w_bf[:])
-                for h in range(2):
-                    for pair in range(2):
-                        turn_back(h, pair, bank_o[pair], nc.scalar.copy)
-            if s == PER_PASS:
+                for h, pair in ((0, 0), (0, 1), (1, 0)):
+                    turn_back(h, pair, bank_o[pair], nc.scalar.copy)
+            if s == SLICES - 3:
+                turn_back(1, 1, bank_o1, nc.scalar.copy)
                 quantise_z(0, 0, F)
 
         quarter = HALF // 2
         late = {
             4: (put[1][:, 0:HALF], put[1][:, HALF:S]),
             6: (inner[1][:], outer[1][:]),
-            7: (z_words[:, 0:HALF], z_words[:, HALF : 2 * HALF]),
+            7: (z_words[:, 0:HALF], outer[0][:]),
         }
         for k, s in enumerate((4, 6)):
             fetch(s, 1, *late[s])
-            combine(s, 1, *late[s], bank_d[k], 2 * k, 0, BLOCKS, False)
+            combine(s, 1, *late[s], (bank_d0, bank_o1)[k], 2 * k, 0, BLOCKS, False)
+            if k == 0:
+                turn_back(0, 0, bank_o1, nc.scalar.copy)
+                turn_back(0, 1, bank_d1, nc.scalar.copy)
         quantise_z(1, 0, HALF)
         wide = (bank_a, bank_b0, bank_b1, bank_c)
-        features(0, HALF, [bank[:] for bank in wide], False, (1, 0))
         s = SLICES - 1
         x1, x2 = late[s]
         fetch_outer(s, 1, x2)
@@ -317,10 +330,11 @@ def tile_list_bone_face_features_kernel(
             fetch_inner(s, HALF + pair * quarter, HALF + (pair + 1) * quarter, x1[:, pair * quarter : (pair + 1) * quarter])
         for pair in range(2):
             combine(s, 1, x1, x2, bank_d[pair], pair, 2 * pair, 2 * pair + 2, True)
+        features(0, HALF, [bank[:] for bank in wide], False, [(0, 1)] * 4)
         for pair in range(2):
-            turn_back(1, pair, bank_d[pair], (nc.scalar.copy, nc.vector.tensor_copy)[pair])
+            turn_back(1, pair, bank_d[pair], (nc.vector.tensor_copy, nc.scalar.copy)[pair])
             quantise_z(1, HALF + pair * quarter, HALF + (pair + 1) * quarter)
         features(HALF, HALF + quarter,
                  [bank_o0[:, 0:quarter], bank_o1[:, 0:quarter], bank_o0[:, quarter:HALF], bank_o1[:, quarter:HALF]],
-                 True, (1, 0))
-        features(HALF + quarter, F, [bank[:, 0:quarter] for bank in wide], True, (0, 1))
+                 True, [(0, 1), (0, 1), (1, 0), (1, 0)])
+        features(HALF + quarter, F, [bank[:, 0:quarter] for bank in wide], True, [(0, 1)] * 4)

@@ -77,8 +77,10 @@ def tile_list_bone_face_features_kernel(
         resp = tiles("resp", 2, [P, HALF], F32)
         plain = tiles("plain", 2, [P, HALF], F32)
         put = tiles("put", 2, [P, S], F32)
-        inner = tiles("inner", 2, [P, HALF], F32)
-        outer = tiles("outer", 2, [P, HALF], F32)
+        inner_all = one("inner", [P, F], F32)
+        outer_all = one("outer", [P, F], F32)
+        inner = (inner_all[:, 0:HALF], inner_all[:, HALF:F])
+        outer = (outer_all[:, 0:HALF], outer_all[:, HALF:F])
         jump = tiles("jump", 3, [P, HALF], F32)
         stiff_sb = tiles("stiff_sb", 2, [P, F], F32)
         stiff_t = tiles("stiff_t", SLICES, [P, F], F32)
@@ -172,9 +174,9 @@ def tile_list_bone_face_features_kernel(
                 nc.tensor.matmul_mx(out=bank[:], lhsT=codes, lhsT_scale=scales, rhs=v_w[h][:].bitcast(FP8X4),
                                     rhs_scale=v_s[h][:], start=True, stop=True)
             nc.scalar.activation(jump[h][:], first_b[:], SIGMOID)
-            nc.vector.tensor_tensor(inner[h][:], first_a[:], jump[h][:], MULT)
-            nc.vector.tensor_tensor(outer[h][:], first_c[:], inner[h][:], ADD)
-            nc.gpsimd.tensor_tensor(put[0][:, cols], outer[h][:], wgs_sb[:, cols], MULT)
+            nc.vector.tensor_tensor(inner[h], first_a[:], jump[h][:], MULT)
+            nc.vector.tensor_tensor(outer[h], first_c[:], inner[h], ADD)
+            nc.gpsimd.tensor_tensor(put[0][:, cols], outer[h], wgs_sb[:, cols], MULT)
             nc.vector.tensor_copy(pages[0][:].indirect(half_of(idx2, h)), put[0][:, cols])
 
         def respond(s, h):
@@ -240,21 +242,31 @@ def tile_list_bone_face_features_kernel(
             nc.vector.quantize_mx(out=z_w[g][:, m0:m1].bitcast(FP8X4), scales=z_s[g][:, m0:m1],
                                   in_=z_words[:, 2 * m0 : 2 * m1].bitcast(BF16))
 
-        def features(m0, m1, targets, shared, orders):
-            cols = slice(m0, m1)
+        def product(acc, g, nb, cols, start, stop):
+            w_cols = slice(g * N + nb * P, g * N + (nb + 1) * P)
+            nc.tensor.matmul_mx(out=acc, lhsT=wd_w[:, w_cols].bitcast(FP8X4), lhsT_scale=wd_s[:, w_cols],
+                                rhs=z_w[g][:, cols].bitcast(FP8X4), rhs_scale=z_s[g][:, cols], start=start, stop=stop)
+
+        def features_half(out_banks):
+            cols = slice(0, HALF)
             for nb in range(N // P):
-                acc = targets[nb]
-                order = orders[nb]
-                for g in order:
-                    w_cols = slice(g * N + nb * P, g * N + (nb + 1) * P)
-                    nc.tensor.matmul_mx(out=acc, lhsT=wd_w[:, w_cols].bitcast(FP8X4), lhsT_scale=wd_s[:, w_cols],
-                                        rhs=z_w[g][:, cols].bitcast(FP8X4), rhs_scale=z_s[g][:, cols],
-                                        start=(g == order[0]), stop=(g == order[1]))
-                if shared and nb % 2 == 1:
-                    nc.vector.tensor_copy(staged[nb][:, cols], acc)
-                else:
-                    nc.scalar.copy(staged[nb][:, cols], acc)
+                for g in range(2):
+                    product(out_banks[nb][:], g, nb, cols, g == 0, g == 1)
+                nc.scalar.copy(staged[nb][:, cols], out_banks[nb][:])
                 nc.sync.dma_start(out=out[block(nb), cols], in_=staged[nb][:, cols])
+
+        def features_quarter(pair, out_banks):
+            width = HALF // 2
+            cols = slice(HALF + pair * width, HALF + (pair + 1) * width)
+            for b in range(2):
+                for g in range(2):
+                    for a in range(2):
+                        product(out_banks[b][:, a * width : (a + 1) * width], g, 2 * b + a, cols,
+                                g == 0 and a == 0, g == 1 and a == 1)
+                stage = staged[2 * pair + b][:, HALF:F]
+                (nc.scalar.copy, nc.vector.tensor_copy)[b](out=stage, in_=out_banks[b][:])
+                nc.sync.dma_start(out=out[2 * b * P : 2 * (b + 1) * P, cols].rearrange("(a p) m -> p a m", a=2),
+                                  in_=stage.rearrange("p (a m) -> p a m", a=2))
 
         def load_wd(g):
             nc.sync.dma_start(out=wb_raw[2][:], in_=wd[g * K : (g + 1) * K, :].rearrange("(p j) c -> p j c", j=4))
@@ -264,10 +276,10 @@ def tile_list_bone_face_features_kernel(
 
         def early(s, h):
             if s >= PER_PASS:
-                return inner[s % 2][:], outer[s % 2][:]
+                return inner[s % 2], outer[s % 2]
             if s % 2 == 0:
-                return inner[h][:], outer[h][:]
-            return staged[h][:, 0:HALF], staged[h][:, HALF:F]
+                return inner[h], outer[h]
+            return staged[0][:, h * HALF : (h + 1) * HALF], staged[1][:, h * HALF : (h + 1) * HALF]
 
         respond_first(0)
         respond_first(1)
@@ -279,8 +291,12 @@ def tile_list_bone_face_features_kernel(
             if s > 0:
                 nc.vector.tensor_copy(page_of[s][:].indirect(idx2[:]), put[s % 2][:])
             halves = range(2) if s < PER_PASS else range(1)
-            for h in halves:
-                fetch(s, h, *early(s, h))
+            if s < PER_PASS:
+                for h in halves:
+                    fetch_outer(s, h, early(s, h)[1])
+                fetch_inner(s, 0, F, (inner_all, staged[0])[s % 2][:])
+            else:
+                fetch(s, 0, *early(s, 0))
             if s == SLICES - 2:
                 fetch(s - 1, 1, gate[1][:], plain[1][:])
             if s == 0:
@@ -312,8 +328,8 @@ def tile_list_bone_face_features_kernel(
         quarter = HALF // 2
         late = {
             4: (put[1][:, 0:HALF], put[1][:, HALF:S]),
-            6: (inner[1][:], outer[1][:]),
-            7: (z_words[:, 0:HALF], outer[0][:]),
+            6: (inner[1], outer[1]),
+            7: (z_words[:, 0:HALF], outer[0]),
         }
         for k, s in enumerate((4, 6)):
             fetch(s, 1, *late[s])
@@ -330,11 +346,9 @@ def tile_list_bone_face_features_kernel(
             fetch_inner(s, HALF + pair * quarter, HALF + (pair + 1) * quarter, x1[:, pair * quarter : (pair + 1) * quarter])
         for pair in range(2):
             combine(s, 1, x1, x2, bank_d[pair], pair, 2 * pair, 2 * pair + 2, True)
-        features(0, HALF, [bank[:] for bank in wide], False, [(0, 1)] * 4)
+        features_half(wide)
         for pair in range(2):
             turn_back(1, pair, bank_d[pair], (nc.vector.tensor_copy, nc.scalar.copy)[pair])
             quantise_z(1, HALF + pair * quarter, HALF + (pair + 1) * quarter)
-        features(HALF, HALF + quarter,
-                 [bank_o0[:, 0:quarter], bank_o1[:, 0:quarter], bank_o0[:, quarter:HALF], bank_o1[:, quarter:HALF]],
-                 True, [(0, 1), (0, 1), (1, 0), (1, 0)])
-        features(HALF + quarter, F, [bank[:, 0:quarter] for bank in wide], True, [(0, 1)] * 4)
+        features_quarter(0, (bank_o0, bank_o1))
+        features_quarter(1, (bank_a, bank_b0))

@@ -23,7 +23,7 @@ HALF = 512
 BLOCKS = HALF // P
 SLICES = H // P
 PER_PASS = 4
-WB_CHUNKS = ((0, 128), (128, 512), (512, 1024))
+WB_CHUNKS = ((0, 128), (128, 256), (256, 512), (512, 1024))
 
 
 def tile_list_bone_face_features_kernel(
@@ -39,8 +39,8 @@ def tile_list_bone_face_features_kernel(
         def tiles(name, count, shape, dtype):
             return [sb.tile(shape, dtype, name="%s%d" % (name, i), align_bytes=64) for i in range(count)]
 
-        def one(name, shape, dtype):
-            return sb.tile(shape, dtype, name=name, align_bytes=64)
+        def one(name, shape, dtype, tag=""):
+            return sb.tile(shape, dtype, name=name, align_bytes=64, tag=tag)
 
         idx1 = lists.tile([P, S // 16], U16, name="idx1")
         idx2 = lists.tile([P, S // 16], U16, name="idx2")
@@ -66,17 +66,20 @@ def tile_list_bone_face_features_kernel(
         wc_s = one("wc_s", [P, H], U8)
         wb_raw = [one("wb_raw%d" % i, [P, 4, c1 - c0], F32) for i, (c0, c1) in enumerate(WB_CHUNKS)]
         w_bf = one("w_bf", [P, 4 * H], BF16)
-        wb_w = one("wb_w", [P, H], U32)
+        wb_w = [one("wb_w0", [P, HALF], U32)]
         wb_s = one("wb_s", [P, H], U8)
-        wd_w = one("wd_w", [P, 2 * N], U32)
+        wd_w = []
         wd_s = one("wd_s", [P, 2 * N], U8)
         wgs_sb = one("wgs_sb", [P, S], F32)
-        pages = tiles("page", 3, [P, T2], F32)
-        page_of = [pages[i] for i in (0, 1, 0, 1, 0, 1, 2, 1)]
+        pages = tiles("page", 4, [P, T2], F32)
+        page_of = [pages[i] for i in (0, 1, 0, 1, 0, 1, 2, 3)]
         gate = tiles("gate", 2, [P, HALF], F32)
         resp = tiles("resp", 2, [P, HALF], F32)
         plain = tiles("plain", 2, [P, HALF], F32)
         put = tiles("put", 2, [P, S], F32)
+        first_put = (put[0][:, 0:HALF], one("first_put", [P, HALF], F32, "late_wb")[:])
+        put_of = [put[s % 2][:] for s in range(SLICES)]
+        put_of[2] = one("put_2", [P, S], F32, "late_wd")[:]
         inner_all = one("inner", [P, F], F32)
         outer_all = one("outer", [P, F], F32)
         inner = (inner_all[:, 0:HALF], inner_all[:, HALF:F])
@@ -86,9 +89,10 @@ def tile_list_bone_face_features_kernel(
         stiff_t = tiles("stiff_t", SLICES, [P, F], F32)
         z_t = tiles("z_t", 2, [P, BLOCKS * HALF], BF16)
         z_words = one("z_words", [P, 2 * F], F32)
-        h_sb = (z_words[:, 3 * HALF : 4 * HALF], one("h_sb", [P, HALF], F32)[:])
-        z_w = tiles("z_w", 2, [P, F], U32)
+        h_sb = [t[:] for t in tiles("h_sb", 2, [P, HALF], F32)]
+        z_w = {1: one("z_w1", [P, F], U32)}
         z_s = tiles("z_s", 2, [P, F], U8)
+        put_of[5] = one("put_5", [P, S], F32, "late_z")[:]
         staged = tiles("staged", 4, [P, F], F32)
 
         nc.vector.memset(tab_s[:, 0 : T // 2].bitcast(I32), 0)
@@ -114,86 +118,106 @@ def tile_list_bone_face_features_kernel(
         def interleave(dst, raw, copy):
             copy(out=dst.rearrange("p (c i t) -> p c t i", i=4, t=4), in_=raw.rearrange("p t (c i) -> p c t i", i=4))
 
-        def quantise_wb(i, c0, c1, copy):
-            first = WB_CHUNKS[i][0]
-            for a in range(c0, c1, 256):
-                b = min(a + 256, c1)
-                interleave(w_bf[:, 4 * a : 4 * b], wb_raw[i][:, :, a - first : b - first], copy)
-            nc.vector.quantize_mx(out=wb_w[:, c0:c1].bitcast(FP8X4), scales=wb_s[:, c0:c1],
-                                  in_=w_bf[:, 4 * c0 : 4 * c1])
+        def round_wb(i, rounded, copy):
+            c0, c1 = WB_CHUNKS[i]
+            for a in range(0, c1 - c0, 256):
+                b = min(a + 256, c1 - c0)
+                interleave(rounded[:, 4 * a : 4 * b], wb_raw[i][:, :, a:b], copy)
 
-        nc.sync.dma_start(out=wa_w[:].bitcast(I32), in_=wa_words[0].bitcast(I32))
+        def quantise_wb(i, rounded):
+            c0, c1 = WB_CHUNKS[i]
+            nc.vector.quantize_mx(out=wb_w[c0 // HALF][:, c0 % HALF : (c1 - 1) % HALF + 1].bitcast(FP8X4), scales=wb_s[:, c0:c1], in_=rounded)
+
+        wa_rows = wa_words[0].bitcast(I32)
+        nc.sync.dma_start(out=wa_w[:, 0:512].bitcast(I32), in_=wa_rows[:, 0:128])
         for q in range(4):
             nc.sync.dma_start(out=wa_s[32 * q : 32 * q + 4, :].bitcast(I32),
                               in_=wa_scales[0][4 * q : 4 * q + 4, :].bitcast(I32))
-        nc.sync.dma_start(out=wc_w[:].bitcast(I32), in_=wc_words[0].rearrange("p n t -> p (n t)").bitcast(I32))
+        wc_rows = wc_words[0].rearrange("p n t -> p (n t)").bitcast(I32)
+        nc.sync.dma_start(out=wc_w[:, 0:256].bitcast(I32), in_=wc_rows[:, 0:256])
         load_wb(1)
+        nc.sync.dma_start(out=wgs_sb[:, 0:HALF], in_=wgs[:, 0:HALF])
         nc.sync.dma_start(idx2[:], offs2)
-        nc.sync.dma_start(out=wgs_sb[:], in_=wgs)
+        nc.sync.dma_start(out=wgs_sb[:, HALF:S], in_=wgs[:, HALF:S])
+        load_wb(2)
+        nc.sync.dma_start(out=wa_w[:, 512 : 2 * H].bitcast(I32), in_=wa_rows[:, 128 : H // 2])
+        nc.sync.dma_start(out=wc_w[:, 256:H].bitcast(I32), in_=wc_rows[:, 256:H])
         nc.sync.dma_start(idx3[:], offs3)
         nc.sync.dma_start(idx4[:], offs4)
-        load_wb(2)
+        load_wb(3)
 
         make_identity(nc, ident[:])
-        for page in pages[:2]:
+        for page in pages[:1]:
             nc.vector.memset(page[:], 0.0)
-        for page in pages[2:]:
+        for page in pages[1:]:
             nc.gpsimd.memset(page[:], 0.0)
 
-        quantise_wb(0, 0, 128, nc.vector.tensor_copy)
+        round_wb(0, w_bf[:, 0:512], nc.vector.tensor_copy)
+        quantise_wb(0, w_bf[:, 0:512])
         for h in range(2):
             nc.vector.tensor_copy(v_s[h][:], tab_s[:].indirect(half_of(idx1, h)))
             nc.vector.tensor_copy(v_w[h][:], tab_w[:].indirect(half_of(idx1, h)))
-        quantise_wb(1, 128, 256, nc.vector.tensor_copy)
-        quantise_wb(1, 256, 512, nc.vector.tensor_copy)
 
         def block(i):
             return slice(i * P, (i + 1) * P)
 
-        def add_transposed(bank, x, y, b0, b1, x_first=False):
-            steps = [(term, i) for i in range(b0, b1) for term in (0, 1)]
-            if x_first:
+        def add_transposed(bank, x, y, count, one_group=False):
+            steps = [(term, i) for i in range(count) for term in (0, 1)]
+            if one_group:
                 steps = sorted(steps)
             for n, (term, i) in enumerate(steps):
-                start = n == 0 if x_first else term == 0
-                stop = n == len(steps) - 1 if x_first else term == 1
+                start = n == 0 if one_group else term == 0
+                stop = n == len(steps) - 1 if one_group else term == 1
                 nc.tensor.matmul(bank[:, block(i)], (x, y)[term][:, block(i)], ident[:], start=start, stop=stop,
                                  is_transpose=True)
 
         def weights(s):
             return (
-                (wb_w[:, block(s)].bitcast(FP8X4), wb_s[:, block(s)]),
+                (wb_w[s // PER_PASS][:, block(s % PER_PASS)].bitcast(FP8X4), wb_s[:, block(s)]),
                 (wa_w[:, 2 * P * s : 2 * P * (s + 1)].bitcast(FP4X4), wa_s[:, block(s)]),
                 (wc_w[:, block(s)].bitcast(FP8X4), wc_s[:, block(s)]),
             )
 
         def respond_first(h):
             cols = slice(h * HALF, (h + 1) * HALF)
-            first_b, first_a, first_c = ((bank_b0, bank_a, bank_c), (bank_b1, bank_o0, bank_o1))[h]
+            first_b, first_a, first_c = bank_b0, bank_a, bank_c
+            gated = outer[h]
             for bank, (codes, scales) in zip((first_b, first_a, first_c), weights(0)):
                 nc.tensor.matmul_mx(out=bank[:], lhsT=codes, lhsT_scale=scales, rhs=v_w[h][:].bitcast(FP8X4),
                                     rhs_scale=v_s[h][:], start=True, stop=True)
-            nc.scalar.activation(jump[h][:], first_b[:], SIGMOID)
-            nc.vector.tensor_tensor(inner[h], first_a[:], jump[h][:], MULT)
-            nc.vector.tensor_tensor(outer[h], first_c[:], inner[h], ADD)
-            nc.gpsimd.tensor_tensor(put[0][:, cols], outer[h], wgs_sb[:, cols], MULT)
-            nc.vector.tensor_copy(pages[0][:].indirect(half_of(idx2, h)), put[0][:, cols])
+            first_gate = (first_put[0], jump[1][:])[h]
+            nc.scalar.activation(first_gate, first_b[:], SIGMOID)
+            nc.vector.tensor_tensor(gated, first_a[:], first_gate, MULT)
+            if h == 0:
+                nc.vector.tensor_tensor(inner[0], first_c[:], gated, ADD)
+                round_wb(1, put[0][:, 0:256].bitcast(BF16), nc.scalar.copy)
+                quantise_wb(1, put[0][:, 0:256].bitcast(BF16))
+                nc.vector.tensor_tensor(put[0][:, cols], inner[0], wgs_sb[:, cols], MULT)
+            else:
+                nc.scalar.copy(jump[2][:], first_c[:])
+                nc.gpsimd.tensor_tensor(inner[0], jump[2][:], gated, ADD)
+                nc.gpsimd.tensor_tensor(first_put[1], inner[0], wgs_sb[:, cols], MULT)
 
         def respond(s, h):
-            bank_b = (bank_b0, bank_b1)[h]
-            for bank, (codes, scales) in zip((bank_b, bank_a, bank_c), weights(s)):
+            bank_b, bank_plain = bank_b0, (bank_c, bank_b1)[h if s > 1 else 0]
+            for bank, (codes, scales) in zip((bank_b, bank_a, bank_plain), weights(s)):
                 for i in range(BLOCKS):
                     nc.tensor.matmul_mx(out=bank[:, block(i)], lhsT=v_w[h][:, block(i)].bitcast(FP8X4),
                                         lhsT_scale=v_s[h][:, block(i)], rhs=codes, rhs_scale=scales,
                                         start=True, stop=True)
-            cols = slice(h * HALF, (h + 1) * HALF)
             nc.scalar.activation(gate[h][:], bank_b[:], SIGMOID)
             nc.scalar.copy(resp[h][:], bank_a[:])
-            nc.scalar.copy(plain[h][:], bank_c[:])
+            nc.scalar.copy(plain[h][:], bank_plain[:])
             nc.gpsimd.tensor_tensor(gate[h][:], resp[h][:], gate[h][:], MULT)
-            add_transposed(bank_d[h], gate[h][:], plain[h][:], 0, BLOCKS)
-            nc.scalar.copy(h_sb[h], bank_d[h][:])
-            nc.gpsimd.tensor_tensor(put[s % 2][:, cols], h_sb[h], wgs_sb[:, cols], MULT)
+
+        def total(s, h):
+            bank = (bank_a, bank_c)[h] if s == SLICES - 1 else bank_d[h]
+            add_transposed(bank, gate[h][:], plain[h][:], BLOCKS)
+            nc.scalar.copy(h_sb[h], bank[:])
+
+        def weigh(s, h):
+            cols = slice(h * HALF, (h + 1) * HALF)
+            nc.gpsimd.tensor_tensor(put_of[s][:, cols], h_sb[h], wgs_sb[:, cols], MULT)
 
         def turn_stiff(s):
             nc.sync.dma_start(out=stiff_sb[s % 2][:], in_=stiff[block(s), :])
@@ -213,22 +237,23 @@ def tile_list_bone_face_features_kernel(
             fetch_outer(s, h, x2)
             fetch_inner(s, h * HALF, (h + 1) * HALF, x1)
 
-        def combine(s, h, x1, x2, bank, k, b0, b1, direct):
-            add_transposed(bank, x2, x1, b0, b1, direct)
+        def combine(s, m0, m1, first, second, bank, spare, one_group=False):
+            count = (m1 - m0) // P
+            h, b0 = divmod(m0 // P, BLOCKS)
+            add_transposed(bank, first, second, count, one_group)
             place = slice(64 * (s % PER_PASS), 64 * (s % PER_PASS + 1))
-            dst = z_t[h][:].rearrange("p (b u r) -> p b u r", b=BLOCKS, u=2)[:, :, :, place]
-            factor = stiff_t[s][:, h * HALF : (h + 1) * HALF]
-            if direct:
-                for b in range(b0, b1):
+            dst = z_t[h][:].rearrange("p (b u r) -> p b u r", b=BLOCKS, u=2)[:, b0 : b0 + count, :, place]
+            factor = stiff_t[s][:, m0:m1]
+            if spare is None:
+                for b in range(count):
                     nc.vector.tensor_tensor(dst[:, b, :, :].rearrange("p u (q e) -> p u q e", e=2),
                                             bank[:, block(b)].rearrange("p (q u e) -> p u q e", u=2, e=2),
                                             factor[:, block(b)].rearrange("p (u q e) -> p u q e", u=2, e=2), MULT)
             else:
-                cols = slice(b0 * P, b1 * P)
-                nc.scalar.copy(out=jump[k][:, cols].rearrange("p (b u q e) -> p b u q e", u=2, q=32, e=2),
-                               in_=bank[:, cols].rearrange("p (b q u e) -> p b u q e", u=2, q=32, e=2))
-                nc.gpsimd.tensor_tensor(dst[:, b0:b1, :, :], jump[k][:, cols].rearrange("p (b u r) -> p b u r", u=2, r=64),
-                                        factor[:, cols].rearrange("p (b u r) -> p b u r", u=2, r=64), MULT)
+                nc.scalar.copy(out=spare.rearrange("p (b u q e) -> p b u q e", u=2, q=32, e=2),
+                               in_=bank[:, 0 : m1 - m0].rearrange("p (b q u e) -> p b u q e", u=2, q=32, e=2))
+                nc.gpsimd.tensor_tensor(dst, spare.rearrange("p (b u r) -> p b u r", u=2, r=64),
+                                        factor.rearrange("p (b u r) -> p b u r", u=2, r=64), MULT)
 
         def turn_back(h, pair, bank, copy):
             words = z_t[h][:].bitcast(F32)
@@ -244,34 +269,39 @@ def tile_list_bone_face_features_kernel(
 
         def product(acc, g, nb, cols, start, stop):
             w_cols = slice(g * N + nb * P, g * N + (nb + 1) * P)
-            nc.tensor.matmul_mx(out=acc, lhsT=wd_w[:, w_cols].bitcast(FP8X4), lhsT_scale=wd_s[:, w_cols],
+            nc.tensor.matmul_mx(out=acc, lhsT=wd_w[0][:, w_cols].bitcast(FP8X4), lhsT_scale=wd_s[:, w_cols],
                                 rhs=z_w[g][:, cols].bitcast(FP8X4), rhs_scale=z_s[g][:, cols], start=start, stop=stop)
 
-        def features_half(out_banks):
-            cols = slice(0, HALF)
-            for nb in range(N // P):
-                for g in range(2):
-                    product(out_banks[nb][:], g, nb, cols, g == 0, g == 1)
-                nc.scalar.copy(staged[nb][:, cols], out_banks[nb][:])
-                nc.sync.dma_start(out=out[block(nb), cols], in_=staged[nb][:, cols])
+        def half_products(nb, bank):
+            for g in range(2):
+                product(bank[:], g, nb, slice(0, HALF), g == 0, g == 1)
 
-        def features_quarter(pair, out_banks):
+        def half_store(nb, bank):
+            cols = slice(0, HALF)
+            nc.scalar.copy(staged[nb][:, cols], bank[:])
+            nc.sync.dma_start(out=out[block(nb), cols], in_=staged[nb][:, cols])
+
+        def quarter_products(pair, out_banks, g):
             width = HALF // 2
             cols = slice(HALF + pair * width, HALF + (pair + 1) * width)
             for b in range(2):
-                for g in range(2):
-                    for a in range(2):
-                        product(out_banks[b][:, a * width : (a + 1) * width], g, 2 * b + a, cols,
-                                g == 0 and a == 0, g == 1 and a == 1)
+                for a in range(2):
+                    product(out_banks[b][:, a * width : (a + 1) * width], g, 2 * b + a, cols,
+                            g == 0 and a == 0, g == 1 and a == 1)
+
+        def quarter_store(pair, out_banks):
+            width = HALF // 2
+            cols = slice(HALF + pair * width, HALF + (pair + 1) * width)
+            for b in range(2):
                 stage = staged[2 * pair + b][:, HALF:F]
                 (nc.scalar.copy, nc.vector.tensor_copy)[b](out=stage, in_=out_banks[b][:])
                 nc.sync.dma_start(out=out[2 * b * P : 2 * (b + 1) * P, cols].rearrange("(a p) m -> p a m", a=2),
                                   in_=stage.rearrange("p (a m) -> p a m", a=2))
 
         def load_wd(g):
-            nc.sync.dma_start(out=wb_raw[2][:], in_=wd[g * K : (g + 1) * K, :].rearrange("(p j) c -> p j c", j=4))
+            nc.sync.dma_start(out=wb_raw[3][:], in_=wd[g * K : (g + 1) * K, :].rearrange("(p j) c -> p j c", j=4))
             for c0 in (0, N // 2):
-                interleave(w_bf[:, 4 * (g * N + c0) : 4 * (g * N + c0 + N // 2)], wb_raw[2][:, :, c0 : c0 + N // 2],
+                interleave(w_bf[:, 4 * (g * N + c0) : 4 * (g * N + c0 + N // 2)], wb_raw[3][:, :, c0 : c0 + N // 2],
                            nc.scalar.copy)
 
         def early(s, h):
@@ -283,13 +313,26 @@ def tile_list_bone_face_features_kernel(
 
         respond_first(0)
         respond_first(1)
-        respond(1, 0)
-        respond(1, 1)
+        for h in range(2):
+            nc.vector.tensor_copy(pages[0][:].indirect(half_of(idx2, h)), first_put[h])
+        for h in range(2):
+            respond(1, h)
+        round_wb(2, outer[0].bitcast(BF16), nc.scalar.copy)
+        quantise_wb(2, outer[0].bitcast(BF16))
+        for h in range(2):
+            total(1, h)
+            weigh(1, h)
+        round_wb(3, w_bf[:, 2048:4096], nc.scalar.copy)
+        for h in range(2):
+            respond(2, h)
+        for h in range(2):
+            total(2, h)
         turn_stiff(0)
+        quarter = HALF // 2
 
         for s in range(SLICES):
             if s > 0:
-                nc.vector.tensor_copy(page_of[s][:].indirect(idx2[:]), put[s % 2][:])
+                nc.vector.tensor_copy(page_of[s][:].indirect(idx2[:]), put_of[s])
             halves = range(2) if s < PER_PASS else range(1)
             if s < PER_PASS:
                 for h in halves:
@@ -297,58 +340,77 @@ def tile_list_bone_face_features_kernel(
                 fetch_inner(s, 0, F, (inner_all, staged[0])[s % 2][:])
             else:
                 fetch(s, 0, *early(s, 0))
-            if s == SLICES - 2:
-                fetch(s - 1, 1, gate[1][:], plain[1][:])
             if s == 0:
-                quantise_wb(2, 512, 1024, nc.scalar.copy)
-            if s + 2 < SLICES:
-                respond(s + 2, 0)
-                respond(s + 2, 1)
+                wb_w.append(one("wb_w1", [P, HALF], U32, "late_wb"))
+                quantise_wb(3, w_bf[:, 2048:4096])
+            for h in range(2):
+                if s + 2 < SLICES:
+                    weigh(s + 2, h)
+            for h in range(2):
+                if s + 3 < SLICES:
+                    respond(s + 3, h)
             if s + 1 < SLICES:
                 turn_stiff(s + 1)
             for h in halves:
                 k = h if s < PER_PASS else s % 2
+                x1, x2 = early(s, h)
                 if s < SLICES - 1:
-                    combine(s, h, *early(s, h), bank_d[h if s < PER_PASS else 1], k, 0, BLOCKS, False)
+                    combine(s, h * HALF, (h + 1) * HALF, x2, x1, (bank_d[h], bank_b0, bank_b1, bank_d1)[max(0, s - 3)], jump[k][:])
                 else:
                     for pair in range(2):
-                        combine(s, h, *early(s, h), bank_d[pair], k, 2 * pair, 2 * pair + 2, False)
-            if s == SLICES - 2:
-                combine(s - 1, 1, gate[1][:], plain[1][:], bank_d0, 2, 0, BLOCKS, False)
-            if s in (1, 2):
-                load_wd(s - 1)
+                        cols = slice(pair * quarter, (pair + 1) * quarter)
+                        combine(s, cols.start, cols.stop, x2[:, cols], x1[:, cols], bank_d[pair], jump[k][:, cols])
+            for h in range(2):
+                if s + 3 < SLICES:
+                    total(s + 3, h)
+            if s in (0, 1):
+                load_wd(s)
+            if s == 2:
+                wd_w.append(one("wd_w", [P, 2 * N], U32, "late_wd"))
+                nc.vector.quantize_mx(out=wd_w[0][:].bitcast(FP8X4), scales=wd_s[:], in_=w_bf[:])
             if s == PER_PASS - 1:
-                nc.vector.quantize_mx(out=wd_w[:].bitcast(FP8X4), scales=wd_s[:], in_=w_bf[:])
-                for h, pair in ((0, 0), (0, 1), (1, 0)):
+                for h, pair in ((0, 0), (0, 1), (1, 0), (1, 1)):
                     turn_back(h, pair, bank_o[pair], nc.scalar.copy)
             if s == SLICES - 3:
-                turn_back(1, 1, bank_o1, nc.scalar.copy)
+                z_w.setdefault(0, one("z_w0", [P, F], U32, "late_z"))
                 quantise_z(0, 0, F)
 
-        quarter = HALF // 2
-        late = {
-            4: (put[1][:, 0:HALF], put[1][:, HALF:S]),
-            6: (inner[1], outer[1]),
-            7: (z_words[:, 0:HALF], outer[0]),
-        }
-        for k, s in enumerate((4, 6)):
-            fetch(s, 1, *late[s])
-            combine(s, 1, *late[s], (bank_d0, bank_o1)[k], 2 * k, 0, BLOCKS, False)
-            if k == 0:
-                turn_back(0, 0, bank_o1, nc.scalar.copy)
-                turn_back(0, 1, bank_d1, nc.scalar.copy)
-        quantise_z(1, 0, HALF)
+        def piece(tile, k):
+            return tile[:, k * quarter : (k + 1) * quarter]
+
+        third, fourth = (HALF, HALF + quarter), (HALF + quarter, F)
         wide = (bank_a, bank_b0, bank_b1, bank_c)
-        s = SLICES - 1
-        x1, x2 = late[s]
-        fetch_outer(s, 1, x2)
+        x2 = {4: put[1][:, 0:HALF], 5: outer[1], 6: z_words[:, 0:HALF], 7: outer[1]}
+        x1 = {4: put[1][:, HALF:S], 5: inner[1], 6: z_words[:, HALF:F]}
+        x1_last = (piece(x2[6], 0), piece(x1[6], 0))
         for pair in range(2):
-            fetch_inner(s, HALF + pair * quarter, HALF + (pair + 1) * quarter, x1[:, pair * quarter : (pair + 1) * quarter])
-        for pair in range(2):
-            combine(s, 1, x1, x2, bank_d[pair], pair, 2 * pair, 2 * pair + 2, True)
-        features_half(wide)
-        for pair in range(2):
-            turn_back(1, pair, bank_d[pair], (nc.vector.tensor_copy, nc.scalar.copy)[pair])
-            quantise_z(1, HALF + pair * quarter, HALF + (pair + 1) * quarter)
-        features_quarter(0, (bank_o0, bank_o1))
-        features_quarter(1, (bank_a, bank_b0))
+            turn_back(0, pair, bank_o[pair], nc.scalar.copy)
+        for s in (4, 5):
+            fetch(s, 1, x1[s], x2[s])
+            combine(s, HALF, F, x1[s], x2[s], bank_o[s % 2], jump[2 * (s % 2)][:])
+        quantise_z(1, 0, HALF)
+        for nb in range(N // P):
+            half_products(nb, wide[nb])
+        fetch(6, 1, x1[6], x2[6])
+        fetch_outer(7, 1, x2[7])
+        for k, cols in enumerate((third, fourth)):
+            combine(6, *cols, piece(x2[6], k), piece(x1[6], k), bank_d[k], piece(gate[0], k), True)
+        for k, cols in enumerate((third, fourth)):
+            fetch_inner(7, *cols, x1_last[k])
+        third_banks = (bank_o1, bank_d0)
+        for nb in range(2):
+            half_store(nb, wide[nb])
+        quarter_products(1, wide[:2], 0)
+        for k, cols in enumerate((third, fourth)):
+            combine(7, *cols, piece(x2[7], k), x1_last[k], bank_o[k], None, True)
+        turn_back(1, 0, bank_d0, nc.scalar.copy)
+        turn_back(1, 1, bank_d1, nc.vector.tensor_copy)
+        for nb in range(2, 4):
+            half_store(nb, wide[nb])
+        quarter_products(0, third_banks, 0)
+        quantise_z(1, *third)
+        quantise_z(1, *fourth)
+        quarter_products(0, third_banks, 1)
+        quarter_products(1, wide[:2], 1)
+        quarter_store(0, third_banks)
+        quarter_store(1, wide[:2])

@@ -23,6 +23,8 @@ HALF = 512
 BLOCKS = HALF // P
 SLICES = H // P
 PER_PASS = 4
+QUANTISE_BEHIND = ((3, 1), (4, 1), (7, 0))
+DEFERRED = {0: 1, 1: 1, 4: 0, 5: 0}
 WB_CHUNKS = ((0, 128), (128, 256), (256, 512), (512, 1024))
 
 
@@ -64,22 +66,22 @@ def tile_list_bone_face_features_kernel(
         wc_w = one("wc_w", [P, H], U32)
         wa_s = one("wa_s", [P, H], U8)
         wc_s = one("wc_s", [P, H], U8)
-        wb_raw = [one("wb_raw%d" % i, [P, 4, c1 - c0], F32) for i, (c0, c1) in enumerate(WB_CHUNKS)]
+        wb_raw = [one("wb_raw%d" % i, [P, 4, c1 - c0], F32, "last_page" if c1 == H else "")
+                  for i, (c0, c1) in enumerate(WB_CHUNKS)]
         w_bf = one("w_bf", [P, 4 * H], BF16)
-        wb_w = [one("wb_w0", [P, HALF], U32)]
+        wb_w = tiles("wb_w", 2, [P, HALF], U32)
         wb_s = one("wb_s", [P, H], U8)
         wd_w = []
         wd_s = one("wd_s", [P, 2 * N], U8)
         wgs_sb = one("wgs_sb", [P, S], F32)
-        pages = tiles("page", 4, [P, T2], F32)
-        page_of = [pages[i] for i in (0, 1, 0, 1, 0, 1, 2, 3)]
+        pages = tiles("page", 3, [P, T2], F32)
+        page_of = [pages[i] for i in (0, 1, 0, 1, 0, 1, 2)]
         gate = tiles("gate", 2, [P, HALF], F32)
         resp = tiles("resp", 2, [P, HALF], F32)
         plain = tiles("plain", 2, [P, HALF], F32)
         put = tiles("put", 2, [P, S], F32)
-        first_put = (put[0][:, 0:HALF], one("first_put", [P, HALF], F32, "late_wb")[:])
+        first_put = (put[0][:, 0:HALF], put[0][:, HALF:S])
         put_of = [put[s % 2][:] for s in range(SLICES)]
-        put_of[2] = one("put_2", [P, S], F32, "late_wd")[:]
         inner_all = one("inner", [P, F], F32)
         outer_all = one("outer", [P, F], F32)
         inner = (inner_all[:, 0:HALF], inner_all[:, HALF:F])
@@ -92,7 +94,11 @@ def tile_list_bone_face_features_kernel(
         h_sb = [t[:] for t in tiles("h_sb", 2, [P, HALF], F32)]
         z_w = {1: one("z_w1", [P, F], U32)}
         z_s = tiles("z_s", 2, [P, F], U8)
-        put_of[5] = one("put_5", [P, S], F32, "late_z")[:]
+        h_of = {(s, h): h_sb[h] for s in range(1, SLICES) for h in range(2)}
+        for s, h in QUANTISE_BEHIND:
+            h_of[s, h] = one("h_%d" % s, [P, HALF], F32, "behind%d" % s)[:]
+        for s in DEFERRED:
+            h_of[s + 1, 1] = one("h_%d" % (s + 1), [P, HALF], F32)[:]
         staged = tiles("staged", 4, [P, F], F32)
 
         nc.vector.memset(tab_s[:, 0 : T // 2].bitcast(I32), 0)
@@ -185,7 +191,7 @@ def tile_list_bone_face_features_kernel(
             for bank, (codes, scales) in zip((first_b, first_a, first_c), weights(0)):
                 nc.tensor.matmul_mx(out=bank[:], lhsT=codes, lhsT_scale=scales, rhs=v_w[h][:].bitcast(FP8X4),
                                     rhs_scale=v_s[h][:], start=True, stop=True)
-            first_gate = (first_put[0], jump[1][:])[h]
+            first_gate = (first_put[0], wb_raw[1][:].rearrange("p j c -> p (j c)"))[h]
             nc.scalar.activation(first_gate, first_b[:], SIGMOID)
             nc.vector.tensor_tensor(gated, first_a[:], first_gate, MULT)
             if h == 0:
@@ -211,21 +217,21 @@ def tile_list_bone_face_features_kernel(
             nc.gpsimd.tensor_tensor(gate[h][:], resp[h][:], gate[h][:], MULT)
 
         def total(s, h):
-            bank = (bank_a, bank_c)[h] if s == SLICES - 1 else bank_d[h]
+            bank = (bank_c, bank_a)[h] if s == SLICES - 1 else bank_d[h]
             add_transposed(bank, gate[h][:], plain[h][:], BLOCKS)
-            nc.scalar.copy(h_sb[h], bank[:])
+            nc.scalar.copy(h_of[s, h], bank[:])
 
         def weigh(s, h):
             cols = slice(h * HALF, (h + 1) * HALF)
-            nc.gpsimd.tensor_tensor(put_of[s][:, cols], h_sb[h], wgs_sb[:, cols], MULT)
+            nc.gpsimd.tensor_tensor(put_of[s][:, cols], h_of[s, h], wgs_sb[:, cols], MULT)
 
         def turn_stiff(s):
             nc.sync.dma_start(out=stiff_sb[s % 2][:], in_=stiff[block(s), :])
-            for h in range(2):
+            for h, bank in enumerate(bank_o):
                 for i in range(BLOCKS):
-                    nc.tensor.transpose(bank_o[h][:, block(i)], stiff_sb[s % 2][:, block(BLOCKS * h + i)], ident[:])
+                    nc.tensor.transpose(bank[:, block(i)], stiff_sb[s % 2][:, block(BLOCKS * h + i)], ident[:])
                 nc.scalar.copy(out=stiff_t[s][:, h * HALF : (h + 1) * HALF].rearrange("p (b u q e) -> p b u q e", u=2, q=32, e=2),
-                               in_=bank_o[h][:].rearrange("p (b q u e) -> p b u q e", u=2, q=32, e=2))
+                               in_=bank[:].rearrange("p (b q u e) -> p b u q e", u=2, q=32, e=2))
 
         def fetch_outer(s, h, x2):
             nc.vector.tensor_scalar(x2, page_of[s][:].indirect(half_of(idx4, h)), -1.0, 1.0, MULT, ADD)
@@ -269,7 +275,7 @@ def tile_list_bone_face_features_kernel(
 
         def product(acc, g, nb, cols, start, stop):
             w_cols = slice(g * N + nb * P, g * N + (nb + 1) * P)
-            nc.tensor.matmul_mx(out=acc, lhsT=wd_w[0][:, w_cols].bitcast(FP8X4), lhsT_scale=wd_s[:, w_cols],
+            nc.tensor.matmul_mx(out=acc, lhsT=wd_w[g][:, block(nb)].bitcast(FP8X4), lhsT_scale=wd_s[:, w_cols],
                                 rhs=z_w[g][:, cols].bitcast(FP8X4), rhs_scale=z_s[g][:, cols], start=start, stop=stop)
 
         def half_products(nb, bank):
@@ -281,22 +287,23 @@ def tile_list_bone_face_features_kernel(
             nc.scalar.copy(staged[nb][:, cols], bank[:])
             nc.sync.dma_start(out=out[block(nb), cols], in_=staged[nb][:, cols])
 
-        def quarter_products(pair, out_banks, g):
+        def quarter_products(pair, b, bank, g, alone=False):
             width = HALF // 2
             cols = slice(HALF + pair * width, HALF + (pair + 1) * width)
-            for b in range(2):
-                for a in range(2):
-                    product(out_banks[b][:, a * width : (a + 1) * width], g, 2 * b + a, cols,
-                            g == 0 and a == 0, g == 1 and a == 1)
+            for a in range(2):
+                product(bank[:, a * width : (a + 1) * width], g, 2 * b + a, cols,
+                        (alone or g == 0) and a == 0, (alone or g == 1) and a == 1)
 
-        def quarter_store(pair, out_banks):
+        def quarter_store(pair, b, bank):
             width = HALF // 2
             cols = slice(HALF + pair * width, HALF + (pair + 1) * width)
-            for b in range(2):
-                stage = staged[2 * pair + b][:, HALF:F]
-                (nc.scalar.copy, nc.vector.tensor_copy)[b](out=stage, in_=out_banks[b][:])
-                nc.sync.dma_start(out=out[2 * b * P : 2 * (b + 1) * P, cols].rearrange("(a p) m -> p a m", a=2),
-                                  in_=stage.rearrange("p (a m) -> p a m", a=2))
+            stage = staged[2 * pair + b][:, HALF:F]
+            if b == 0:
+                nc.scalar.copy(stage, bank[:])
+            else:
+                nc.vector.tensor_tensor(stage, bank[:], resp[pair][:], ADD)
+            nc.sync.dma_start(out=out[2 * b * P : 2 * (b + 1) * P, cols].rearrange("(a p) m -> p a m", a=2),
+                              in_=stage.rearrange("p (a m) -> p a m", a=2))
 
         def load_wd(g):
             nc.sync.dma_start(out=wb_raw[3][:], in_=wd[g * K : (g + 1) * K, :].rearrange("(p j) c -> p j c", j=4))
@@ -306,10 +313,14 @@ def tile_list_bone_face_features_kernel(
 
         def early(s, h):
             if s >= PER_PASS:
-                return inner[s % 2], outer[s % 2]
-            if s % 2 == 0:
-                return inner[h], outer[h]
-            return staged[0][:, h * HALF : (h + 1) * HALF], staged[1][:, h * HALF : (h + 1) * HALF]
+                x1, x2 = inner[s % 2], outer[s % 2]
+            elif s % 2 == 0:
+                x1, x2 = inner[h], outer[h]
+            else:
+                x1, x2 = staged[0][:, h * HALF : (h + 1) * HALF], staged[1][:, h * HALF : (h + 1) * HALF]
+            if DEFERRED.get(s) == h:
+                return h_of[s + 1, 1], staged[3][:, s % 2 * HALF : (s % 2 + 1) * HALF]
+            return x1, x2
 
         respond_first(0)
         respond_first(1)
@@ -322,7 +333,7 @@ def tile_list_bone_face_features_kernel(
         for h in range(2):
             total(1, h)
             weigh(1, h)
-        round_wb(3, w_bf[:, 2048:4096], nc.scalar.copy)
+        round_wb(3, staged[2][:].bitcast(BF16), nc.scalar.copy)
         for h in range(2):
             respond(2, h)
         for h in range(2):
@@ -333,29 +344,43 @@ def tile_list_bone_face_features_kernel(
         for s in range(SLICES):
             if s > 0:
                 nc.vector.tensor_copy(page_of[s][:].indirect(idx2[:]), put_of[s])
+            if s - 1 in DEFERRED:
+                h = DEFERRED[s - 1]
+                fetch_inner(s - 1, h * HALF, (h + 1) * HALF, early(s - 1, h)[0])
+            if s in (3, 4):
+                g = s - 3
+                wd_w.append(one("wd_w%d" % g, [P, N], U32, "behind%d" % s))
+                nc.vector.quantize_mx(out=wd_w[g][:].bitcast(FP8X4), scales=wd_s[:, g * N : (g + 1) * N],
+                                      in_=w_bf[:, 4 * g * N : 4 * (g + 1) * N])
             halves = range(2) if s < PER_PASS else range(1)
-            if s < PER_PASS:
-                for h in halves:
-                    fetch_outer(s, h, early(s, h)[1])
+            for h in halves:
+                fetch_outer(s, h, early(s, h)[1])
+            if s in (2, 3):
                 fetch_inner(s, 0, F, (inner_all, staged[0])[s % 2][:])
-            else:
-                fetch(s, 0, *early(s, 0))
+            elif DEFERRED.get(s) != 0:
+                fetch_inner(s, 0, HALF, early(s, 0)[0])
             if s == 0:
-                wb_w.append(one("wb_w1", [P, HALF], U32, "late_wb"))
-                quantise_wb(3, w_bf[:, 2048:4096])
+                quantise_wb(3, staged[2][:].bitcast(BF16))
+            if s == 6:
+                z_w.setdefault(0, one("z_w0", [P, F], U32, "behind7"))
+                quantise_z(0, 0, F)
+                for pair in range(2):
+                    quarter_products(pair, 1, bank_d[pair], 0, True)
+                    nc.scalar.copy(resp[pair][:], bank_d[pair][:])
             for h in range(2):
                 if s + 2 < SLICES:
                     weigh(s + 2, h)
             for h in range(2):
                 if s + 3 < SLICES:
                     respond(s + 3, h)
-            if s + 1 < SLICES:
-                turn_stiff(s + 1)
-            for h in halves:
-                k = h if s < PER_PASS else s % 2
-                x1, x2 = early(s, h)
-                if s < SLICES - 1:
-                    combine(s, h * HALF, (h + 1) * HALF, x2, x1, (bank_d[h], bank_b0, bank_b1, bank_d1)[max(0, s - 3)], jump[k][:])
+            ready = [(s - 1, DEFERRED[s - 1])] if s - 1 in DEFERRED else []
+            ready = ready + [(s, h) for h in halves if DEFERRED.get(s) != h]
+            for k, (r, h) in enumerate(ready):
+                x1, x2 = early(r, h)
+                if r < SLICES - 1:
+                    bank = (bank_b1, bank_b0, bank_a)[k] if s < SLICES - 2 else bank_a
+                    spare = z_words[:, 3 * HALF : 4 * HALF] if r == 5 else jump[k][:]
+                    combine(r, h * HALF, (h + 1) * HALF, x2, x1, bank, spare)
                 else:
                     for pair in range(2):
                         cols = slice(pair * quarter, (pair + 1) * quarter)
@@ -363,17 +388,16 @@ def tile_list_bone_face_features_kernel(
             for h in range(2):
                 if s + 3 < SLICES:
                     total(s + 3, h)
+            if s + 1 < SLICES:
+                turn_stiff(s + 1)
             if s in (0, 1):
                 load_wd(s)
             if s == 2:
-                wd_w.append(one("wd_w", [P, 2 * N], U32, "late_wd"))
-                nc.vector.quantize_mx(out=wd_w[0][:].bitcast(FP8X4), scales=wd_s[:], in_=w_bf[:])
+                page_of.append(one("last_page", [P, T2], F32, "last_page"))
+                nc.gpsimd.memset(page_of[-1][:], 0.0)
             if s == PER_PASS - 1:
                 for h, pair in ((0, 0), (0, 1), (1, 0), (1, 1)):
                     turn_back(h, pair, bank_o[pair], nc.scalar.copy)
-            if s == SLICES - 3:
-                z_w.setdefault(0, one("z_w0", [P, F], U32, "late_z"))
-                quantise_z(0, 0, F)
 
         def piece(tile, k):
             return tile[:, k * quarter : (k + 1) * quarter]
@@ -397,20 +421,21 @@ def tile_list_bone_face_features_kernel(
             combine(6, *cols, piece(x2[6], k), piece(x1[6], k), bank_d[k], piece(gate[0], k), True)
         for k, cols in enumerate((third, fourth)):
             fetch_inner(7, *cols, x1_last[k])
-        third_banks = (bank_o1, bank_d0)
         for nb in range(2):
             half_store(nb, wide[nb])
-        quarter_products(1, wide[:2], 0)
+        quarter_products(1, 0, bank_a, 0)
         for k, cols in enumerate((third, fourth)):
             combine(7, *cols, piece(x2[7], k), x1_last[k], bank_o[k], None, True)
         turn_back(1, 0, bank_d0, nc.scalar.copy)
-        turn_back(1, 1, bank_d1, nc.vector.tensor_copy)
+        turn_back(1, 1, bank_d1, nc.scalar.copy)
         for nb in range(2, 4):
             half_store(nb, wide[nb])
-        quarter_products(0, third_banks, 0)
+        quarter_products(0, 0, bank_d0, 0)
         quantise_z(1, *third)
         quantise_z(1, *fourth)
-        quarter_products(0, third_banks, 1)
-        quarter_products(1, wide[:2], 1)
-        quarter_store(0, third_banks)
-        quarter_store(1, wide[:2])
+        for pair, pair_banks in enumerate(((bank_d0, bank_o0), (bank_a, bank_b0))):
+            for b in range(2):
+                quarter_products(pair, b, pair_banks[b], 1, b == 1)
+        for pair, pair_banks in enumerate(((bank_d0, bank_o0), (bank_a, bank_b0))):
+            for b in range(2):
+                quarter_store(pair, b, pair_banks[b])

@@ -23,8 +23,8 @@ HALF = 512
 BLOCKS = HALF // P
 SLICES = H // P
 PER_PASS = 4
-QUANTISE_BEHIND = ((3, 1), (4, 1), (7, 0))
-DEFERRED = {0: 1, 1: 1, 4: 0, 5: 0}
+QUANTISE_BEHIND = (6,)
+DEFERRED = {0: 1, 1: 1, 2: 1, 3: 1, 4: 0}
 WB_CHUNKS = ((0, 128), (128, 256), (256, 512), (512, 1024))
 
 
@@ -76,9 +76,10 @@ def tile_list_bone_face_features_kernel(
         wgs_sb = one("wgs_sb", [P, S], F32)
         pages = tiles("page", 3, [P, T2], F32)
         page_of = [pages[i] for i in (0, 1, 0, 1, 0, 1, 2)]
-        gate = tiles("gate", 2, [P, HALF], F32)
-        resp = tiles("resp", 2, [P, HALF], F32)
-        plain = tiles("plain", 2, [P, HALF], F32)
+        gate_all = one("gate", [P, S], F32)
+        resp_all = one("resp", [P, S], F32)
+        plain_all = one("plain", [P, S], F32)
+        gate, resp, plain = ((t[:, 0:HALF], t[:, HALF:S]) for t in (gate_all, resp_all, plain_all))
         put = tiles("put", 2, [P, S], F32)
         first_put = (put[0][:, 0:HALF], put[0][:, HALF:S])
         put_of = [put[s % 2][:] for s in range(SLICES)]
@@ -91,14 +92,13 @@ def tile_list_bone_face_features_kernel(
         stiff_t = tiles("stiff_t", SLICES, [P, F], F32)
         z_t = tiles("z_t", 2, [P, BLOCKS * HALF], BF16)
         z_words = one("z_words", [P, 2 * F], F32)
-        h_sb = [t[:] for t in tiles("h_sb", 2, [P, HALF], F32)]
-        z_w = {1: one("z_w1", [P, F], U32)}
+        z_w = tiles("z_w", 2, [P, F], U32)
         z_s = tiles("z_s", 2, [P, F], U8)
-        h_of = {(s, h): h_sb[h] for s in range(1, SLICES) for h in range(2)}
-        for s, h in QUANTISE_BEHIND:
-            h_of[s, h] = one("h_%d" % s, [P, HALF], F32, "behind%d" % s)[:]
-        for s in DEFERRED:
-            h_of[s + 1, 1] = one("h_%d" % (s + 1), [P, HALF], F32)[:]
+        h_ring = tiles("h_ring", 3, [P, S], F32)
+        h_of = {s: h_ring[s % 3] for s in range(1, SLICES)}
+        for s in QUANTISE_BEHIND:
+            h_of[s] = one("h_%d" % s, [P, S], F32, "behind%d" % s)
+        h_of[SLICES - 1] = z_t[1][:].bitcast(F32)
         staged = tiles("staged", 4, [P, F], F32)
 
         nc.vector.memset(tab_s[:, 0 : T // 2].bitcast(I32), 0)
@@ -167,15 +167,18 @@ def tile_list_bone_face_features_kernel(
         def block(i):
             return slice(i * P, (i + 1) * P)
 
-        def add_transposed(bank, x, y, count, one_group=False):
-            steps = [(term, i) for i in range(count) for term in (0, 1)]
-            if one_group:
-                steps = sorted(steps)
-            for n, (term, i) in enumerate(steps):
-                start = n == 0 if one_group else term == 0
-                stop = n == len(steps) - 1 if one_group else term == 1
-                nc.tensor.matmul(bank[:, block(i)], (x, y)[term][:, block(i)], ident[:], start=start, stop=stop,
-                                 is_transpose=True)
+        def weave(*runs):
+            for k in range(max(len(run) for run in runs)):
+                for run in runs:
+                    if k < len(run):
+                        run[k]()
+
+        def turning(out_ap, in_ap, start, stop):
+            return lambda: nc.tensor.matmul(out_ap, in_ap, ident[:], start=start, stop=stop, is_transpose=True)
+
+        def add_transposed(bank, x, y, count):
+            return [turning(bank[:, block(i)], (x, y)[term][:, block(i)], term + i == 0, term + i == count)
+                    for term in (0, 1) for i in range(count)]
 
         def weights(s):
             return (
@@ -183,6 +186,8 @@ def tile_list_bone_face_features_kernel(
                 (wa_w[:, 2 * P * s : 2 * P * (s + 1)].bitcast(FP4X4), wa_s[:, block(s)]),
                 (wc_w[:, block(s)].bitcast(FP8X4), wc_s[:, block(s)]),
             )
+
+        first_banks = ((bank_b0, bank_a, bank_c), (bank_b1, bank_o0, bank_o1))
 
         def respond_first(h):
             cols = slice(h * HALF, (h + 1) * HALF)
@@ -204,34 +209,49 @@ def tile_list_bone_face_features_kernel(
                 nc.gpsimd.tensor_tensor(inner[0], jump[2][:], gated, ADD)
                 nc.gpsimd.tensor_tensor(first_put[1], inner[0], wgs_sb[:, cols], MULT)
 
-        def respond(s, h):
-            bank_b, bank_plain = bank_b0, (bank_c, bank_b1)[h if s > 1 else 0]
-            for bank, (codes, scales) in zip((bank_b, bank_a, bank_plain), weights(s)):
+        def respond(s):
+            sets = first_banks if s > 1 else first_banks[:1] * 2
+            for part in ((0, 1),) if s > 1 else ((0,), (1,)):
                 for i in range(BLOCKS):
-                    nc.tensor.matmul_mx(out=bank[:, block(i)], lhsT=v_w[h][:, block(i)].bitcast(FP8X4),
-                                        lhsT_scale=v_s[h][:, block(i)], rhs=codes, rhs_scale=scales,
-                                        start=True, stop=True)
-            nc.scalar.activation(gate[h][:], bank_b[:], SIGMOID)
-            nc.scalar.copy(resp[h][:], bank_a[:])
-            nc.scalar.copy(plain[h][:], bank_plain[:])
-            nc.gpsimd.tensor_tensor(gate[h][:], resp[h][:], gate[h][:], MULT)
+                    for h in part:
+                        for bank, (codes, scales) in zip(sets[h], weights(s)):
+                            nc.tensor.matmul_mx(out=bank[:, block(i)], lhsT=v_w[h][:, block(i)].bitcast(FP8X4),
+                                                lhsT_scale=v_s[h][:, block(i)], rhs=codes, rhs_scale=scales,
+                                                start=True, stop=True)
+                for h in part:
+                    nc.scalar.activation(gate[h], sets[h][0][:], SIGMOID)
+                    nc.scalar.copy(resp[h], sets[h][1][:])
+                for h in part:
+                    nc.scalar.copy(plain[h], sets[h][2][:])
+                for cols in [slice(h * HALF, (h + 1) * HALF) for h in part] if s < 3 else [slice(0, S)]:
+                    nc.gpsimd.tensor_tensor(gate_all[:, cols], resp_all[:, cols], gate_all[:, cols], MULT)
 
-        def total(s, h):
-            bank = (bank_c, bank_a)[h] if s == SLICES - 1 else bank_d[h]
-            add_transposed(bank, gate[h][:], plain[h][:], BLOCKS)
-            nc.scalar.copy(h_of[s, h], bank[:])
+        def total(s, turned):
+            quarters = [slice(k * HALF // 2, (k + 1) * HALF // 2) for k in (0, 2, 1, 3)]
+            four = (bank_a, bank_o0, bank_c, bank_o1)
+            runs = [add_transposed(bank, gate_all[:, cols], plain_all[:, cols], 2) for bank, cols in zip(four, quarters)]
+            weave(*(run[:2] for run in runs))
+            turns = [stiff_turns(turned, h, (bank_b0, bank_b1)[h]) for h in range(2)]
+            weave(*(run[2:3] for run in runs), *(run[:2] for run in turns))
+            weave(*(run[3:] for run in runs), *(run[2:] for run in turns))
+            for bank, cols in zip(four, quarters):
+                nc.scalar.copy(h_of[s][:, cols], bank[:, 0 : HALF // 2])
+            for h in range(2):
+                keep_stiff(turned, h, (bank_b0, bank_b1)[h])
 
-        def weigh(s, h):
-            cols = slice(h * HALF, (h + 1) * HALF)
-            nc.gpsimd.tensor_tensor(put_of[s][:, cols], h_of[s, h], wgs_sb[:, cols], MULT)
+        def weigh(s, cols=slice(0, S)):
+            nc.gpsimd.tensor_tensor(put_of[s][:, cols], h_of[s][:, cols], wgs_sb[:, cols], MULT)
 
-        def turn_stiff(s):
+        def load_stiff(s):
             nc.sync.dma_start(out=stiff_sb[s % 2][:], in_=stiff[block(s), :])
-            for h, bank in enumerate(bank_o):
-                for i in range(BLOCKS):
-                    nc.tensor.transpose(bank[:, block(i)], stiff_sb[s % 2][:, block(BLOCKS * h + i)], ident[:])
-                nc.scalar.copy(out=stiff_t[s][:, h * HALF : (h + 1) * HALF].rearrange("p (b u q e) -> p b u q e", u=2, q=32, e=2),
-                               in_=bank[:].rearrange("p (b q u e) -> p b u q e", u=2, q=32, e=2))
+
+        def stiff_turns(s, h, bank):
+            return [turning(bank[:, block(i)], stiff_sb[s % 2][:, block(BLOCKS * h + i)], True, True)
+                    for i in range(BLOCKS)]
+
+        def keep_stiff(s, h, bank):
+            nc.scalar.copy(out=stiff_t[s][:, h * HALF : (h + 1) * HALF].rearrange("p (b u q e) -> p b u q e", u=2, q=32, e=2),
+                           in_=bank[:].rearrange("p (b q u e) -> p b u q e", u=2, q=32, e=2))
 
         def fetch_outer(s, h, x2):
             nc.vector.tensor_scalar(x2, page_of[s][:].indirect(half_of(idx4, h)), -1.0, 1.0, MULT, ADD)
@@ -243,10 +263,9 @@ def tile_list_bone_face_features_kernel(
             fetch_outer(s, h, x2)
             fetch_inner(s, h * HALF, (h + 1) * HALF, x1)
 
-        def combine(s, m0, m1, first, second, bank, spare, one_group=False):
+        def combine(s, m0, m1, bank, spare):
             count = (m1 - m0) // P
             h, b0 = divmod(m0 // P, BLOCKS)
-            add_transposed(bank, first, second, count, one_group)
             place = slice(64 * (s % PER_PASS), 64 * (s % PER_PASS + 1))
             dst = z_t[h][:].rearrange("p (b u r) -> p b u r", b=BLOCKS, u=2)[:, b0 : b0 + count, :, place]
             factor = stiff_t[s][:, m0:m1]
@@ -261,10 +280,11 @@ def tile_list_bone_face_features_kernel(
                 nc.gpsimd.tensor_tensor(dst, spare.rearrange("p (b u r) -> p b u r", u=2, r=64),
                                         factor.rearrange("p (b u r) -> p b u r", u=2, r=64), MULT)
 
-        def turn_back(h, pair, bank, copy):
+        def back_turns(h, pair, bank):
             words = z_t[h][:].bitcast(F32)
-            for i in range(BLOCKS):
-                nc.tensor.transpose(bank[:, block(i)], words[:, block(BLOCKS * pair + i)], ident[:])
+            return [turning(bank[:, block(i)], words[:, block(BLOCKS * pair + i)], True, True) for i in range(BLOCKS)]
+
+        def keep_back(h, pair, bank, copy):
             first = 2 * (h * HALF + pair * 256)
             copy(out=z_words[:, first : first + 512].rearrange("p (b m u) -> p b m u", b=2, u=2),
                  in_=bank[:].rearrange("p (b u m) -> p b m u", b=2, u=2))
@@ -275,12 +295,12 @@ def tile_list_bone_face_features_kernel(
 
         def product(acc, g, nb, cols, start, stop):
             w_cols = slice(g * N + nb * P, g * N + (nb + 1) * P)
-            nc.tensor.matmul_mx(out=acc, lhsT=wd_w[g][:, block(nb)].bitcast(FP8X4), lhsT_scale=wd_s[:, w_cols],
+            return lambda: nc.tensor.matmul_mx(out=acc, lhsT=wd_w[0][:, w_cols].bitcast(FP8X4), lhsT_scale=wd_s[:, w_cols],
                                 rhs=z_w[g][:, cols].bitcast(FP8X4), rhs_scale=z_s[g][:, cols], start=start, stop=stop)
 
-        def half_products(nb, bank):
-            for g in range(2):
-                product(bank[:], g, nb, slice(0, HALF), g == 0, g == 1)
+        def half_products(g, out_banks):
+            for nb, bank in enumerate(out_banks):
+                product(bank[:], g, nb, slice(0, HALF), g == 0, g == 1)()
 
         def half_store(nb, bank):
             cols = slice(0, HALF)
@@ -290,9 +310,8 @@ def tile_list_bone_face_features_kernel(
         def quarter_products(pair, b, bank, g, alone=False):
             width = HALF // 2
             cols = slice(HALF + pair * width, HALF + (pair + 1) * width)
-            for a in range(2):
-                product(bank[:, a * width : (a + 1) * width], g, 2 * b + a, cols,
-                        (alone or g == 0) and a == 0, (alone or g == 1) and a == 1)
+            return [product(bank[:, a * width : (a + 1) * width], g, 2 * b + a, cols,
+                            (alone or g == 0) and a == 0, (alone or g == 1) and a == 1) for a in range(2)]
 
         def quarter_store(pair, b, bank):
             width = HALF // 2
@@ -301,7 +320,7 @@ def tile_list_bone_face_features_kernel(
             if b == 0:
                 nc.scalar.copy(stage, bank[:])
             else:
-                nc.vector.tensor_tensor(stage, bank[:], resp[pair][:], ADD)
+                nc.vector.tensor_tensor(stage, bank[:], resp[pair], ADD)
             nc.sync.dma_start(out=out[2 * b * P : 2 * (b + 1) * P, cols].rearrange("(a p) m -> p a m", a=2),
                               in_=stage.rearrange("p (a m) -> p a m", a=2))
 
@@ -312,34 +331,37 @@ def tile_list_bone_face_features_kernel(
                            nc.scalar.copy)
 
         def early(s, h):
-            if s >= PER_PASS:
-                x1, x2 = inner[s % 2], outer[s % 2]
-            elif s % 2 == 0:
-                x1, x2 = inner[h], outer[h]
-            else:
-                x1, x2 = staged[0][:, h * HALF : (h + 1) * HALF], staged[1][:, h * HALF : (h + 1) * HALF]
             if DEFERRED.get(s) == h:
-                return h_of[s + 1, 1], staged[3][:, s % 2 * HALF : (s % 2 + 1) * HALF]
-            return x1, x2
+                kept = (staged[0][:, HALF:F], staged[3][:, 0:HALF], staged[1][:, HALF:F], staged[3][:, HALF:F],
+                        staged[2][:, HALF:F])
+                return h_of[s + 1][:, HALF:S], kept[s]
+            if s >= PER_PASS:
+                return inner[s % 2], outer[s % 2]
+            return (inner[0], outer[0]) if s % 2 == 0 else (staged[0][:, 0:HALF], staged[1][:, 0:HALF])
 
         respond_first(0)
         respond_first(1)
         for h in range(2):
             nc.vector.tensor_copy(pages[0][:].indirect(half_of(idx2, h)), first_put[h])
-        for h in range(2):
-            respond(1, h)
+        respond(1)
         round_wb(2, outer[0].bitcast(BF16), nc.scalar.copy)
         quantise_wb(2, outer[0].bitcast(BF16))
+        load_stiff(0)
         for h in range(2):
-            total(1, h)
-            weigh(1, h)
+            cols = slice(h * HALF, (h + 1) * HALF)
+            two = ((bank_a, bank_c), (bank_b0, bank_b1))[h]
+            parts = [slice(cols.start + k * HALF // 2, cols.start + (k + 1) * HALF // 2) for k in range(2)]
+            weave(*(add_transposed(two[k], gate_all[:, parts[k]], plain_all[:, parts[k]], 2) for k in range(2)))
+            for k in range(2):
+                nc.scalar.copy(h_of[1][:, parts[k]], two[k][:, 0 : HALF // 2])
+            weigh(1, cols)
         round_wb(3, staged[2][:].bitcast(BF16), nc.scalar.copy)
-        for h in range(2):
-            respond(2, h)
-        for h in range(2):
-            total(2, h)
-        turn_stiff(0)
+        respond(2)
+        total(2, 0)
         quarter = HALF // 2
+
+        def piece(tile, k):
+            return tile[:, k * quarter : (k + 1) * quarter]
 
         for s in range(SLICES):
             if s > 0:
@@ -347,95 +369,100 @@ def tile_list_bone_face_features_kernel(
             if s - 1 in DEFERRED:
                 h = DEFERRED[s - 1]
                 fetch_inner(s - 1, h * HALF, (h + 1) * HALF, early(s - 1, h)[0])
-            if s in (3, 4):
-                g = s - 3
-                wd_w.append(one("wd_w%d" % g, [P, N], U32, "behind%d" % s))
-                nc.vector.quantize_mx(out=wd_w[g][:].bitcast(FP8X4), scales=wd_s[:, g * N : (g + 1) * N],
-                                      in_=w_bf[:, 4 * g * N : 4 * (g + 1) * N])
+            if s == 6:
+                wd_w.append(one("wd_w", [P, 2 * N], U32, "behind6"))
+                nc.vector.quantize_mx(out=wd_w[0][:].bitcast(FP8X4), scales=wd_s[:], in_=w_bf[:])
             halves = range(2) if s < PER_PASS else range(1)
             for h in halves:
                 fetch_outer(s, h, early(s, h)[1])
-            if s in (2, 3):
-                fetch_inner(s, 0, F, (inner_all, staged[0])[s % 2][:])
-            elif DEFERRED.get(s) != 0:
+            if DEFERRED.get(s) != 0:
                 fetch_inner(s, 0, HALF, early(s, 0)[0])
             if s == 0:
                 quantise_wb(3, staged[2][:].bitcast(BF16))
             if s == 6:
-                z_w.setdefault(0, one("z_w0", [P, F], U32, "behind7"))
                 quantise_z(0, 0, F)
+                weave(*(quarter_products(pair, 1, bank_d[pair], 0, True) for pair in range(2)))
                 for pair in range(2):
-                    quarter_products(pair, 1, bank_d[pair], 0, True)
-                    nc.scalar.copy(resp[pair][:], bank_d[pair][:])
-            for h in range(2):
-                if s + 2 < SLICES:
-                    weigh(s + 2, h)
-            for h in range(2):
-                if s + 3 < SLICES:
-                    respond(s + 3, h)
-            ready = [(s - 1, DEFERRED[s - 1])] if s - 1 in DEFERRED else []
-            ready = ready + [(s, h) for h in halves if DEFERRED.get(s) != h]
-            for k, (r, h) in enumerate(ready):
-                x1, x2 = early(r, h)
-                if r < SLICES - 1:
-                    bank = (bank_b1, bank_b0, bank_a)[k] if s < SLICES - 2 else bank_a
-                    spare = z_words[:, 3 * HALF : 4 * HALF] if r == 5 else jump[k][:]
-                    combine(r, h * HALF, (h + 1) * HALF, x2, x1, bank, spare)
-                else:
+                    nc.scalar.copy(resp[pair], bank_d[pair][:])
+            if s + 2 < SLICES:
+                weigh(s + 2)
+            for r in {5: (6, 7), 6: (), 7: ()}.get(s, (s + 1,)):
+                load_stiff(r)
+            if s + 3 < SLICES:
+                respond(s + 3)
+            if s < SLICES - 2:
+                ready = [(s - 1, DEFERRED[s - 1])] if s - 1 in DEFERRED else []
+                ready = ready + [(s, h) for h in halves if DEFERRED.get(s) != h]
+                sum_banks = (bank_b0, bank_b1) if s + 3 < SLICES else (bank_a, bank_o0)
+                runs = [add_transposed(sum_banks[k], *reversed(early(r, h)), BLOCKS) for k, (r, h) in enumerate(ready)]
+                late_stiff = []
+                if s == PER_PASS + 1:
+                    late_stiff = [(6, 0, bank_b0), (6, 1, bank_b1), (7, 0, bank_c), (7, 1, bank_o1)]
+                weave(*runs, *(stiff_turns(*item) for item in late_stiff))
+                for k, (r, h) in enumerate(ready):
+                    combine(r, h * HALF, (h + 1) * HALF, sum_banks[k], jump[k][:])
+                for item in late_stiff:
+                    keep_stiff(*item)
+            else:
+                x1, x2 = early(s, 0)
+                two = bank_d if s == SLICES - 1 else (bank_a, bank_o0)
+                weave(*(add_transposed(two[k], piece(x2, k), piece(x1, k), 2) for k in range(2)))
+                for k in range(2):
+                    combine(s, k * quarter, (k + 1) * quarter, two[k], piece(jump[0], k))
+            if s == PER_PASS:
+                for h, back_banks in enumerate(((bank_c, bank_o1), bank_d)):
+                    weave(*(back_turns(h, pair, back_banks[pair]) for pair in range(2)))
                     for pair in range(2):
-                        cols = slice(pair * quarter, (pair + 1) * quarter)
-                        combine(s, cols.start, cols.stop, x2[:, cols], x1[:, cols], bank_d[pair], jump[k][:, cols])
-            for h in range(2):
-                if s + 3 < SLICES:
-                    total(s + 3, h)
-            if s + 1 < SLICES:
-                turn_stiff(s + 1)
+                        keep_back(h, pair, back_banks[pair], nc.scalar.copy)
+            if s + 3 < SLICES:
+                total(s + 3, s + 1)
             if s in (0, 1):
                 load_wd(s)
             if s == 2:
                 page_of.append(one("last_page", [P, T2], F32, "last_page"))
                 nc.gpsimd.memset(page_of[-1][:], 0.0)
-            if s == PER_PASS - 1:
-                for h, pair in ((0, 0), (0, 1), (1, 0), (1, 1)):
-                    turn_back(h, pair, bank_o[pair], nc.scalar.copy)
-
-        def piece(tile, k):
-            return tile[:, k * quarter : (k + 1) * quarter]
 
         third, fourth = (HALF, HALF + quarter), (HALF + quarter, F)
         wide = (bank_a, bank_b0, bank_b1, bank_c)
         x2 = {4: put[1][:, 0:HALF], 5: outer[1], 6: z_words[:, 0:HALF], 7: outer[1]}
         x1 = {4: put[1][:, HALF:S], 5: inner[1], 6: z_words[:, HALF:F]}
         x1_last = (piece(x2[6], 0), piece(x1[6], 0))
+        half_products(0, wide)
         for pair in range(2):
-            turn_back(0, pair, bank_o[pair], nc.scalar.copy)
+            weave(back_turns(0, pair, bank_o[pair]))
+            keep_back(0, pair, bank_o[pair], nc.scalar.copy)
         for s in (4, 5):
             fetch(s, 1, x1[s], x2[s])
-            combine(s, HALF, F, x1[s], x2[s], bank_o[s % 2], jump[2 * (s % 2)][:])
+            two = (bank_d, bank_o)[s % 2]
+            weave(*(add_transposed(two[k], piece(x2[s], k), piece(x1[s], k), 2) for k in range(2)))
+            for k, cols in enumerate((third, fourth)):
+                combine(s, *cols, two[k], piece(jump[1 + s % 2], k))
         quantise_z(1, 0, HALF)
-        for nb in range(N // P):
-            half_products(nb, wide[nb])
+        half_products(1, wide)
         fetch(6, 1, x1[6], x2[6])
         fetch_outer(7, 1, x2[7])
+        weave(*(add_transposed(bank_d[k], piece(x2[6], k), piece(x1[6], k), 2) for k in range(2)))
         for k, cols in enumerate((third, fourth)):
-            combine(6, *cols, piece(x2[6], k), piece(x1[6], k), bank_d[k], piece(gate[0], k), True)
+            combine(6, *cols, bank_d[k], piece(gate[0], k))
         for k, cols in enumerate((third, fourth)):
             fetch_inner(7, *cols, x1_last[k])
         for nb in range(2):
             half_store(nb, wide[nb])
-        quarter_products(1, 0, bank_a, 0)
+        weave(quarter_products(1, 0, bank_a, 0))
         for k, cols in enumerate((third, fourth)):
-            combine(7, *cols, piece(x2[7], k), x1_last[k], bank_o[k], None, True)
-        turn_back(1, 0, bank_d0, nc.scalar.copy)
-        turn_back(1, 1, bank_d1, nc.scalar.copy)
+            weave(add_transposed(bank_o[k], piece(x2[7], k), x1_last[k], 2))
+            combine(7, *cols, bank_o[k], None)
+        for pair in range(2):
+            weave(back_turns(1, pair, bank_d[pair]))
+            keep_back(1, pair, bank_d[pair], nc.scalar.copy)
         for nb in range(2, 4):
             half_store(nb, wide[nb])
-        quarter_products(0, 0, bank_d0, 0)
+        weave(quarter_products(0, 0, bank_d0, 0))
         quantise_z(1, *third)
         quantise_z(1, *fourth)
-        for pair, pair_banks in enumerate(((bank_d0, bank_o0), (bank_a, bank_b0))):
+        last_banks = ((bank_d0, bank_o0), (bank_a, bank_b0))
+        for pair in range(2):
+            weave(*(quarter_products(pair, b, last_banks[pair][b], 1, b == 1) for b in range(2)))
+        for pair in range(2):
             for b in range(2):
-                quarter_products(pair, b, pair_banks[b], 1, b == 1)
-        for pair, pair_banks in enumerate(((bank_d0, bank_o0), (bank_a, bank_b0))):
-            for b in range(2):
-                quarter_store(pair, b, pair_banks[b])
+                quarter_store(pair, b, last_banks[pair][b])

@@ -24,7 +24,7 @@ BLOCKS = HALF // P
 SLICES = H // P
 PER_PASS = 4
 QUANTISE_BEHIND = (6,)
-DEFERRED = {0: 1, 1: 1, 2: 1, 3: 1, 4: 0}
+DEFERRED = {0: 1, 1: 1, 2: 1, 4: 0}
 WB_CHUNKS = ((0, 128), (128, 256), (256, 512), (512, 1024))
 
 
@@ -76,10 +76,10 @@ def tile_list_bone_face_features_kernel(
         wgs_sb = one("wgs_sb", [P, S], F32)
         pages = tiles("page", 3, [P, T2], F32)
         page_of = [pages[i] for i in (0, 1, 0, 1, 0, 1, 2)]
-        gate_all = one("gate", [P, S], F32)
+        gate_all = tiles("gate", 2, [P, S], F32)
         resp_all = one("resp", [P, S], F32)
-        plain_all = one("plain", [P, S], F32)
-        gate, resp, plain = ((t[:, 0:HALF], t[:, HALF:S]) for t in (gate_all, resp_all, plain_all))
+        plain_all = tiles("plain", 2, [P, S], F32)
+        gate, resp = ((t[:, 0:HALF], t[:, HALF:S]) for t in (gate_all[0], resp_all))
         put = tiles("put", 2, [P, S], F32)
         first_put = (put[0][:, 0:HALF], put[0][:, HALF:S])
         put_of = [put[s % 2][:] for s in range(SLICES)]
@@ -88,8 +88,8 @@ def tile_list_bone_face_features_kernel(
         inner = (inner_all[:, 0:HALF], inner_all[:, HALF:F])
         outer = (outer_all[:, 0:HALF], outer_all[:, HALF:F])
         jump = tiles("jump", 3, [P, HALF], F32)
-        stiff_sb = tiles("stiff_sb", 2, [P, F], F32)
-        stiff_t = tiles("stiff_t", SLICES, [P, F], F32)
+        stiff_sb = tiles("stiff_sb", 4, [P, F], F32)
+        stiff_t = tiles("stiff_t", 6, [P, F], F32)
         z_t = tiles("z_t", 2, [P, BLOCKS * HALF], BF16)
         z_words = one("z_words", [P, 2 * F], F32)
         z_w = tiles("z_w", 2, [P, F], U32)
@@ -168,7 +168,7 @@ def tile_list_bone_face_features_kernel(
             return slice(i * P, (i + 1) * P)
 
         def weave(*runs):
-            for k in range(max(len(run) for run in runs)):
+            for k in range(max([0] + [len(run) for run in runs])):
                 for run in runs:
                     if k < len(run):
                         run[k]()
@@ -219,38 +219,38 @@ def tile_list_bone_face_features_kernel(
                                                 lhsT_scale=v_s[h][:, block(i)], rhs=codes, rhs_scale=scales,
                                                 start=True, stop=True)
                 for h in part:
-                    nc.scalar.activation(gate[h], sets[h][0][:], SIGMOID)
+                    nc.scalar.activation(gate_all[s % 2][:, h * HALF : (h + 1) * HALF], sets[h][0][:], SIGMOID)
                     nc.scalar.copy(resp[h], sets[h][1][:])
                 for h in part:
-                    nc.scalar.copy(plain[h], sets[h][2][:])
+                    nc.scalar.copy(plain_all[s % 2][:, h * HALF : (h + 1) * HALF], sets[h][2][:])
                 for cols in [slice(h * HALF, (h + 1) * HALF) for h in part] if s < 3 else [slice(0, S)]:
-                    nc.gpsimd.tensor_tensor(gate_all[:, cols], resp_all[:, cols], gate_all[:, cols], MULT)
+                    nc.gpsimd.tensor_tensor(gate_all[s % 2][:, cols], resp_all[:, cols], gate_all[s % 2][:, cols], MULT)
 
         def total(s, turned):
             quarters = [slice(k * HALF // 2, (k + 1) * HALF // 2) for k in (0, 2, 1, 3)]
             four = (bank_a, bank_o0, bank_c, bank_o1)
-            runs = [add_transposed(bank, gate_all[:, cols], plain_all[:, cols], 2) for bank, cols in zip(four, quarters)]
+            runs = [add_transposed(bank, gate_all[s % 2][:, cols], plain_all[s % 2][:, cols], 2) for bank, cols in zip(four, quarters)]
             weave(*(run[:2] for run in runs))
-            turns = [stiff_turns(turned, h, (bank_b0, bank_b1)[h]) for h in range(2)]
+            turns = [stiff_turns(*item) for item in turned]
             weave(*(run[2:3] for run in runs), *(run[:2] for run in turns))
             weave(*(run[3:] for run in runs), *(run[2:] for run in turns))
             for bank, cols in zip(four, quarters):
                 nc.scalar.copy(h_of[s][:, cols], bank[:, 0 : HALF // 2])
-            for h in range(2):
-                keep_stiff(turned, h, (bank_b0, bank_b1)[h])
+            for item in turned:
+                keep_stiff(*item)
 
         def weigh(s, cols=slice(0, S)):
             nc.gpsimd.tensor_tensor(put_of[s][:, cols], h_of[s][:, cols], wgs_sb[:, cols], MULT)
 
         def load_stiff(s):
-            nc.sync.dma_start(out=stiff_sb[s % 2][:], in_=stiff[block(s), :])
+            nc.sync.dma_start(out=stiff_sb[s % 4][:], in_=stiff[block(s), :])
 
         def stiff_turns(s, h, bank):
-            return [turning(bank[:, block(i)], stiff_sb[s % 2][:, block(BLOCKS * h + i)], True, True)
+            return [turning(bank[:, block(i)], stiff_sb[s % 4][:, block(BLOCKS * h + i)], True, True)
                     for i in range(BLOCKS)]
 
         def keep_stiff(s, h, bank):
-            nc.scalar.copy(out=stiff_t[s][:, h * HALF : (h + 1) * HALF].rearrange("p (b u q e) -> p b u q e", u=2, q=32, e=2),
+            nc.scalar.copy(out=stiff_t[s % 6][:, h * HALF : (h + 1) * HALF].rearrange("p (b u q e) -> p b u q e", u=2, q=32, e=2),
                            in_=bank[:].rearrange("p (b q u e) -> p b u q e", u=2, q=32, e=2))
 
         def fetch_outer(s, h, x2):
@@ -268,7 +268,7 @@ def tile_list_bone_face_features_kernel(
             h, b0 = divmod(m0 // P, BLOCKS)
             place = slice(64 * (s % PER_PASS), 64 * (s % PER_PASS + 1))
             dst = z_t[h][:].rearrange("p (b u r) -> p b u r", b=BLOCKS, u=2)[:, b0 : b0 + count, :, place]
-            factor = stiff_t[s][:, m0:m1]
+            factor = stiff_t[s % 6][:, m0:m1]
             if spare is None:
                 for b in range(count):
                     nc.vector.tensor_tensor(dst[:, b, :, :].rearrange("p u (q e) -> p u q e", e=2),
@@ -332,12 +332,12 @@ def tile_list_bone_face_features_kernel(
 
         def early(s, h):
             if DEFERRED.get(s) == h:
-                kept = (staged[0][:, HALF:F], staged[3][:, 0:HALF], staged[1][:, HALF:F], staged[3][:, HALF:F],
-                        staged[2][:, HALF:F])
+                kept = (outer[1], staged[3][:, 0:HALF], inner[1], None, staged[2][:, HALF:F])
                 return h_of[s + 1][:, HALF:S], kept[s]
             if s >= PER_PASS:
                 return inner[s % 2], outer[s % 2]
-            return (inner[0], outer[0]) if s % 2 == 0 else (staged[0][:, 0:HALF], staged[1][:, 0:HALF])
+            cols = slice(h * HALF, (h + 1) * HALF)
+            return (inner[0], outer[0]) if s % 2 == 0 else (staged[0][:, cols], staged[1][:, cols])
 
         respond_first(0)
         respond_first(1)
@@ -351,13 +351,14 @@ def tile_list_bone_face_features_kernel(
             cols = slice(h * HALF, (h + 1) * HALF)
             two = ((bank_a, bank_c), (bank_b0, bank_b1))[h]
             parts = [slice(cols.start + k * HALF // 2, cols.start + (k + 1) * HALF // 2) for k in range(2)]
-            weave(*(add_transposed(two[k], gate_all[:, parts[k]], plain_all[:, parts[k]], 2) for k in range(2)))
+            weave(*(add_transposed(two[k], gate_all[1][:, parts[k]], plain_all[1][:, parts[k]], 2) for k in range(2)))
             for k in range(2):
                 nc.scalar.copy(h_of[1][:, parts[k]], two[k][:, 0 : HALF // 2])
             weigh(1, cols)
         round_wb(3, staged[2][:].bitcast(BF16), nc.scalar.copy)
         respond(2)
-        total(2, 0)
+        respond(3)
+        total(2, [(0, 0, bank_b0), (0, 1, bank_b1)])
         quarter = HALF // 2
 
         def piece(tile, k):
@@ -375,7 +376,9 @@ def tile_list_bone_face_features_kernel(
             halves = range(2) if s < PER_PASS else range(1)
             for h in halves:
                 fetch_outer(s, h, early(s, h)[1])
-            if DEFERRED.get(s) != 0:
+            if s == PER_PASS - 1:
+                fetch_inner(s, 0, F, staged[0][:])
+            elif DEFERRED.get(s) != 0:
                 fetch_inner(s, 0, HALF, early(s, 0)[0])
             if s == 0:
                 quantise_wb(3, staged[2][:].bitcast(BF16))
@@ -386,23 +389,30 @@ def tile_list_bone_face_features_kernel(
                     nc.scalar.copy(resp[pair], bank_d[pair][:])
             if s + 2 < SLICES:
                 weigh(s + 2)
-            for r in {5: (6, 7), 6: (), 7: ()}.get(s, (s + 1,)):
+            for r in {4: (5, 6, 7), 5: (), 6: (), 7: ()}.get(s, (s + 1,)):
                 load_stiff(r)
-            if s + 3 < SLICES:
-                respond(s + 3)
+            if s + 4 < SLICES:
+                respond(s + 4)
             if s < SLICES - 2:
                 ready = [(s - 1, DEFERRED[s - 1])] if s - 1 in DEFERRED else []
                 ready = ready + [(s, h) for h in halves if DEFERRED.get(s) != h]
-                sum_banks = (bank_b0, bank_b1) if s + 3 < SLICES else (bank_a, bank_o0)
+                sum_banks = (bank_b0, bank_b1, bank_a) if s + 3 < SLICES else (bank_a, bank_o0)
                 runs = [add_transposed(sum_banks[k], *reversed(early(r, h)), BLOCKS) for k, (r, h) in enumerate(ready)]
                 late_stiff = []
                 if s == PER_PASS + 1:
-                    late_stiff = [(6, 0, bank_b0), (6, 1, bank_b1), (7, 0, bank_c), (7, 1, bank_o1)]
+                    late_stiff = [(5, 0, bank_b0), (6, 0, bank_b1), (7, 0, bank_c), (4, 1, bank_o1)]
                 weave(*runs, *(stiff_turns(*item) for item in late_stiff))
+                for item in late_stiff[:1]:
+                    keep_stiff(*item)
                 for k, (r, h) in enumerate(ready):
                     combine(r, h * HALF, (h + 1) * HALF, sum_banks[k], jump[k][:])
-                for item in late_stiff:
+                for item in late_stiff[1:]:
                     keep_stiff(*item)
+                if s == PER_PASS + 1:
+                    last_stiff = [(5, 1, bank_b0), (6, 1, bank_b1), (7, 1, bank_c)]
+                    weave(*(stiff_turns(*item) for item in last_stiff))
+                    for item in last_stiff:
+                        keep_stiff(*item)
             else:
                 x1, x2 = early(s, 0)
                 two = bank_d if s == SLICES - 1 else (bank_a, bank_o0)
@@ -410,12 +420,12 @@ def tile_list_bone_face_features_kernel(
                 for k in range(2):
                     combine(s, k * quarter, (k + 1) * quarter, two[k], piece(jump[0], k))
             if s == PER_PASS:
-                for h, back_banks in enumerate(((bank_c, bank_o1), bank_d)):
+                for h, back_banks in enumerate(((bank_b0, bank_b1), bank_d)):
                     weave(*(back_turns(h, pair, back_banks[pair]) for pair in range(2)))
                     for pair in range(2):
                         keep_back(h, pair, back_banks[pair], nc.scalar.copy)
             if s + 3 < SLICES:
-                total(s + 3, s + 1)
+                total(s + 3, [(s + 1, 0, bank_b0), (s + 1, 1, bank_b1)][: max(0, min(2, PER_PASS - s))])
             if s in (0, 1):
                 load_wd(s)
             if s == 2:
@@ -433,10 +443,8 @@ def tile_list_bone_face_features_kernel(
             keep_back(0, pair, bank_o[pair], nc.scalar.copy)
         for s in (4, 5):
             fetch(s, 1, x1[s], x2[s])
-            two = (bank_d, bank_o)[s % 2]
-            weave(*(add_transposed(two[k], piece(x2[s], k), piece(x1[s], k), 2) for k in range(2)))
-            for k, cols in enumerate((third, fourth)):
-                combine(s, *cols, two[k], piece(jump[1 + s % 2], k))
+            weave(add_transposed(bank_o[s % 2], x1[s], x2[s], BLOCKS))
+            combine(s, HALF, F, bank_o[s % 2], jump[2 * (s % 2)][:])
         quantise_z(1, 0, HALF)
         half_products(1, wide)
         fetch(6, 1, x1[6], x2[6])

@@ -92,8 +92,9 @@ def tile_list_bone_face_features_kernel(
         stiff_t = tiles("stiff_t", 6, [P, F], F32)
         z_t = tiles("z_t", 2, [P, BLOCKS * HALF], BF16)
         z_words = one("z_words", [P, 2 * F], F32)
-        z_w = tiles("z_w", 2, [P, F], U32)
+        z_w = {1: one("z_w1", [P, F], U32)}
         z_s = tiles("z_s", 2, [P, F], U8)
+        put_of[6] = one("put_6", [P, S], F32, "behind6b")[:]
         h_ring = tiles("h_ring", 3, [P, S], F32)
         h_of = {s: h_ring[s % 3] for s in range(1, SLICES)}
         for s in QUANTISE_BEHIND:
@@ -334,6 +335,8 @@ def tile_list_bone_face_features_kernel(
             if DEFERRED.get(s) == h:
                 kept = (outer[1], staged[3][:, 0:HALF], inner[1], None, staged[2][:, HALF:F])
                 return h_of[s + 1][:, HALF:S], kept[s]
+            if s == SLICES - 1:
+                return plain_all[0][:, 0:HALF], plain_all[0][:, HALF:S]
             if s >= PER_PASS:
                 return inner[s % 2], outer[s % 2]
             cols = slice(h * HALF, (h + 1) * HALF)
@@ -383,6 +386,7 @@ def tile_list_bone_face_features_kernel(
             if s == 0:
                 quantise_wb(3, staged[2][:].bitcast(BF16))
             if s == 6:
+                z_w.setdefault(0, one("z_w0", [P, F], U32, "behind6b"))
                 quantise_z(0, 0, F)
                 weave(*(quarter_products(pair, 1, bank_d[pair], 0, True) for pair in range(2)))
                 for pair in range(2):
@@ -397,6 +401,9 @@ def tile_list_bone_face_features_kernel(
                 ready = [(s - 1, DEFERRED[s - 1])] if s - 1 in DEFERRED else []
                 ready = ready + [(s, h) for h in halves if DEFERRED.get(s) != h]
                 sum_banks = (bank_b0, bank_b1, bank_a) if s + 3 < SLICES else (bank_a, bank_o0)
+                if s == PER_PASS - 1:
+                    total(s + 3, [(s + 1, 0, bank_b0)])
+                    sum_banks = (bank_b1, bank_a, bank_o0)
                 runs = [add_transposed(sum_banks[k], *reversed(early(r, h)), BLOCKS) for k, (r, h) in enumerate(ready)]
                 late_stiff = []
                 if s == PER_PASS + 1:
@@ -415,17 +422,19 @@ def tile_list_bone_face_features_kernel(
                         keep_stiff(*item)
             else:
                 x1, x2 = early(s, 0)
-                two = bank_d if s == SLICES - 1 else (bank_a, bank_o0)
-                weave(*(add_transposed(two[k], piece(x2, k), piece(x1, k), 2) for k in range(2)))
+                two = bank_d if s == SLICES - 1 else bank_o
                 for k in range(2):
+                    weave(add_transposed(two[k], piece(x2, k), piece(x1, k), 2))
                     combine(s, k * quarter, (k + 1) * quarter, two[k], piece(jump[0], k))
             if s == PER_PASS:
                 for h, back_banks in enumerate(((bank_b0, bank_b1), bank_d)):
                     weave(*(back_turns(h, pair, back_banks[pair]) for pair in range(2)))
                     for pair in range(2):
                         keep_back(h, pair, back_banks[pair], nc.scalar.copy)
-            if s + 3 < SLICES:
-                total(s + 3, [(s + 1, 0, bank_b0), (s + 1, 1, bank_b1)][: max(0, min(2, PER_PASS - s))])
+            if s < PER_PASS - 1:
+                total(s + 3, [(s + 1, 0, bank_b0), (s + 1, 1, bank_b1)])
+            if s == PER_PASS:
+                total(s + 3, [])
             if s in (0, 1):
                 load_wd(s)
             if s == 2:
@@ -434,8 +443,9 @@ def tile_list_bone_face_features_kernel(
 
         third, fourth = (HALF, HALF + quarter), (HALF + quarter, F)
         wide = (bank_a, bank_b0, bank_b1, bank_c)
-        x2 = {4: put[1][:, 0:HALF], 5: outer[1], 6: z_words[:, 0:HALF], 7: outer[1]}
-        x1 = {4: put[1][:, HALF:S], 5: inner[1], 6: z_words[:, HALF:F]}
+        x1_first, x2_first = early(SLICES - 1, 0)
+        x2 = {4: put[1][:, 0:HALF], 5: x2_first, 6: z_words[:, 0:HALF], 7: x2_first}
+        x1 = {4: put[1][:, HALF:S], 5: x1_first, 6: z_words[:, HALF:F]}
         x1_last = (piece(x2[6], 0), piece(x1[6], 0))
         half_products(0, wide)
         for pair in range(2):
@@ -449,8 +459,8 @@ def tile_list_bone_face_features_kernel(
         half_products(1, wide)
         fetch(6, 1, x1[6], x2[6])
         fetch_outer(7, 1, x2[7])
-        weave(*(add_transposed(bank_d[k], piece(x2[6], k), piece(x1[6], k), 2) for k in range(2)))
         for k, cols in enumerate((third, fourth)):
+            weave(add_transposed(bank_d[k], piece(x2[6], k), piece(x1[6], k), 2))
             combine(6, *cols, bank_d[k], piece(gate[0], k))
         for k, cols in enumerate((third, fourth)):
             fetch_inner(7, *cols, x1_last[k])
@@ -470,7 +480,8 @@ def tile_list_bone_face_features_kernel(
         quantise_z(1, *fourth)
         last_banks = ((bank_d0, bank_o0), (bank_a, bank_b0))
         for pair in range(2):
-            weave(*(quarter_products(pair, b, last_banks[pair][b], 1, b == 1) for b in range(2)))
+            for b in range(2):
+                weave(quarter_products(pair, b, last_banks[pair][b], 1, b == 1))
         for pair in range(2):
             for b in range(2):
                 quarter_store(pair, b, last_banks[pair][b])

@@ -20,12 +20,11 @@ SIGMOID = mybir.ActivationFunctionType.Sigmoid
 
 P = 128
 HALF = 512
+QUARTER = 256
 BLOCKS = HALF // P
 SLICES = H // P
 PER_PASS = 4
-QUANTISE_BEHIND = (6,)
-DEFERRED = {0: 1, 1: 1, 2: 1, 4: 0}
-WB_CHUNKS = ((0, 128), (128, 256), (256, 512), (512, 1024))
+WB_CHUNKS = ((0, 128), (128, 384), (384, 512), (512, 1024))
 
 
 def tile_list_bone_face_features_kernel(
@@ -38,27 +37,32 @@ def tile_list_bone_face_features_kernel(
         sb = ctx.enter_context(tc.tile_pool(name="sb", bufs=1))
         ps = ctx.enter_context(tc.psum_pool(name="ps", bufs=1))
 
-        def tiles(name, count, shape, dtype):
-            return [sb.tile(shape, dtype, name="%s%d" % (name, i), align_bytes=64) for i in range(count)]
-
         def one(name, shape, dtype, tag=""):
             return sb.tile(shape, dtype, name=name, align_bytes=64, tag=tag)
+
+        def tiles(name, count, shape, dtype):
+            return [one("%s%d" % (name, i), shape, dtype) for i in range(count)]
+
+        def block(i):
+            return slice(i * P, (i + 1) * P)
+
+        def half(h):
+            return slice(h * HALF, (h + 1) * HALF)
 
         idx1 = lists.tile([P, S // 16], U16, name="idx1")
         idx2 = lists.tile([P, S // 16], U16, name="idx2")
         idx3 = lists.tile([P, F // 16], U16, name="idx3")
         idx4 = lists.tile([P, F // 16], U16, name="idx4")
 
-        def half_of(idx, h):
-            return idx[:, h * (HALF // 16) : (h + 1) * (HALF // 16)]
+        def entries(idx, cols):
+            return idx[:, cols.start // 16 : cols.stop // 16]
 
         banks = [ps.tile([P, HALF], F32, name="bank%d" % i) for i in range(8)]
-        bank_a, bank_b0, bank_b1, bank_c, bank_d0, bank_d1, bank_o0, bank_o1 = banks
-        bank_d = (bank_d0, bank_d1)
-        bank_o = (bank_o0, bank_o1)
+        bank_a, bank_b, bank_c, bank_s = banks[0:2], banks[2:4], banks[4:6], banks[6:8]
 
         ident = one("ident", [P, P], F32)
-        tab_w = one("tab_w", [P, T], U32)
+        ident_bf = one("ident_bf", [P, P], BF16)
+        tab_w = one("tab_w", [P, T], U32, "table")
         tab_s = one("tab_s", [P, T], U8)
         v_w = tiles("v_w", 2, [P, HALF], U32)
         v_s = tiles("v_s", 2, [P, HALF], U8)
@@ -66,41 +70,47 @@ def tile_list_bone_face_features_kernel(
         wc_w = one("wc_w", [P, H], U32)
         wa_s = one("wa_s", [P, H], U8)
         wc_s = one("wc_s", [P, H], U8)
-        wb_raw = [one("wb_raw%d" % i, [P, 4, c1 - c0], F32, "last_page" if c1 == H else "")
-                  for i, (c0, c1) in enumerate(WB_CHUNKS)]
+        first_outer = one("first_outer", [P, F], F32)
+        wb_flat = [one("wb_raw%d" % i, [P, 4 * (c1 - c0)], F32)[:] for i, (c0, c1) in enumerate(WB_CHUNKS)]
+        wb_raw = [flat.rearrange("p (j c) -> p j c", j=4) for flat in wb_flat]
         w_bf = one("w_bf", [P, 4 * H], BF16)
-        wb_w = tiles("wb_w", 2, [P, HALF], U32)
+        wb_w = {i: one("wb_w%d" % i, [P, c1 - c0], U32) for i, (c0, c1) in enumerate(WB_CHUNKS) if i < 2}
         wb_s = one("wb_s", [P, H], U8)
-        wd_w = []
+        wd_w = one("wd_w", [P, 2 * N], U32)
         wd_s = one("wd_s", [P, 2 * N], U8)
         wgs_sb = one("wgs_sb", [P, S], F32)
-        pages = tiles("page", 3, [P, T2], F32)
-        page_of = [pages[i] for i in (0, 1, 0, 1, 0, 1, 2)]
-        gate_all = tiles("gate", 2, [P, S], F32)
-        resp_all = one("resp", [P, S], F32)
-        plain_all = tiles("plain", 2, [P, S], F32)
-        gate, resp = ((t[:, 0:HALF], t[:, HALF:S]) for t in (gate_all[0], resp_all))
+        wgs_dealt = [one("wgs_dealt%d" % t, [P, S], F32, "behind%d" % (t + PER_PASS) if t < 2 else "") for t in range(PER_PASS)]
+        pages = tiles("page", 2, [P, T2], F32)
+        work = tiles("work", 2, [P, 2 * S], F32)
+        gate = one("gate", [P, S], F32)
+        resp = tiles("resp", 2, [P, S], F32)
+        plain = one("plain", [P, S], F32)
         put = tiles("put", 2, [P, S], F32)
-        first_put = (put[0][:, 0:HALF], put[0][:, HALF:S])
-        put_of = [put[s % 2][:] for s in range(SLICES)]
-        inner_all = one("inner", [P, F], F32)
-        outer_all = one("outer", [P, F], F32)
-        inner = (inner_all[:, 0:HALF], inner_all[:, HALF:F])
-        outer = (outer_all[:, 0:HALF], outer_all[:, HALF:F])
-        jump = tiles("jump", 3, [P, HALF], F32)
-        stiff_sb = tiles("stiff_sb", 4, [P, F], F32)
-        stiff_t = tiles("stiff_t", 6, [P, F], F32)
+        gate_of = {n: gate[:] for n in range(3, SLICES)}
+        gate_of.update({1: w_bf[:, 2 * S : 4 * S].bitcast(F32), 2: one("second_gate", [P, S], F32, "behind2")[:]})
+        stiff_sb = tiles("stiff_sb", SLICES - 2, [P, F], F32)
         z_t = tiles("z_t", 2, [P, BLOCKS * HALF], BF16)
+        z_pair = resp[(SLICES - 1) % 2][:].bitcast(BF16)
+        z_last = one("z_last", [P, 4 * F], BF16)
+        stiff6 = one("stiff6", [P, F], F32, "behind6")[:, half(0)]
+        late = one("late", [P, 3 * HALF], F32)
         z_words = one("z_words", [P, 2 * F], F32)
         z_w = {1: one("z_w1", [P, F], U32)}
         z_s = tiles("z_s", 2, [P, F], U8)
-        put_of[6] = one("put_6", [P, S], F32, "behind6b")[:]
-        h_ring = tiles("h_ring", 3, [P, S], F32)
-        h_of = {s: h_ring[s % 3] for s in range(1, SLICES)}
-        for s in QUANTISE_BEHIND:
-            h_of[s] = one("h_%d" % s, [P, S], F32, "behind%d" % s)
-        h_of[SLICES - 1] = z_t[1][:].bitcast(F32)
-        staged = tiles("staged", 4, [P, F], F32)
+
+        outer = [first_outer[:]] + [work[(s + 1) % 2][:, S : 2 * S] for s in range(1, SLICES)]
+        gated = {n: outer[n - 3] if n >= 3 else work[n % 2][:, S : 2 * S] for n in range(1, SLICES)}
+        put_of = [put[s % 2][:] for s in range(SLICES)]
+        put_of[2] = wb_flat[3][:, 0:S]
+        gated[2] = work[1][:, 0:S]
+        jump = [work[s % 2][:, 0:S] for s in range(SLICES)]
+        summed = {n: work[n % 2][:].rearrange("p (k h c) -> p h k c", k=2, h=2)[:, :, :, 0:QUARTER] for n in range(1, SLICES)}
+        first_summed = [t.rearrange("p (k c) -> p k c", k=2) for t in (work[0][:, half(0)], gated[2][:, QUARTER : QUARTER + HALF])]
+        z_rows = [resp[(s + 3) % 2][:, QUARTER : QUARTER + HALF].bitcast(BF16) for s in range(PER_PASS)]
+        staged = stiff_sb[0:4]
+
+        def dealt(rows, t):
+            return rows.rearrange("(g t i) c -> t g i c", t=PER_PASS, i=8)[t]
 
         nc.vector.memset(tab_s[:, 0 : T // 2].bitcast(I32), 0)
         nc.gpsimd.memset(tab_s[:, T // 2 : T].bitcast(I32), 0)
@@ -110,378 +120,300 @@ def tile_list_bone_face_features_kernel(
 
         def load_wb(i):
             c0, c1 = WB_CHUNKS[i]
-            nc.sync.dma_start(out=wb_raw[i][:], in_=wb_rows[:, :, c0:c1])
+            nc.sync.dma_start(out=wb_raw[i], in_=wb_rows[:, :, c0:c1])
+
+        def load_scales(queue, plane, rows):
+            for q in range(4):
+                queue.dma_start(out=plane[32 * q : 32 * q + 4, :].bitcast(I32), in_=rows[4 * q : 4 * q + 4, :].bitcast(I32))
+
+        def load_stiff(s):
+            rows = stiff[block(s), :] if s < PER_PASS else dealt(stiff[K:H, :], s - PER_PASS)
+            nc.sync.dma_start(out=stiff_sb[s][:], in_=rows)
 
         nc.sync.dma_start(idx1[:], offs)
         load_wb(0)
-        for q in range(4):
-            nc.sync.dma_start(out=tab_s[32 * q : 32 * q + 4, :].bitcast(I32),
-                              in_=tab_scales[0][4 * q : 4 * q + 4, :].bitcast(I32))
+        load_scales(nc.sync, tab_s, tab_scales[0])
+        nc.sync.dma_start(idx2[:], offs2)
         nc.sync.dma_start(out=tab_w[:].bitcast(I32), in_=tab_words[0].rearrange("p n t -> p (n t)").bitcast(I32))
-        for q in range(4):
-            nc.gpsimd.dma_start(out=wc_s[32 * q : 32 * q + 4, :].bitcast(I32),
-                                in_=wc_scales[0][4 * q : 4 * q + 4, :].bitcast(I32))
+        load_scales(nc.gpsimd, wc_s, wc_scales[0])
+        wa_rows = wa_words[0].bitcast(I32)
+        wc_rows = wc_words[0].rearrange("p n t -> p (n t)").bitcast(I32)
+        nc.sync.dma_start(out=wa_w[:, 0:512].bitcast(I32), in_=wa_rows[:, 0:128])
+        load_scales(nc.sync, wa_s, wa_scales[0])
+        nc.sync.dma_start(out=wc_w[:, 0:256].bitcast(I32), in_=wc_rows[:, 0:256])
+        load_wb(1)
+        nc.sync.dma_start(out=wgs_sb[:, half(0)], in_=wgs[:, half(0)])
+        nc.sync.dma_start(out=wgs_sb[:, half(1)], in_=wgs[:, half(1)])
+        load_wb(2)
+        nc.sync.dma_start(idx4[:], offs4)
+        nc.sync.dma_start(out=wa_w[:, 512 : 2 * H].bitcast(I32), in_=wa_rows[:, 128 : H // 2])
+        nc.sync.dma_start(out=wc_w[:, 256:H].bitcast(I32), in_=wc_rows[:, 256:H])
+        nc.sync.dma_start(idx3[:], offs3)
+        load_wb(3)
+        wd_raw = one("wd_raw", [P, 2, 4, N], F32, "table")
+        for s in range(SLICES - 2):
+            load_stiff(s)
+            if s < PER_PASS:
+                for a in range(4):
+                    nc.sync.dma_start(out=wgs_dealt[s][32 * a : 32 * (a + 1), :], in_=dealt(wgs, s))
+            if s == 2:
+                nc.sync.dma_start(out=wd_raw[:, 0], in_=wd[0:K, :].rearrange("(p j) c -> p j c", j=4))
+            if s == 3:
+                for t in range(PER_PASS):
+                    nc.sync.dma_start(out=wd_raw[:, 1, t], in_=dealt(wd[K:H, :], t))
+        for dst, t, h in ((stiff6, 2, 0), (late[:, HALF:S], 2, 1), (late[:, 0:HALF], 3, 0), (late[:, S : 3 * HALF], 3, 1)):
+            nc.sync.dma_start(out=dst, in_=dealt(stiff[K:H, half(h)], t))
+
+        make_identity(nc, ident[:])
+        make_identity(nc, ident_bf[:])
+        nc.vector.memset(pages[0][:], 0.0)
+        nc.gpsimd.memset(pages[1][:], 0.0)
 
         def interleave(dst, raw, copy):
             copy(out=dst.rearrange("p (c i t) -> p c t i", i=4, t=4), in_=raw.rearrange("p t (c i) -> p c t i", i=4))
 
-        def round_wb(i, rounded, copy):
+        def round_wb(i, copy):
             c0, c1 = WB_CHUNKS[i]
-            for a in range(0, c1 - c0, 256):
-                b = min(a + 256, c1 - c0)
-                interleave(rounded[:, 4 * a : 4 * b], wb_raw[i][:, :, a:b], copy)
+            for a in range(0, c1 - c0, P):
+                interleave(w_bf[:, 4 * (c0 + a) : 4 * (c0 + a + P)], wb_raw[i][:, :, a : a + P], copy)
 
-        def quantise_wb(i, rounded):
+        def round_wb_dealt():
+            src = wb_raw[3].rearrange("p j (g t h i) -> p t g h j i", t=PER_PASS, h=2, i=4)
+            for t in range(PER_PASS):
+                dst = w_bf[:, 4 * (K + t * P) : 4 * (K + (t + 1) * P)]
+                nc.scalar.copy(out=dst.rearrange("p (g h i j) -> p g h j i", h=2, i=4, j=4), in_=src[:, t])
+
+        def quantise_wb(i):
             c0, c1 = WB_CHUNKS[i]
-            nc.vector.quantize_mx(out=wb_w[c0 // HALF][:, c0 % HALF : (c1 - 1) % HALF + 1].bitcast(FP8X4), scales=wb_s[:, c0:c1], in_=rounded)
+            nc.vector.quantize_mx(out=wb_w[i][:, :].bitcast(FP8X4),
+                                  scales=wb_s[:, c0:c1], in_=w_bf[:, 4 * c0 : 4 * c1])
 
-        wa_rows = wa_words[0].bitcast(I32)
-        nc.sync.dma_start(out=wa_w[:, 0:512].bitcast(I32), in_=wa_rows[:, 0:128])
-        for q in range(4):
-            nc.sync.dma_start(out=wa_s[32 * q : 32 * q + 4, :].bitcast(I32),
-                              in_=wa_scales[0][4 * q : 4 * q + 4, :].bitcast(I32))
-        wc_rows = wc_words[0].rearrange("p n t -> p (n t)").bitcast(I32)
-        nc.sync.dma_start(out=wc_w[:, 0:256].bitcast(I32), in_=wc_rows[:, 0:256])
-        load_wb(1)
-        nc.sync.dma_start(out=wgs_sb[:, 0:HALF], in_=wgs[:, 0:HALF])
-        nc.sync.dma_start(idx2[:], offs2)
-        nc.sync.dma_start(out=wgs_sb[:, HALF:S], in_=wgs[:, HALF:S])
-        load_wb(2)
-        nc.sync.dma_start(out=wa_w[:, 512 : 2 * H].bitcast(I32), in_=wa_rows[:, 128 : H // 2])
-        nc.sync.dma_start(out=wc_w[:, 256:H].bitcast(I32), in_=wc_rows[:, 256:H])
-        nc.sync.dma_start(idx3[:], offs3)
-        nc.sync.dma_start(idx4[:], offs4)
-        load_wb(3)
-
-        make_identity(nc, ident[:])
-        for page in pages[:1]:
-            nc.vector.memset(page[:], 0.0)
-        for page in pages[1:]:
-            nc.gpsimd.memset(page[:], 0.0)
-
-        round_wb(0, w_bf[:, 0:512], nc.vector.tensor_copy)
-        quantise_wb(0, w_bf[:, 0:512])
-        for h in range(2):
-            nc.vector.tensor_copy(v_s[h][:], tab_s[:].indirect(half_of(idx1, h)))
-            nc.vector.tensor_copy(v_w[h][:], tab_w[:].indirect(half_of(idx1, h)))
-
-        def block(i):
-            return slice(i * P, (i + 1) * P)
-
-        def weave(*runs):
-            for k in range(max([0] + [len(run) for run in runs])):
-                for run in runs:
-                    if k < len(run):
-                        run[k]()
-
-        def turning(out_ap, in_ap, start, stop):
-            return lambda: nc.tensor.matmul(out_ap, in_ap, ident[:], start=start, stop=stop, is_transpose=True)
-
-        def add_transposed(bank, x, y, count):
-            return [turning(bank[:, block(i)], (x, y)[term][:, block(i)], term + i == 0, term + i == count)
-                    for term in (0, 1) for i in range(count)]
+        def deal_columns(dst, src):
+            nc.scalar.copy(out=dst.bitcast(U32).rearrange("p (t g w) -> p t g w", t=PER_PASS, g=16),
+                           in_=src.bitcast(U32).rearrange("p (g t w) -> p t g w", t=PER_PASS, g=16))
 
         def weights(s):
-            return (
-                (wb_w[s // PER_PASS][:, block(s % PER_PASS)].bitcast(FP8X4), wb_s[:, block(s)]),
-                (wa_w[:, 2 * P * s : 2 * P * (s + 1)].bitcast(FP4X4), wa_s[:, block(s)]),
-                (wc_w[:, block(s)].bitcast(FP8X4), wc_s[:, block(s)]),
-            )
+            b = block(s % PER_PASS)
+            wide = slice(2 * b.start, 2 * b.stop)
+            a_w, a_s, c_w, c_s = (wa_w, wa_s, wc_w, wc_s) if s < PER_PASS else dealt_weights
+            i = max(k for k, (c0, c1) in enumerate(WB_CHUNKS) if c0 <= s * P)
+            c0 = s * P - WB_CHUNKS[i][0]
+            return ((wb_w[i][:, c0 : c0 + P].bitcast(FP8X4), wb_s[:, block(s)]),
+                    (a_w[:, wide].bitcast(FP4X4), a_s[:, b]),
+                    (c_w[:, b].bitcast(FP8X4), c_s[:, b]))
 
-        first_banks = ((bank_b0, bank_a, bank_c), (bank_b1, bank_o0, bank_o1))
+        def turn(out_ap, in_ap, start=True, stop=True, by=ident):
+            nc.tensor.matmul(out_ap, in_ap, by[:], start=start, stop=stop, is_transpose=True)
 
-        def respond_first(h):
-            cols = slice(h * HALF, (h + 1) * HALF)
-            first_b, first_a, first_c = bank_b0, bank_a, bank_c
-            gated = outer[h]
-            for bank, (codes, scales) in zip((first_b, first_a, first_c), weights(0)):
-                nc.tensor.matmul_mx(out=bank[:], lhsT=codes, lhsT_scale=scales, rhs=v_w[h][:].bitcast(FP8X4),
-                                    rhs_scale=v_s[h][:], start=True, stop=True)
-            first_gate = (first_put[0], wb_raw[1][:].rearrange("p j c -> p (j c)"))[h]
-            nc.scalar.activation(first_gate, first_b[:], SIGMOID)
-            nc.vector.tensor_tensor(gated, first_a[:], first_gate, MULT)
-            if h == 0:
-                nc.vector.tensor_tensor(inner[0], first_c[:], gated, ADD)
-                round_wb(1, put[0][:, 0:256].bitcast(BF16), nc.scalar.copy)
-                quantise_wb(1, put[0][:, 0:256].bitcast(BF16))
-                nc.vector.tensor_tensor(put[0][:, cols], inner[0], wgs_sb[:, cols], MULT)
-            else:
-                nc.scalar.copy(jump[2][:], first_c[:])
-                nc.gpsimd.tensor_tensor(inner[0], jump[2][:], gated, ADD)
-                nc.gpsimd.tensor_tensor(first_put[1], inner[0], wgs_sb[:, cols], MULT)
+        def products(n):
+            for three, (codes, scales) in zip((bank_b, bank_a, bank_c), weights(n)):
+                for h in range(2):
+                    for i in range(BLOCKS):
+                        nc.tensor.matmul_mx(out=three[h][:, block(i)], lhsT=v_w[h][:, block(i)].bitcast(FP8X4),
+                                            lhsT_scale=v_s[h][:, block(i)], rhs=codes, rhs_scale=scales,
+                                            start=True, stop=True)
+            for h in range(2):
+                nc.scalar.activation(gate_of[n][:, half(h)], bank_b[h][:], SIGMOID)
+                nc.scalar.copy(resp[n % 2][:, half(h)], bank_a[h][:])
+            for h in range(2):
+                nc.scalar.copy(plain[:, half(h)], bank_c[h][:])
 
-        def respond(s):
-            sets = first_banks if s > 1 else first_banks[:1] * 2
-            for part in ((0, 1),) if s > 1 else ((0,), (1,)):
+        def gate_and_sum(n):
+            bank_s = bank_b if n == 2 else banks[6:8]
+            for h in range(2):
                 for i in range(BLOCKS):
-                    for h in part:
-                        for bank, (codes, scales) in zip(sets[h], weights(s)):
-                            nc.tensor.matmul_mx(out=bank[:, block(i)], lhsT=v_w[h][:, block(i)].bitcast(FP8X4),
-                                                lhsT_scale=v_s[h][:, block(i)], rhs=codes, rhs_scale=scales,
-                                                start=True, stop=True)
-                for h in part:
-                    nc.scalar.activation(gate_all[s % 2][:, h * HALF : (h + 1) * HALF], sets[h][0][:], SIGMOID)
-                    nc.scalar.copy(resp[h], sets[h][1][:])
-                for h in part:
-                    nc.scalar.copy(plain_all[s % 2][:, h * HALF : (h + 1) * HALF], sets[h][2][:])
-                for cols in [slice(h * HALF, (h + 1) * HALF) for h in part] if s < 3 else [slice(0, S)]:
-                    nc.gpsimd.tensor_tensor(gate_all[s % 2][:, cols], resp_all[:, cols], gate_all[s % 2][:, cols], MULT)
+                    turn(bank_s[h][:, block(i)], plain[:, block(BLOCKS * h + i)], i == 0, False)
+            for h in range(2):
+                nc.gpsimd.tensor_tensor(gated[n][:, half(h)], resp[n % 2][:, half(h)], gate_of[n][:, half(h)], MULT)
+                for i in range(BLOCKS):
+                    turn(bank_s[h][:, block(i)], gated[n][:, block(BLOCKS * h + i)], False, i == BLOCKS - 1)
+                nc.scalar.copy(out=first_summed[h] if n == 1 else summed[n][:, h], in_=bank_s[h][:].rearrange("p (k c) -> p k c", k=2))
 
-        def total(s, turned):
-            quarters = [slice(k * HALF // 2, (k + 1) * HALF // 2) for k in (0, 2, 1, 3)]
-            four = (bank_a, bank_o0, bank_c, bank_o1)
-            runs = [add_transposed(bank, gate_all[s % 2][:, cols], plain_all[s % 2][:, cols], 2) for bank, cols in zip(four, quarters)]
-            weave(*(run[:2] for run in runs))
-            turns = [stiff_turns(*item) for item in turned]
-            weave(*(run[2:3] for run in runs), *(run[:2] for run in turns))
-            weave(*(run[3:] for run in runs), *(run[2:] for run in turns))
-            for bank, cols in zip(four, quarters):
-                nc.scalar.copy(h_of[s][:, cols], bank[:, 0 : HALF // 2])
-            for item in turned:
-                keep_stiff(*item)
-
-        def weigh(s, cols=slice(0, S)):
-            nc.gpsimd.tensor_tensor(put_of[s][:, cols], h_of[s][:, cols], wgs_sb[:, cols], MULT)
-
-        def load_stiff(s):
-            nc.sync.dma_start(out=stiff_sb[s % 4][:], in_=stiff[block(s), :])
-
-        def stiff_turns(s, h, bank):
-            return [turning(bank[:, block(i)], stiff_sb[s % 4][:, block(BLOCKS * h + i)], True, True)
-                    for i in range(BLOCKS)]
-
-        def keep_stiff(s, h, bank):
-            nc.scalar.copy(out=stiff_t[s % 6][:, h * HALF : (h + 1) * HALF].rearrange("p (b u q e) -> p b u q e", u=2, q=32, e=2),
-                           in_=bank[:].rearrange("p (b q u e) -> p b u q e", u=2, q=32, e=2))
-
-        def fetch_outer(s, h, x2):
-            nc.vector.tensor_scalar(x2, page_of[s][:].indirect(half_of(idx4, h)), -1.0, 1.0, MULT, ADD)
-
-        def fetch_inner(s, m0, m1, x1):
-            nc.vector.tensor_copy(x1, page_of[s][:].indirect(idx3[:, m0 // 16 : m1 // 16]))
-
-        def fetch(s, h, x1, x2):
-            fetch_outer(s, h, x2)
-            fetch_inner(s, h * HALF, (h + 1) * HALF, x1)
-
-        def combine(s, m0, m1, bank, spare):
-            count = (m1 - m0) // P
-            h, b0 = divmod(m0 // P, BLOCKS)
-            place = slice(64 * (s % PER_PASS), 64 * (s % PER_PASS + 1))
-            dst = z_t[h][:].rearrange("p (b u r) -> p b u r", b=BLOCKS, u=2)[:, b0 : b0 + count, :, place]
-            factor = stiff_t[s % 6][:, m0:m1]
-            if spare is None:
-                for b in range(count):
-                    nc.vector.tensor_tensor(dst[:, b, :, :].rearrange("p u (q e) -> p u q e", e=2),
-                                            bank[:, block(b)].rearrange("p (q u e) -> p u q e", u=2, e=2),
-                                            factor[:, block(b)].rearrange("p (u q e) -> p u q e", u=2, e=2), MULT)
+        def weigh(n):
+            factor = wgs_sb if n < PER_PASS else wgs_dealt[n - PER_PASS]
+            dst, factor = (t.rearrange("p (h k c) -> p h k c", h=2, k=2) for t in (put_of[n], factor[:]))
+            if n == 1:
+                for h in range(2):
+                    nc.gpsimd.tensor_tensor(dst[:, h], first_summed[h], factor[:, h], MULT)
             else:
-                nc.scalar.copy(out=spare.rearrange("p (b u q e) -> p b u q e", u=2, q=32, e=2),
-                               in_=bank[:, 0 : m1 - m0].rearrange("p (b q u e) -> p b u q e", u=2, q=32, e=2))
-                nc.gpsimd.tensor_tensor(dst, spare.rearrange("p (b u r) -> p b u r", u=2, r=64),
-                                        factor.rearrange("p (b u r) -> p b u r", u=2, r=64), MULT)
+                nc.gpsimd.tensor_tensor(dst, summed[n], factor, MULT)
 
-        def back_turns(h, pair, bank):
-            words = z_t[h][:].bitcast(F32)
-            return [turning(bank[:, block(i)], words[:, block(BLOCKS * pair + i)], True, True) for i in range(BLOCKS)]
+        def place(s, cols):
+            nc.vector.tensor_copy(pages[s % 2][:].indirect(entries(idx2, cols)), put_of[s][:, cols])
 
-        def keep_back(h, pair, bank, copy):
-            first = 2 * (h * HALF + pair * 256)
-            copy(out=z_words[:, first : first + 512].rearrange("p (b m u) -> p b m u", b=2, u=2),
-                 in_=bank[:].rearrange("p (b u m) -> p b m u", b=2, u=2))
+        def fetch_outer(s, h, dst):
+            nc.vector.tensor_scalar(dst, pages[s % 2][:].indirect(entries(idx4, half(h))), -1.0, 1.0, MULT, ADD)
 
-        def quantise_z(g, m0, m1):
-            nc.vector.quantize_mx(out=z_w[g][:, m0:m1].bitcast(FP8X4), scales=z_s[g][:, m0:m1],
-                                  in_=z_words[:, 2 * m0 : 2 * m1].bitcast(BF16))
+        def add_inner(s, cols, dst, outer_part):
+            nc.vector.tensor_tensor(dst, pages[s % 2][:].indirect(entries(idx3, cols)), outer_part, ADD)
 
-        def product(acc, g, nb, cols, start, stop):
-            w_cols = slice(g * N + nb * P, g * N + (nb + 1) * P)
-            return lambda: nc.tensor.matmul_mx(out=acc, lhsT=wd_w[0][:, w_cols].bitcast(FP8X4), lhsT_scale=wd_s[:, w_cols],
-                                rhs=z_w[g][:, cols].bitcast(FP8X4), rhs_scale=z_s[g][:, cols], start=start, stop=stop)
+        def fetch_inner(s, cols):
+            add_inner(s, cols, jump[s][:, cols], outer[s][:, cols])
 
-        def half_products(g, out_banks):
-            for nb, bank in enumerate(out_banks):
-                product(bank[:], g, nb, slice(0, HALF), g == 0, g == 1)()
+        def stiffen(s):
+            dst = z_rows[s] if s < PER_PASS else z_pair.rearrange("p (m e) -> p m e", e=2)[:, :, s - PER_PASS]
+            nc.gpsimd.tensor_tensor(dst, jump[s], stiff_sb[s][:], MULT)
 
-        def half_store(nb, bank):
-            cols = slice(0, HALF)
-            nc.scalar.copy(staged[nb][:, cols], bank[:])
-            nc.sync.dma_start(out=out[block(nb), cols], in_=staged[nb][:, cols])
+        def turn_rows(s):
+            for h in range(2):
+                turned = bank_s[h][:].bitcast(BF16)
+                for i in range(BLOCKS):
+                    turn(turned[:, block(i)], z_rows[s][:, block(BLOCKS * h + i)], by=ident_bf)
+                dst = z_t[h][:].bitcast(F32).rearrange("p (b u w) -> p b u w", b=BLOCKS, u=2)[:, :, :, 32 * s : 32 * (s + 1)]
+                nc.scalar.copy(out=dst, in_=bank_s[h][:, 0:QUARTER].rearrange("p (b q u) -> p b u q", b=BLOCKS, u=2))
 
-        def quarter_products(pair, b, bank, g, alone=False):
-            width = HALF // 2
-            cols = slice(HALF + pair * width, HALF + (pair + 1) * width)
-            return [product(bank[:, a * width : (a + 1) * width], g, 2 * b + a, cols,
-                            (alone or g == 0) and a == 0, (alone or g == 1) and a == 1) for a in range(2)]
-
-        def quarter_store(pair, b, bank):
-            width = HALF // 2
-            cols = slice(HALF + pair * width, HALF + (pair + 1) * width)
-            stage = staged[2 * pair + b][:, HALF:F]
-            if b == 0:
-                nc.scalar.copy(stage, bank[:])
-            else:
-                nc.vector.tensor_tensor(stage, bank[:], resp[pair], ADD)
-            nc.sync.dma_start(out=out[2 * b * P : 2 * (b + 1) * P, cols].rearrange("(a p) m -> p a m", a=2),
-                              in_=stage.rearrange("p (a m) -> p a m", a=2))
-
-        def load_wd(g):
-            nc.sync.dma_start(out=wb_raw[3][:], in_=wd[g * K : (g + 1) * K, :].rearrange("(p j) c -> p j c", j=4))
-            for c0 in (0, N // 2):
-                interleave(w_bf[:, 4 * (g * N + c0) : 4 * (g * N + c0 + N // 2)], wb_raw[3][:, :, c0 : c0 + N // 2],
-                           nc.scalar.copy)
-
-        def early(s, h):
-            if DEFERRED.get(s) == h:
-                kept = (outer[1], staged[3][:, 0:HALF], inner[1], None, staged[2][:, HALF:F])
-                return h_of[s + 1][:, HALF:S], kept[s]
-            if s == SLICES - 1:
-                return plain_all[0][:, 0:HALF], plain_all[0][:, HALF:S]
-            if s >= PER_PASS:
-                return inner[s % 2], outer[s % 2]
-            cols = slice(h * HALF, (h + 1) * HALF)
-            return (inner[0], outer[0]) if s % 2 == 0 else (staged[0][:, cols], staged[1][:, cols])
-
-        respond_first(0)
-        respond_first(1)
-        for h in range(2):
-            nc.vector.tensor_copy(pages[0][:].indirect(half_of(idx2, h)), first_put[h])
-        respond(1)
-        round_wb(2, outer[0].bitcast(BF16), nc.scalar.copy)
-        quantise_wb(2, outer[0].bitcast(BF16))
-        load_stiff(0)
-        for h in range(2):
-            cols = slice(h * HALF, (h + 1) * HALF)
-            two = ((bank_a, bank_c), (bank_b0, bank_b1))[h]
-            parts = [slice(cols.start + k * HALF // 2, cols.start + (k + 1) * HALF // 2) for k in range(2)]
-            weave(*(add_transposed(two[k], gate_all[1][:, parts[k]], plain_all[1][:, parts[k]], 2) for k in range(2)))
-            for k in range(2):
-                nc.scalar.copy(h_of[1][:, parts[k]], two[k][:, 0 : HALF // 2])
-            weigh(1, cols)
-        round_wb(3, staged[2][:].bitcast(BF16), nc.scalar.copy)
-        respond(2)
-        respond(3)
-        total(2, [(0, 0, bank_b0), (0, 1, bank_b1)])
-        quarter = HALF // 2
-
-        def piece(tile, k):
-            return tile[:, k * quarter : (k + 1) * quarter]
-
-        for s in range(SLICES):
-            if s > 0:
-                nc.vector.tensor_copy(page_of[s][:].indirect(idx2[:]), put_of[s])
-            if s - 1 in DEFERRED:
-                h = DEFERRED[s - 1]
-                fetch_inner(s - 1, h * HALF, (h + 1) * HALF, early(s - 1, h)[0])
-            if s == 6:
-                wd_w.append(one("wd_w", [P, 2 * N], U32, "behind6"))
-                nc.vector.quantize_mx(out=wd_w[0][:].bitcast(FP8X4), scales=wd_s[:], in_=w_bf[:])
-            halves = range(2) if s < PER_PASS else range(1)
-            for h in halves:
-                fetch_outer(s, h, early(s, h)[1])
-            if s == PER_PASS - 1:
-                fetch_inner(s, 0, F, staged[0][:])
-            elif DEFERRED.get(s) != 0:
-                fetch_inner(s, 0, HALF, early(s, 0)[0])
-            if s == 0:
-                quantise_wb(3, staged[2][:].bitcast(BF16))
-            if s == 6:
-                z_w.setdefault(0, one("z_w0", [P, F], U32, "behind6b"))
-                quantise_z(0, 0, F)
-                weave(*(quarter_products(pair, 1, bank_d[pair], 0, True) for pair in range(2)))
+        def turn_back():
+            for h in range(2):
+                words = z_t[h][:].bitcast(F32)
                 for pair in range(2):
-                    nc.scalar.copy(resp[pair], bank_d[pair][:])
+                    bank = (bank_a, bank_b)[h][pair]
+                    for i in range(BLOCKS):
+                        turn(bank[:, block(i)], words[:, block(BLOCKS * pair + i)])
+                    first = 2 * (h * HALF + pair * QUARTER)
+                    nc.scalar.copy(out=z_words[:, first : first + HALF].rearrange("p (b m u) -> p b m u", b=2, u=2),
+                                   in_=bank[:].rearrange("p (b u m) -> p b m u", b=2, u=2))
+
+        def quantise_z(g, cols, values):
+            nc.vector.quantize_mx(out=z_w[g][:, cols].bitcast(FP8X4), scales=z_s[g][:, cols],
+                                  in_=values[:, 4 * cols.start : 4 * cols.stop])
+
+        pieces = ((half(0), (bank_a[0], bank_a[1], bank_b[0], bank_b[1])),
+                  (slice(HALF, HALF + QUARTER), bank_c), (slice(HALF + QUARTER, F), bank_s))
+
+        def last_products(g, cols, out_banks):
+            width = cols.stop - cols.start
+            per_bank = HALF // width
+            for nb in range(N // P):
+                a = nb % per_bank
+                w_cols = slice(g * N + nb * P, g * N + (nb + 1) * P)
+                nc.tensor.matmul_mx(out=out_banks[nb // per_bank][:, a * width : (a + 1) * width],
+                                    lhsT=wd_w[:, w_cols].bitcast(FP8X4), lhsT_scale=wd_s[:, w_cols],
+                                    rhs=z_w[g][:, cols].bitcast(FP8X4), rhs_scale=z_s[g][:, cols],
+                                    start=g == 0 and a == 0, stop=g == 1 and a == per_bank - 1)
+
+        def store(cols, out_banks, stages, copies):
+            per_bank = HALF // (cols.stop - cols.start)
+            for b, bank in enumerate(out_banks):
+                copies[b](out=stages[b], in_=bank[:])
+                rows = out[b * per_bank * P : (b + 1) * per_bank * P, cols]
+                nc.sync.dma_start(out=rows.rearrange("(a p) m -> p a m", a=per_bank),
+                                  in_=stages[b].rearrange("p (a m) -> p a m", a=per_bank))
+
+        round_wb(0, nc.vector.tensor_copy)
+        quantise_wb(0)
+        first = (slice(0, QUARTER), slice(QUARTER, HALF), half(1))
+        first_banks = ((bank_b[0][:, 0:QUARTER], bank_a[0][:, 0:QUARTER], bank_c[0][:, 0:QUARTER]),
+                       (bank_s[0][:, 0:QUARTER], bank_s[1][:, 0:QUARTER], bank_c[0][:, QUARTER:HALF]),
+                       (bank_b[1][:], bank_a[1][:], bank_c[1][:]))
+        first_gate = (put[1][:, first[0]], w_bf[:, 3 * HALF : 4 * HALF].bitcast(F32), put[1][:, first[2]])
+        first_put = (put[1][:, QUARTER:HALF], put[1][:, HALF : HALF + QUARTER], put[0][:, half(1)])
+        for c0 in (P, 2 * P):
+            nc.gpsimd.tensor_scalar(w_bf[:, 4 * c0 : 4 * (c0 + P)].rearrange("p (c t) -> p c t", t=4),
+                                    wb_raw[1][:, :, c0 - P : c0].rearrange("p t c -> p c t"), 1.0, 0.0, MULT, ADD)
+        for h in range(2):
+            nc.vector.tensor_copy(v_s[h][:], tab_s[:].indirect(entries(idx1, half(h))))
+        for k, cols in enumerate(first):
+            h, c0 = divmod(cols.start, HALF)
+            here = slice(c0, c0 + cols.stop - cols.start)
+            nc.vector.tensor_copy(v_w[h][:, here], tab_w[:].indirect(entries(idx1, cols)))
+            for acc, (codes, scales) in zip(first_banks[k], weights(0)):
+                nc.tensor.matmul_mx(out=acc, lhsT=codes, lhsT_scale=scales, rhs=v_w[h][:, here].bitcast(FP8X4),
+                                    rhs_scale=v_s[h][:, here], start=True, stop=True)
+            nc.scalar.activation(first_gate[k], first_banks[k][0], SIGMOID)
+        first_gated = [work[1][:, cols] for cols in first]
+        first_sum = (work[0][:, first[0]], work[0][:, first[1]], gated[1][:, QUARTER : QUARTER + HALF])
+        for k in range(2):
+            nc.vector.tensor_tensor(first_gated[k], first_banks[k][1], first_gate[k], MULT)
+        for k in range(2):
+            nc.vector.tensor_tensor(first_sum[k], first_banks[k][2], first_gated[k], ADD)
+        nc.vector.tensor_tensor(first_gated[2], first_banks[2][1], first_gate[2], MULT)
+        quantise_wb(1)
+        nc.vector.tensor_tensor(first_sum[2], first_banks[2][2], first_gated[2], ADD)
+        for k, cols in enumerate(first):
+            nc.gpsimd.tensor_tensor(first_put[k], first_sum[k], wgs_sb[:, cols], MULT)
+        for h, values in enumerate((put[1][:, QUARTER : QUARTER + HALF], first_put[2])):
+            nc.vector.tensor_copy(pages[0][:].indirect(entries(idx2, half(h))), values)
+        products(1)
+        gate_and_sum(1)
+        weigh(1)
+        for h in range(2):
+            fetch_outer(0, h, outer[0][:, half(h)])
+        round_wb(2, nc.scalar.copy)
+        products(2)
+        gate_and_sum(2)
+        dealt_bytes = one("dealt_bytes", [P, 13 * K], U8, "behind2")
+        wb_w.update({2: dealt_bytes[:, 8 * K : 9 * K].bitcast(U32), 3: dealt_bytes[:, 9 * K : 13 * K].bitcast(U32)})
+        quantise_wb(2)
+        round_wb_dealt()
+        quantise_wb(3)
+        weigh(2)
+        products(3)
+        dealt_weights = (dealt_bytes[:, 0 : 2 * K], dealt_bytes[:, 2 * K : 3 * K],
+                         dealt_bytes[:, 4 * K : 8 * K].bitcast(U32), dealt_bytes[:, 3 * K : 4 * K])
+        for dst, src in zip(dealt_weights, (wa_w[:, 2 * K : 2 * H], wa_s[:, K:H], wc_w[:, K:H], wc_s[:, K:H])):
+            deal_columns(dst, src)
+
+        last = SLICES - 1
+        wd_bf = []
+        for s in range(1, last):
+            place(s, slice(0, S))
+            if s in (PER_PASS, PER_PASS + 1):
+                cols = half(s - PER_PASS)
+                nc.vector.quantize_mx(out=wd_w[:, cols].bitcast(FP8X4), scales=wd_s[:, cols], in_=wd_bf[s - PER_PASS][:])
+            fetch_inner(s - 1, slice(0, F))
+            if s + 2 < SLICES:
+                gate_and_sum(s + 2)
+            stiffen(s - 1)
             if s + 2 < SLICES:
                 weigh(s + 2)
-            for r in {4: (5, 6, 7), 5: (), 6: (), 7: ()}.get(s, (s + 1,)):
-                load_stiff(r)
-            if s + 4 < SLICES:
-                respond(s + 4)
-            if s < SLICES - 2:
-                ready = [(s - 1, DEFERRED[s - 1])] if s - 1 in DEFERRED else []
-                ready = ready + [(s, h) for h in halves if DEFERRED.get(s) != h]
-                sum_banks = (bank_b0, bank_b1, bank_a) if s + 3 < SLICES else (bank_a, bank_o0)
-                if s == PER_PASS - 1:
-                    total(s + 3, [(s + 1, 0, bank_b0)])
-                    sum_banks = (bank_b1, bank_a, bank_o0)
-                runs = [add_transposed(sum_banks[k], *reversed(early(r, h)), BLOCKS) for k, (r, h) in enumerate(ready)]
-                late_stiff = []
-                if s == PER_PASS + 1:
-                    late_stiff = [(5, 0, bank_b0), (6, 0, bank_b1), (7, 0, bank_c), (4, 1, bank_o1)]
-                weave(*runs, *(stiff_turns(*item) for item in late_stiff))
-                for item in late_stiff[:1]:
-                    keep_stiff(*item)
-                for k, (r, h) in enumerate(ready):
-                    combine(r, h * HALF, (h + 1) * HALF, sum_banks[k], jump[k][:])
-                for item in late_stiff[1:]:
-                    keep_stiff(*item)
-                if s == PER_PASS + 1:
-                    last_stiff = [(5, 1, bank_b0), (6, 1, bank_b1), (7, 1, bank_c)]
-                    weave(*(stiff_turns(*item) for item in last_stiff))
-                    for item in last_stiff:
-                        keep_stiff(*item)
-            else:
-                x1, x2 = early(s, 0)
-                two = bank_d if s == SLICES - 1 else bank_o
-                for k in range(2):
-                    weave(add_transposed(two[k], piece(x2, k), piece(x1, k), 2))
-                    combine(s, k * quarter, (k + 1) * quarter, two[k], piece(jump[0], k))
-            if s == PER_PASS:
-                for h, back_banks in enumerate(((bank_b0, bank_b1), bank_d)):
-                    weave(*(back_turns(h, pair, back_banks[pair]) for pair in range(2)))
-                    for pair in range(2):
-                        keep_back(h, pair, back_banks[pair], nc.scalar.copy)
-            if s < PER_PASS - 1:
-                total(s + 3, [(s + 1, 0, bank_b0), (s + 1, 1, bank_b1)])
-            if s == PER_PASS:
-                total(s + 3, [])
-            if s in (0, 1):
-                load_wd(s)
-            if s == 2:
-                page_of.append(one("last_page", [P, T2], F32, "last_page"))
-                nc.gpsimd.memset(page_of[-1][:], 0.0)
+            if s + 3 < SLICES:
+                products(s + 3)
+            if s - 1 < PER_PASS:
+                turn_rows(s - 1)
+            if s in (2, 3):
+                g = s - 2
+                wd_bf.append(one("wd_bf%d" % g, [P, 4 * N], BF16, "behind%d" % (s + 2)))
+                for c0 in range(0, N, P):
+                    interleave(wd_bf[g][:, 4 * c0 : 4 * (c0 + P)], wd_raw[:, g, :, c0 : c0 + P], nc.scalar.copy)
+            if s == PER_PASS + 1:
+                turn_back()
+            for h in range(2 if s < last - 1 else 1):
+                fetch_outer(s, h, outer[s][:, half(h)])
 
-        third, fourth = (HALF, HALF + quarter), (HALF + quarter, F)
-        wide = (bank_a, bank_b0, bank_b1, bank_c)
-        x1_first, x2_first = early(SLICES - 1, 0)
-        x2 = {4: put[1][:, 0:HALF], 5: x2_first, 6: z_words[:, 0:HALF], 7: x2_first}
-        x1 = {4: put[1][:, HALF:S], 5: x1_first, 6: z_words[:, HALF:F]}
-        x1_last = (piece(x2[6], 0), piece(x1[6], 0))
-        half_products(0, wide)
-        for pair in range(2):
-            weave(back_turns(0, pair, bank_o[pair]))
-            keep_back(0, pair, bank_o[pair], nc.scalar.copy)
-        for s in (4, 5):
-            fetch(s, 1, x1[s], x2[s])
-            weave(add_transposed(bank_o[s % 2], x1[s], x2[s], BLOCKS))
-            combine(s, HALF, F, bank_o[s % 2], jump[2 * (s % 2)][:])
-        quantise_z(1, 0, HALF)
-        half_products(1, wide)
-        fetch(6, 1, x1[6], x2[6])
-        fetch_outer(7, 1, x2[7])
-        for k, cols in enumerate((third, fourth)):
-            weave(add_transposed(bank_d[k], piece(x2[6], k), piece(x1[6], k), 2))
-            combine(6, *cols, bank_d[k], piece(gate[0], k))
-        for k, cols in enumerate((third, fourth)):
-            fetch_inner(7, *cols, x1_last[k])
-        for nb in range(2):
-            half_store(nb, wide[nb])
-        weave(quarter_products(1, 0, bank_a, 0))
-        for k, cols in enumerate((third, fourth)):
-            weave(add_transposed(bank_o[k], piece(x2[7], k), x1_last[k], 2))
-            combine(7, *cols, bank_o[k], None)
-        for pair in range(2):
-            weave(back_turns(1, pair, bank_d[pair]))
-            keep_back(1, pair, bank_d[pair], nc.scalar.copy)
-        for nb in range(2, 4):
-            half_store(nb, wide[nb])
-        weave(quarter_products(0, 0, bank_d0, 0))
-        quantise_z(1, *third)
-        quantise_z(1, *fourth)
-        last_banks = ((bank_d0, bank_o0), (bank_a, bank_b0))
-        for pair in range(2):
-            for b in range(2):
-                weave(quarter_products(pair, b, last_banks[pair][b], 1, b == 1))
-        for pair in range(2):
-            for b in range(2):
-                quarter_store(pair, b, last_banks[pair][b])
+        slots = z_last[:].rearrange("p (m t) -> p m t", t=PER_PASS)
+        for h in range(2):
+            nc.scalar.copy(out=z_last[:].bitcast(F32).rearrange("p (m u) -> p m u", u=2)[:, half(h), 0],
+                           in_=z_pair.bitcast(F32)[:, half(h)])
+        jump6, outer7 = work[0][:, S + QUARTER : S + QUARTER + HALF], work[0][:, S : 2 * S]
+        outer6_late = z_words[:, 0:HALF]
+        stiff7, jump7 = late[:, 0:HALF], work[0][:, 0:HALF]
+        late_jumps = {HALF: stiff7.rearrange("p (e m) -> p m e", e=2),
+                      HALF + QUARTER: work[0][:].rearrange("p (k m) -> p m k", m=QUARTER)[:, :, 0:7:6]}
+        late_stiff = late[:, HALF : 3 * HALF].rearrange("p (e m) -> p m e", e=2)
+        place(last, half(0))
+        add_inner(last - 1, half(0), jump6, outer[last - 1][:, half(0)])
+        place(last, half(1))
+        nc.gpsimd.tensor_tensor(slots[:, half(0), 2], jump6, stiff6, MULT)
+        z_w.setdefault(0, one("z_w0", [P, F], U32, "behind6"))
+        quantise_z(0, half(0), z_words[:].bitcast(BF16))
+        fetch_outer(last, 0, outer7[:, half(0)])
+        quantise_z(0, half(1), z_words[:].bitcast(BF16))
+        add_inner(last, half(0), jump7, outer7[:, half(0)])
+        fetch_outer(last - 1, 1, outer6_late)
+        fetch_outer(last, 1, outer7[:, half(1)])
+        for cols, out_banks in pieces:
+            last_products(0, cols, out_banks)
+        nc.gpsimd.tensor_tensor(slots[:, half(0), 3], jump7, stiff7, MULT)
+        stages = [t[:, half(h)] for h in range(2) for t in staged]
+        at = 0
+        for cols, out_banks in pieces:
+            if cols.start >= HALF:
+                here = slice(cols.start - HALF, cols.stop - HALF)
+                add_inner(last - 1, cols, late_jumps[cols.start][:, :, 0], outer6_late[:, here])
+                add_inner(last, cols, late_jumps[cols.start][:, :, 1], outer7[:, cols])
+                nc.vector.tensor_tensor(slots[:, cols, 2:4], late_jumps[cols.start], late_stiff[:, here], MULT)
+            quantise_z(1, cols, z_last[:])
+            last_products(1, cols, out_banks)
+            copies = [nc.scalar.copy] * len(out_banks) if cols.stop < F else [nc.scalar.copy, nc.vector.tensor_copy]
+            store(cols, out_banks, stages[at : at + len(out_banks)], copies)
+            at = at + len(out_banks)

@@ -70,27 +70,30 @@ def tile_list_bone_face_features_kernel(
         wc_w = one("wc_w", [P, H], U32)
         wa_s = one("wa_s", [P, H], U8)
         wc_s = one("wc_s", [P, H], U8)
-        first_outer = one("first_outer", [P, F], F32)
-        wb_flat = [one("wb_raw%d" % i, [P, 4 * (c1 - c0)], F32)[:] for i, (c0, c1) in enumerate(WB_CHUNKS)]
+        wb_last = one("wb_last", [P, 5 * HALF], F32)
+        wb_flat = [one("wb_raw%d" % i, [P, 4 * (c1 - c0)], F32)[:] for i, (c0, c1) in enumerate(WB_CHUNKS[:3])]
+        wb_flat.append(wb_last[:, HALF : 5 * HALF])
         wb_raw = [flat.rearrange("p (j c) -> p j c", j=4) for flat in wb_flat]
         w_bf = one("w_bf", [P, 4 * H], BF16)
         wb_w = {i: one("wb_w%d" % i, [P, c1 - c0], U32) for i, (c0, c1) in enumerate(WB_CHUNKS) if i < 2}
         wb_s = one("wb_s", [P, H], U8)
-        wd_w = one("wd_w", [P, 2 * N], U32)
         wd_s = one("wd_s", [P, 2 * N], U8)
-        wgs_sb = one("wgs_sb", [P, S], F32)
+        wgs_sb = one("wgs_sb", [P, S], F32, "behind3")
         wgs_dealt = [one("wgs_dealt%d" % t, [P, S], F32, "behind%d" % (t + PER_PASS) if t < 2 else "") for t in range(PER_PASS)]
         pages = tiles("page", 2, [P, T2], F32)
-        work = tiles("work", 2, [P, 2 * S], F32)
+        sum_ring = tiles("sum_ring", 3, [P, S], F32)
+        outer_ring = tiles("outer_ring", 3, [P, F], F32)
         gate = one("gate", [P, S], F32)
         resp = tiles("resp", 2, [P, S], F32)
         plain = one("plain", [P, S], F32)
         put = tiles("put", 2, [P, S], F32)
-        gate_of = {n: gate[:] for n in range(3, SLICES)}
-        gate_of.update({1: w_bf[:, 2 * S : 4 * S].bitcast(F32), 2: one("second_gate", [P, S], F32, "behind2")[:]})
-        stiff_sb = tiles("stiff_sb", SLICES - 2, [P, F], F32)
-        z_t = tiles("z_t", 2, [P, BLOCKS * HALF], BF16)
-        z_pair = resp[(SLICES - 1) % 2][:].bitcast(BF16)
+        gate_of = {n: gate[:] for n in range(1, SLICES)}
+        gate_of.update({2: one("second_gate", [P, S], F32, "behind2")[:]})
+        ends = one("ends", [P, 2 * S], F32)[:]
+        stiff_sb = [t[:] for t in tiles("stiff_sb", SLICES - 3, [P, F], F32)] + [ends[:, S : 2 * S]]
+        z_ends = one("z_t", [P, 2 * BLOCKS * HALF], BF16)
+        z_t = [z_ends[:, h * BLOCKS * HALF : (h + 1) * BLOCKS * HALF] for h in range(2)]
+        z_pair = gate[:].bitcast(BF16)
         z_last = one("z_last", [P, 4 * F], BF16)
         stiff6 = one("stiff6", [P, F], F32, "behind6")[:, half(0)]
         late = one("late", [P, 3 * HALF], F32)
@@ -98,15 +101,17 @@ def tile_list_bone_face_features_kernel(
         z_w = {1: one("z_w1", [P, F], U32)}
         z_s = tiles("z_s", 2, [P, F], U8)
 
-        outer = [first_outer[:]] + [work[(s + 1) % 2][:, S : 2 * S] for s in range(1, SLICES)]
-        gated = {n: outer[n - 3] if n >= 3 else work[n % 2][:, S : 2 * S] for n in range(1, SLICES)}
+        outer = [outer_ring[s % 3][:] for s in range(SLICES)]
+        summed = {n: sum_ring[n % 3][:] for n in range(1, SLICES)}
+        inner = [sum_ring[(s + 1) % 3][:] for s in range(SLICES)]
+        jump = [resp[(s + 3) % 2][:] for s in range(SLICES - 3)] + [stiff_sb[SLICES - 4]]
+        gated = {n: stiff_sb[n - PER_PASS] for n in range(PER_PASS, SLICES)}
+        gated.update({1: z_t[0].bitcast(F32), 2: w_bf[:, S : 3 * S].bitcast(F32), 3: z_t[1].bitcast(F32)})
         put_of = [put[s % 2][:] for s in range(SLICES)]
-        put_of[2] = wb_flat[3][:, 0:S]
-        gated[2] = work[1][:, 0:S]
-        jump = [work[s % 2][:, 0:S] for s in range(SLICES)]
-        summed = {n: work[n % 2][:].rearrange("p (k h c) -> p h k c", k=2, h=2)[:, :, :, 0:QUARTER] for n in range(1, SLICES)}
-        first_summed = [t.rearrange("p (k c) -> p k c", k=2) for t in (work[0][:, half(0)], gated[2][:, QUARTER : QUARTER + HALF])]
-        z_rows = [resp[(s + 3) % 2][:, QUARTER : QUARTER + HALF].bitcast(BF16) for s in range(PER_PASS)]
+        put_of[1] = wb_last[:, 0:S]
+        split_sums = {1: (one("early_sum", [P, HALF], F32, "behind1")[:], summed[1][:, half(1)]),
+                      2: (gated[3][:, half(0)], summed[2][:, half(1)])}
+        z_rows = one("z_rows", [P, F], BF16)
         staged = stiff_sb[0:4]
 
         def dealt(rows, t):
@@ -128,7 +133,7 @@ def tile_list_bone_face_features_kernel(
 
         def load_stiff(s):
             rows = stiff[block(s), :] if s < PER_PASS else dealt(stiff[K:H, :], s - PER_PASS)
-            nc.sync.dma_start(out=stiff_sb[s][:], in_=rows)
+            nc.sync.dma_start(out=stiff_sb[s][:, :], in_=rows)
 
         nc.sync.dma_start(idx1[:], offs)
         load_wb(0)
@@ -145,20 +150,20 @@ def tile_list_bone_face_features_kernel(
         nc.sync.dma_start(out=wgs_sb[:, half(0)], in_=wgs[:, half(0)])
         nc.sync.dma_start(out=wgs_sb[:, half(1)], in_=wgs[:, half(1)])
         load_wb(2)
+        load_wb(3)
         nc.sync.dma_start(idx4[:], offs4)
         nc.sync.dma_start(out=wa_w[:, 512 : 2 * H].bitcast(I32), in_=wa_rows[:, 128 : H // 2])
         nc.sync.dma_start(out=wc_w[:, 256:H].bitcast(I32), in_=wc_rows[:, 256:H])
         nc.sync.dma_start(idx3[:], offs3)
-        load_wb(3)
         wd_raw = one("wd_raw", [P, 2, 4, N], F32, "table")
         for s in range(SLICES - 2):
             load_stiff(s)
             if s < PER_PASS:
                 for a in range(4):
                     nc.sync.dma_start(out=wgs_dealt[s][32 * a : 32 * (a + 1), :], in_=dealt(wgs, s))
-            if s == 2:
+            if s == 0:
                 nc.sync.dma_start(out=wd_raw[:, 0], in_=wd[0:K, :].rearrange("(p j) c -> p j c", j=4))
-            if s == 3:
+            if s == 1:
                 for t in range(PER_PASS):
                     nc.sync.dma_start(out=wd_raw[:, 1, t], in_=dealt(wd[K:H, :], t))
         for dst, t, h in ((stiff6, 2, 0), (late[:, HALF:S], 2, 1), (late[:, 0:HALF], 3, 0), (late[:, S : 3 * HALF], 3, 1)):
@@ -219,24 +224,23 @@ def tile_list_bone_face_features_kernel(
                 nc.scalar.copy(plain[:, half(h)], bank_c[h][:])
 
         def gate_and_sum(n):
-            bank_s = bank_b if n == 2 else banks[6:8]
             for h in range(2):
                 for i in range(BLOCKS):
                     turn(bank_s[h][:, block(i)], plain[:, block(BLOCKS * h + i)], i == 0, False)
+            for cols in (half(0), half(1)) if n == 1 else (slice(0, S),):
+                nc.gpsimd.tensor_tensor(gated[n][:, cols], resp[n % 2][:, cols], gate_of[n][:, cols], MULT)
             for h in range(2):
-                nc.gpsimd.tensor_tensor(gated[n][:, half(h)], resp[n % 2][:, half(h)], gate_of[n][:, half(h)], MULT)
                 for i in range(BLOCKS):
                     turn(bank_s[h][:, block(i)], gated[n][:, block(BLOCKS * h + i)], False, i == BLOCKS - 1)
-                nc.scalar.copy(out=first_summed[h] if n == 1 else summed[n][:, h], in_=bank_s[h][:].rearrange("p (k c) -> p k c", k=2))
+                nc.scalar.copy(split_sums[n][h] if n in split_sums else summed[n][:, half(h)], bank_s[h][:])
 
         def weigh(n):
             factor = wgs_sb if n < PER_PASS else wgs_dealt[n - PER_PASS]
-            dst, factor = (t.rearrange("p (h k c) -> p h k c", h=2, k=2) for t in (put_of[n], factor[:]))
-            if n == 1:
+            if n in split_sums:
                 for h in range(2):
-                    nc.gpsimd.tensor_tensor(dst[:, h], first_summed[h], factor[:, h], MULT)
+                    nc.gpsimd.tensor_tensor(put_of[n][:, half(h)], split_sums[n][h], factor[:, half(h)], MULT)
             else:
-                nc.gpsimd.tensor_tensor(dst, summed[n], factor, MULT)
+                nc.gpsimd.tensor_tensor(put_of[n], summed[n], factor[:], MULT)
 
         def place(s, cols):
             nc.vector.tensor_copy(pages[s % 2][:].indirect(entries(idx2, cols)), put_of[s][:, cols])
@@ -247,24 +251,24 @@ def tile_list_bone_face_features_kernel(
         def add_inner(s, cols, dst, outer_part):
             nc.vector.tensor_tensor(dst, pages[s % 2][:].indirect(entries(idx3, cols)), outer_part, ADD)
 
-        def fetch_inner(s, cols):
-            add_inner(s, cols, jump[s][:, cols], outer[s][:, cols])
+        def fetch_inner(s, cols, dst):
+            nc.vector.tensor_copy(dst, pages[s % 2][:].indirect(entries(idx3, cols)))
 
         def stiffen(s):
-            dst = z_rows[s] if s < PER_PASS else z_pair.rearrange("p (m e) -> p m e", e=2)[:, :, s - PER_PASS]
-            nc.gpsimd.tensor_tensor(dst, jump[s], stiff_sb[s][:], MULT)
+            dst = z_rows[:] if s < PER_PASS else z_pair.rearrange("p (m e) -> p m e", e=2)[:, :, s - PER_PASS]
+            nc.gpsimd.tensor_tensor(dst, jump[s], stiff_sb[s][:, :], MULT)
 
         def turn_rows(s):
             for h in range(2):
                 turned = bank_s[h][:].bitcast(BF16)
                 for i in range(BLOCKS):
-                    turn(turned[:, block(i)], z_rows[s][:, block(BLOCKS * h + i)], by=ident_bf)
-                dst = z_t[h][:].bitcast(F32).rearrange("p (b u w) -> p b u w", b=BLOCKS, u=2)[:, :, :, 32 * s : 32 * (s + 1)]
+                    turn(turned[:, block(i)], z_rows[:, block(BLOCKS * h + i)], by=ident_bf)
+                dst = z_t[h].bitcast(F32).rearrange("p (b u w) -> p b u w", b=BLOCKS, u=2)[:, :, :, 32 * s : 32 * (s + 1)]
                 nc.scalar.copy(out=dst, in_=bank_s[h][:, 0:QUARTER].rearrange("p (b q u) -> p b u q", b=BLOCKS, u=2))
 
         def turn_back():
             for h in range(2):
-                words = z_t[h][:].bitcast(F32)
+                words = z_t[h].bitcast(F32)
                 for pair in range(2):
                     bank = (bank_a, bank_b)[h][pair]
                     for i in range(BLOCKS):
@@ -287,7 +291,7 @@ def tile_list_bone_face_features_kernel(
                 a = nb % per_bank
                 w_cols = slice(g * N + nb * P, g * N + (nb + 1) * P)
                 nc.tensor.matmul_mx(out=out_banks[nb // per_bank][:, a * width : (a + 1) * width],
-                                    lhsT=wd_w[:, w_cols].bitcast(FP8X4), lhsT_scale=wd_s[:, w_cols],
+                                    lhsT=wd_w[g][:, block(nb)].bitcast(FP8X4), lhsT_scale=wd_s[:, w_cols],
                                     rhs=z_w[g][:, cols].bitcast(FP8X4), rhs_scale=z_s[g][:, cols],
                                     start=g == 0 and a == 0, stop=g == 1 and a == per_bank - 1)
 
@@ -320,8 +324,8 @@ def tile_list_bone_face_features_kernel(
                 nc.tensor.matmul_mx(out=acc, lhsT=codes, lhsT_scale=scales, rhs=v_w[h][:, here].bitcast(FP8X4),
                                     rhs_scale=v_s[h][:, here], start=True, stop=True)
             nc.scalar.activation(first_gate[k], first_banks[k][0], SIGMOID)
-        first_gated = [work[1][:, cols] for cols in first]
-        first_sum = (work[0][:, first[0]], work[0][:, first[1]], gated[1][:, QUARTER : QUARTER + HALF])
+        first_gated = [outer_ring[1][:, cols] for cols in first]
+        first_sum = (outer_ring[2][:, first[0]], outer_ring[2][:, first[1]], gated[1][:, QUARTER : QUARTER + HALF])
         for k in range(2):
             nc.vector.tensor_tensor(first_gated[k], first_banks[k][1], first_gate[k], MULT)
         for k in range(2):
@@ -335,64 +339,68 @@ def tile_list_bone_face_features_kernel(
             nc.vector.tensor_copy(pages[0][:].indirect(entries(idx2, half(h))), values)
         products(1)
         gate_and_sum(1)
+        round_wb(2, nc.scalar.copy)
+        round_wb_dealt()
         weigh(1)
         for h in range(2):
             fetch_outer(0, h, outer[0][:, half(h)])
-        round_wb(2, nc.scalar.copy)
+        late_codes = one("late_codes", [P, P + K], U32, "behind1")
+        wb_w.update({2: late_codes[:, 0:P], 3: late_codes[:, P : P + K]})
+        quantise_wb(2)
+        quantise_wb(3)
         products(2)
         gate_and_sum(2)
-        dealt_bytes = one("dealt_bytes", [P, 13 * K], U8, "behind2")
-        wb_w.update({2: dealt_bytes[:, 8 * K : 9 * K].bitcast(U32), 3: dealt_bytes[:, 9 * K : 13 * K].bitcast(U32)})
-        quantise_wb(2)
-        round_wb_dealt()
-        quantise_wb(3)
         weigh(2)
         products(3)
+        dealt_bytes = one("dealt_bytes", [P, 8 * K], U8, "behind2")
         dealt_weights = (dealt_bytes[:, 0 : 2 * K], dealt_bytes[:, 2 * K : 3 * K],
                          dealt_bytes[:, 4 * K : 8 * K].bitcast(U32), dealt_bytes[:, 3 * K : 4 * K])
         for dst, src in zip(dealt_weights, (wa_w[:, 2 * K : 2 * H], wa_s[:, K:H], wc_w[:, K:H], wc_s[:, K:H])):
             deal_columns(dst, src)
+        gate_and_sum(3)
 
         last = SLICES - 1
-        wd_bf = []
+        wd_w = []
+        wd_bf = [w_bf[:, 0 : 4 * N]]
         for s in range(1, last):
             place(s, slice(0, S))
+            fetch_inner(s - 1, slice(0, F), inner[s - 1])
             if s in (PER_PASS, PER_PASS + 1):
-                cols = half(s - PER_PASS)
-                nc.vector.quantize_mx(out=wd_w[:, cols].bitcast(FP8X4), scales=wd_s[:, cols], in_=wd_bf[s - PER_PASS][:])
-            fetch_inner(s - 1, slice(0, F))
-            if s + 2 < SLICES:
-                gate_and_sum(s + 2)
-            stiffen(s - 1)
-            if s + 2 < SLICES:
-                weigh(s + 2)
-            if s + 3 < SLICES:
-                products(s + 3)
-            if s - 1 < PER_PASS:
-                turn_rows(s - 1)
-            if s in (2, 3):
-                g = s - 2
-                wd_bf.append(one("wd_bf%d" % g, [P, 4 * N], BF16, "behind%d" % (s + 2)))
-                for c0 in range(0, N, P):
-                    interleave(wd_bf[g][:, 4 * c0 : 4 * (c0 + P)], wd_raw[:, g, :, c0 : c0 + P], nc.scalar.copy)
-            if s == PER_PASS + 1:
-                turn_back()
+                g = s - PER_PASS
+                wd_w.append(one("wd_w%d" % g, [P, N], U32, "behind%d" % s))
+                nc.vector.quantize_mx(out=wd_w[g][:].bitcast(FP8X4), scales=wd_s[:, half(g)], in_=wd_bf[g])
             for h in range(2 if s < last - 1 else 1):
                 fetch_outer(s, h, outer[s][:, half(h)])
+            nc.gpsimd.tensor_tensor(jump[s - 1], inner[s - 1], outer[s - 1], ADD)
+            if s + 2 < SLICES:
+                weigh(s + 2)
+            stiffen(s - 1)
+            if s + 3 < SLICES:
+                products(s + 3)
+                gate_and_sum(s + 3)
+            if s - 1 < PER_PASS:
+                turn_rows(s - 1)
+            if s == 1:
+                wd_bf.append(one("wd_bf", [P, 4 * N], BF16, "behind3")[:])
+            if s in (1, 2):
+                for c0 in range(0, N, P):
+                    interleave(wd_bf[s - 1][:, 4 * c0 : 4 * (c0 + P)], wd_raw[:, s - 1, :, c0 : c0 + P], nc.scalar.copy)
+            if s == PER_PASS + 1:
+                turn_back()
 
         slots = z_last[:].rearrange("p (m t) -> p m t", t=PER_PASS)
         for h in range(2):
             nc.scalar.copy(out=z_last[:].bitcast(F32).rearrange("p (m u) -> p m u", u=2)[:, half(h), 0],
                            in_=z_pair.bitcast(F32)[:, half(h)])
-        jump6, outer7 = work[0][:, S + QUARTER : S + QUARTER + HALF], work[0][:, S : 2 * S]
+        jump6, outer7 = ends[:, S + QUARTER : S + QUARTER + HALF], ends[:, S : 2 * S]
         outer6_late = z_words[:, 0:HALF]
-        stiff7, jump7 = late[:, 0:HALF], work[0][:, 0:HALF]
+        stiff7, jump7 = late[:, 0:HALF], ends[:, 0:HALF]
         late_jumps = {HALF: stiff7.rearrange("p (e m) -> p m e", e=2),
-                      HALF + QUARTER: work[0][:].rearrange("p (k m) -> p m k", m=QUARTER)[:, :, 0:7:6]}
+                      HALF + QUARTER: ends.rearrange("p (k m) -> p m k", m=QUARTER)[:, :, 0:7:6]}
         late_stiff = late[:, HALF : 3 * HALF].rearrange("p (e m) -> p m e", e=2)
-        place(last, half(0))
-        add_inner(last - 1, half(0), jump6, outer[last - 1][:, half(0)])
-        place(last, half(1))
+        fetch_inner(last - 1, half(0), inner[last - 1][:, half(0)])
+        place(last, slice(0, S))
+        nc.gpsimd.tensor_tensor(jump6, inner[last - 1][:, half(0)], outer[last - 1][:, half(0)], ADD)
         nc.gpsimd.tensor_tensor(slots[:, half(0), 2], jump6, stiff6, MULT)
         z_w.setdefault(0, one("z_w0", [P, F], U32, "behind6"))
         quantise_z(0, half(0), z_words[:].bitcast(BF16))

@@ -79,7 +79,7 @@ def tile_list_bone_face_features_kernel(
         wb_s = one("wb_s", [P, H], U8)
         wd_s = one("wd_s", [P, 2 * N], U8)
         wgs_sb = one("wgs_sb", [P, S], F32, "behind3")
-        wgs_dealt = [one("wgs_dealt%d" % t, [P, S], F32, "behind%d" % (t + PER_PASS) if t < 2 else "") for t in range(PER_PASS)]
+        wgs_dealt = [one("wgs_dealt%d" % t, [P, S], F32, "behind6w" if t == 2 else "") for t in range(PER_PASS)]
         pages = tiles("page", 2, [P, T2], F32)
         sum_ring = tiles("sum_ring", 3, [P, S], F32)
         outer_ring = tiles("outer_ring", 3, [P, F], F32)
@@ -281,60 +281,80 @@ def tile_list_bone_face_features_kernel(
             nc.vector.quantize_mx(out=z_w[g][:, cols].bitcast(FP8X4), scales=z_s[g][:, cols],
                                   in_=values[:, 4 * cols.start : 4 * cols.stop])
 
-        pieces = ((half(0), (bank_a[0], bank_a[1], bank_b[0], bank_b[1])),
-                  (slice(HALF, HALF + QUARTER), bank_c), (slice(HALF + QUARTER, F), bank_s))
+        pieces = [(half(0), (bank_a[0], bank_a[1], bank_b[0], bank_b[1]))]
+        pieces.extend((block(BLOCKS + k), out_banks)
+                      for k, out_banks in enumerate((bank_c[:1], bank_c[1:], bank_s[:1], (bank_s[1], bank_a[0]))))
 
         def last_products(g, cols, out_banks):
             width = cols.stop - cols.start
-            per_bank = HALF // width
+            per_bank = N // P // len(out_banks)
             for nb in range(N // P):
                 a = nb % per_bank
                 w_cols = slice(g * N + nb * P, g * N + (nb + 1) * P)
                 nc.tensor.matmul_mx(out=out_banks[nb // per_bank][:, a * width : (a + 1) * width],
-                                    lhsT=wd_w[g][:, block(nb)].bitcast(FP8X4), lhsT_scale=wd_s[:, w_cols],
+                                    lhsT=wd_w[:, w_cols].bitcast(FP8X4), lhsT_scale=wd_s[:, w_cols],
                                     rhs=z_w[g][:, cols].bitcast(FP8X4), rhs_scale=z_s[g][:, cols],
                                     start=g == 0 and a == 0, stop=g == 1 and a == per_bank - 1)
 
         def store(cols, out_banks, stages, copies):
-            per_bank = HALF // (cols.stop - cols.start)
+            per_bank = N // P // len(out_banks)
+            used = per_bank * (cols.stop - cols.start)
             for b, bank in enumerate(out_banks):
-                copies[b](out=stages[b], in_=bank[:])
+                copies[b](out=stages[b][:, 0:used], in_=bank[:, 0:used])
                 rows = out[b * per_bank * P : (b + 1) * per_bank * P, cols]
                 nc.sync.dma_start(out=rows.rearrange("(a p) m -> p a m", a=per_bank),
-                                  in_=stages[b].rearrange("p (a m) -> p a m", a=per_bank))
+                                  in_=stages[b][:, 0:used].rearrange("p (a m) -> p a m", a=per_bank))
 
         round_wb(0, nc.vector.tensor_copy)
         quantise_wb(0)
-        first = (slice(0, QUARTER), slice(QUARTER, HALF), half(1))
-        first_banks = ((bank_b[0][:, 0:QUARTER], bank_a[0][:, 0:QUARTER], bank_c[0][:, 0:QUARTER]),
-                       (bank_s[0][:, 0:QUARTER], bank_s[1][:, 0:QUARTER], bank_c[0][:, QUARTER:HALF]),
-                       (bank_b[1][:], bank_a[1][:], bank_c[1][:]))
-        first_gate = (put[1][:, first[0]], w_bf[:, 3 * HALF : 4 * HALF].bitcast(F32), put[1][:, first[2]])
-        first_put = (put[1][:, QUARTER:HALF], put[1][:, HALF : HALF + QUARTER], put[0][:, half(1)])
+        first = [slice(k * QUARTER, (k + 1) * QUARTER) for k in range(4)]
+        low, high = slice(0, QUARTER), slice(QUARTER, HALF)
+        first_banks = ((bank_b[0][:, low], bank_a[0][:, low], bank_c[0][:, low]),
+                       (bank_s[0][:, low], bank_s[1][:, low], bank_c[0][:, high]),
+                       (bank_b[1][:, low], bank_a[1][:, low], bank_c[1][:, low]),
+                       (bank_b[0][:, low], bank_a[0][:, low], bank_c[1][:, high]))
+        first_gate = (put[1][:, first[0]], w_bf[:, 3 * HALF : 4 * HALF].bitcast(F32), put[1][:, first[3]], put[1][:, first[2]])
+        first_put = (put[1][:, first[1]], put[1][:, first[2]], put[0][:, half(1)])
+        first_gated = [outer_ring[1][:, cols] for cols in first]
+        second_sum = gated[1][:, QUARTER : QUARTER + HALF]
+        first_sum = (outer_ring[2][:, first[0]], outer_ring[2][:, first[1]], second_sum[:, low], second_sum[:, high])
         for c0 in (P, 2 * P):
             nc.gpsimd.tensor_scalar(w_bf[:, 4 * c0 : 4 * (c0 + P)].rearrange("p (c t) -> p c t", t=4),
                                     wb_raw[1][:, :, c0 - P : c0].rearrange("p t c -> p c t"), 1.0, 0.0, MULT, ADD)
         for h in range(2):
             nc.vector.tensor_copy(v_s[h][:], tab_s[:].indirect(entries(idx1, half(h))))
-        for k, cols in enumerate(first):
+        for cols in first:
             h, c0 = divmod(cols.start, HALF)
-            here = slice(c0, c0 + cols.stop - cols.start)
-            nc.vector.tensor_copy(v_w[h][:, here], tab_w[:].indirect(entries(idx1, cols)))
+            nc.vector.tensor_copy(v_w[h][:, c0 : c0 + QUARTER], tab_w[:].indirect(entries(idx1, cols)))
+
+        def first_products(k):
+            h, c0 = divmod(first[k].start, HALF)
+            here = slice(c0, c0 + QUARTER)
             for acc, (codes, scales) in zip(first_banks[k], weights(0)):
                 nc.tensor.matmul_mx(out=acc, lhsT=codes, lhsT_scale=scales, rhs=v_w[h][:, here].bitcast(FP8X4),
                                     rhs_scale=v_s[h][:, here], start=True, stop=True)
             nc.scalar.activation(first_gate[k], first_banks[k][0], SIGMOID)
-        first_gated = [outer_ring[1][:, cols] for cols in first]
-        first_sum = (outer_ring[2][:, first[0]], outer_ring[2][:, first[1]], gated[1][:, QUARTER : QUARTER + HALF])
-        for k in range(2):
+
+        def first_gating(k):
             nc.vector.tensor_tensor(first_gated[k], first_banks[k][1], first_gate[k], MULT)
-        for k in range(2):
+
+        def first_summing(k):
             nc.vector.tensor_tensor(first_sum[k], first_banks[k][2], first_gated[k], ADD)
-        nc.vector.tensor_tensor(first_gated[2], first_banks[2][1], first_gate[2], MULT)
+
+        for k in range(3):
+            first_products(k)
+        first_gating(0)
+        first_products(3)
+        first_gating(1)
+        first_summing(0)
+        first_summing(1)
+        first_gating(2)
+        first_gating(3)
+        first_summing(2)
         quantise_wb(1)
-        nc.vector.tensor_tensor(first_sum[2], first_banks[2][2], first_gated[2], ADD)
-        for k, cols in enumerate(first):
-            nc.gpsimd.tensor_tensor(first_put[k], first_sum[k], wgs_sb[:, cols], MULT)
+        first_summing(3)
+        for values, cols, dst in zip((first_sum[0], first_sum[1], second_sum), (first[0], first[1], half(1)), first_put):
+            nc.gpsimd.tensor_tensor(dst, values, wgs_sb[:, cols], MULT)
         for h, values in enumerate((put[1][:, QUARTER : QUARTER + HALF], first_put[2])):
             nc.vector.tensor_copy(pages[0][:].indirect(entries(idx2, half(h))), values)
         products(1)
@@ -360,15 +380,14 @@ def tile_list_bone_face_features_kernel(
         gate_and_sum(3)
 
         last = SLICES - 1
-        wd_w = []
         wd_bf = [w_bf[:, 0 : 4 * N]]
         for s in range(1, last):
             place(s, slice(0, S))
+            if s == last - 1:
+                wd_w = one("wd_w", [P, 2 * N], U32, "behind6w")
+                for g in range(2):
+                    nc.vector.quantize_mx(out=wd_w[:, half(g)].bitcast(FP8X4), scales=wd_s[:, half(g)], in_=wd_bf[g])
             fetch_inner(s - 1, slice(0, F), inner[s - 1])
-            if s in (PER_PASS, PER_PASS + 1):
-                g = s - PER_PASS
-                wd_w.append(one("wd_w%d" % g, [P, N], U32, "behind%d" % s))
-                nc.vector.quantize_mx(out=wd_w[g][:].bitcast(FP8X4), scales=wd_s[:, half(g)], in_=wd_bf[g])
             for h in range(2 if s < last - 1 else 1):
                 fetch_outer(s, h, outer[s][:, half(h)])
             nc.gpsimd.tensor_tensor(jump[s - 1], inner[s - 1], outer[s - 1], ADD)
@@ -395,8 +414,9 @@ def tile_list_bone_face_features_kernel(
         jump6, outer7 = ends[:, S + QUARTER : S + QUARTER + HALF], ends[:, S : 2 * S]
         outer6_late = z_words[:, 0:HALF]
         stiff7, jump7 = late[:, 0:HALF], ends[:, 0:HALF]
-        late_jumps = {HALF: stiff7.rearrange("p (e m) -> p m e", e=2),
-                      HALF + QUARTER: ends.rearrange("p (k m) -> p m k", m=QUARTER)[:, :, 0:7:6]}
+        by_block = ends.rearrange("p (k m) -> p m k", m=P)
+        places = [(k % 2, 2 if k == 0 else (S + HALF) // P + k - 1) for k in range(BLOCKS)]
+        late_jumps = [by_block[:, :, a : b + 1 : b - a] for a, b in places]
         late_stiff = late[:, HALF : 3 * HALF].rearrange("p (e m) -> p m e", e=2)
         fetch_inner(last - 1, half(0), inner[last - 1][:, half(0)])
         place(last, slice(0, S))
@@ -409,19 +429,30 @@ def tile_list_bone_face_features_kernel(
         add_inner(last, half(0), jump7, outer7[:, half(0)])
         fetch_outer(last - 1, 1, outer6_late)
         fetch_outer(last, 1, outer7[:, half(1)])
-        for cols, out_banks in pieces:
+        for cols, out_banks in pieces[:-1]:
             last_products(0, cols, out_banks)
         nc.gpsimd.tensor_tensor(slots[:, half(0), 3], jump7, stiff7, MULT)
-        stages = [t[:, half(h)] for h in range(2) for t in staged]
-        at = 0
-        for cols, out_banks in pieces:
-            if cols.start >= HALF:
-                here = slice(cols.start - HALF, cols.stop - HALF)
-                add_inner(last - 1, cols, late_jumps[cols.start][:, :, 0], outer6_late[:, here])
-                add_inner(last, cols, late_jumps[cols.start][:, :, 1], outer7[:, cols])
-                nc.vector.tensor_tensor(slots[:, cols, 2:4], late_jumps[cols.start], late_stiff[:, here], MULT)
+        stages = [t[:, half(h)] for h in range(2) for t in staged] + [put[0][:, half(0)]]
+
+        def late_sum(e, k):
+            others = (outer6_late, outer7[:, half(1)])[e]
+            add_inner(last - 1 + e, pieces[k + 1][0], late_jumps[k][:, :, e], others[:, block(k)])
+
+        def finish(k, at, copies):
+            cols, out_banks = pieces[k]
             quantise_z(1, cols, z_last[:])
             last_products(1, cols, out_banks)
-            copies = [nc.scalar.copy] * len(out_banks) if cols.stop < F else [nc.scalar.copy, nc.vector.tensor_copy]
             store(cols, out_banks, stages[at : at + len(out_banks)], copies)
-            at = at + len(out_banks)
+
+        finish(0, 0, [nc.scalar.copy] * 4)
+        last_products(0, *pieces[-1])
+        late_sum(0, 0)
+        late_sum(1, 0)
+        late_sum(0, 1)
+        for k in range(BLOCKS):
+            nc.vector.tensor_tensor(slots[:, pieces[k + 1][0], 2:4], late_jumps[k], late_stiff[:, block(k)], MULT)
+            if k + 1 < BLOCKS:
+                late_sum(1, k + 1)
+            finish(k + 1, BLOCKS + k, [nc.scalar.copy, nc.vector.tensor_copy])
+            if k + 2 < BLOCKS:
+                late_sum(0, k + 2)

@@ -79,7 +79,7 @@ def tile_list_bone_face_features_kernel(
         wb_s = one("wb_s", [P, H], U8)
         wd_s = one("wd_s", [P, 2 * N], U8)
         wgs_sb = one("wgs_sb", [P, S], F32, "behind3")
-        wgs_dealt = [one("wgs_dealt%d" % t, [P, S], F32, "behind6w" if t == 2 else "") for t in range(PER_PASS)]
+        wgs_dealt = [one("wgs_dealt%d" % t, [P, S], F32, "") for t in range(PER_PASS)]
         pages = tiles("page", 2, [P, T2], F32)
         sum_ring = tiles("sum_ring", 3, [P, S], F32)
         outer_ring = tiles("outer_ring", 3, [P, F], F32)
@@ -104,13 +104,14 @@ def tile_list_bone_face_features_kernel(
         outer = [outer_ring[s % 3][:] for s in range(SLICES)]
         summed = {n: sum_ring[n % 3][:] for n in range(1, SLICES)}
         inner = [sum_ring[(s + 1) % 3][:] for s in range(SLICES)]
-        jump = [resp[(s + 3) % 2][:] for s in range(SLICES - 3)] + [stiff_sb[SLICES - 4]]
-        gated = {n: stiff_sb[n - PER_PASS] for n in range(PER_PASS, SLICES)}
-        gated.update({1: z_t[0].bitcast(F32), 2: w_bf[:, S : 3 * S].bitcast(F32), 3: z_t[1].bitcast(F32)})
+        jump = [z_t[1].bitcast(F32)] + [resp[(s + 3) % 2][:] for s in range(1, SLICES - 3)]
+        gated = {n: summed[n] for n in range(3, SLICES)}
+        gated.update({1: z_t[0].bitcast(F32), 2: w_bf[:, S : 3 * S].bitcast(F32)})
         put_of = [put[s % 2][:] for s in range(SLICES)]
         put_of[1] = wb_last[:, 0:S]
         split_sums = {1: (one("early_sum", [P, HALF], F32, "behind1")[:], summed[1][:, half(1)]),
-                      2: (gated[3][:, half(0)], summed[2][:, half(1)])}
+                      2: (jump[0][:, half(0)], summed[2][:, half(1)])}
+        early_inner = wb_flat[0]
         z_rows = one("z_rows", [P, F], BF16)
         staged = stiff_sb[0:4]
 
@@ -254,9 +255,9 @@ def tile_list_bone_face_features_kernel(
         def fetch_inner(s, cols, dst):
             nc.vector.tensor_copy(dst, pages[s % 2][:].indirect(entries(idx3, cols)))
 
-        def stiffen(s):
+        def stiffen(s, cols, values):
             dst = z_rows[:] if s < PER_PASS else z_pair.rearrange("p (m e) -> p m e", e=2)[:, :, s - PER_PASS]
-            nc.gpsimd.tensor_tensor(dst, jump[s], stiff_sb[s][:, :], MULT)
+            nc.gpsimd.tensor_tensor(dst[:, cols], values, stiff_sb[s][:, cols], MULT)
 
         def turn_rows(s):
             for h in range(2):
@@ -370,7 +371,6 @@ def tile_list_bone_face_features_kernel(
         quantise_wb(3)
         products(2)
         gate_and_sum(2)
-        weigh(2)
         products(3)
         dealt_bytes = one("dealt_bytes", [P, 8 * K], U8, "behind2")
         dealt_weights = (dealt_bytes[:, 0 : 2 * K], dealt_bytes[:, 2 * K : 3 * K],
@@ -378,22 +378,29 @@ def tile_list_bone_face_features_kernel(
         for dst, src in zip(dealt_weights, (wa_w[:, 2 * K : 2 * H], wa_s[:, K:H], wc_w[:, K:H], wc_s[:, K:H])):
             deal_columns(dst, src)
         gate_and_sum(3)
+        weigh(2)
 
         last = SLICES - 1
         wd_bf = [w_bf[:, 0 : 4 * N]]
         for s in range(1, last):
             place(s, slice(0, S))
-            if s == last - 1:
-                wd_w = one("wd_w", [P, 2 * N], U32, "behind6w")
-                for g in range(2):
-                    nc.vector.quantize_mx(out=wd_w[:, half(g)].bitcast(FP8X4), scales=wd_s[:, half(g)], in_=wd_bf[g])
-            fetch_inner(s - 1, slice(0, F), inner[s - 1])
+            if s < last - 1:
+                fetch_inner(s - 1, slice(0, F), inner[s - 1])
+            else:
+                fetch_inner(s - 1, half(1), inner[s - 1][:, half(1)])
             for h in range(2 if s < last - 1 else 1):
                 fetch_outer(s, h, outer[s][:, half(h)])
-            nc.gpsimd.tensor_tensor(jump[s - 1], inner[s - 1], outer[s - 1], ADD)
-            if s + 2 < SLICES:
+            if s == last - 2:
+                fetch_inner(s, half(0), early_inner)
+            if s < last - 1:
+                nc.gpsimd.tensor_tensor(jump[s - 1], inner[s - 1], outer[s - 1], ADD)
                 weigh(s + 2)
-            stiffen(s - 1)
+                stiffen(s - 1, slice(0, F), jump[s - 1])
+            else:
+                for h, values in enumerate((early_inner, inner[s - 1][:, half(1)])):
+                    part = stiff_sb[s - 2 + h][:, half(0)]
+                    nc.gpsimd.tensor_tensor(part, values, outer[s - 1][:, half(h)], ADD)
+                    stiffen(s - 1, half(h), part)
             if s + 3 < SLICES:
                 products(s + 3)
                 gate_and_sum(s + 3)
@@ -422,10 +429,18 @@ def tile_list_bone_face_features_kernel(
         place(last, slice(0, S))
         nc.gpsimd.tensor_tensor(jump6, inner[last - 1][:, half(0)], outer[last - 1][:, half(0)], ADD)
         nc.gpsimd.tensor_tensor(slots[:, half(0), 2], jump6, stiff6, MULT)
-        z_w.setdefault(0, one("z_w0", [P, F], U32, "behind6"))
+        end_codes = one("end_codes", [P, F + 2 * N], U32, "behind6")
+        z_w.setdefault(0, end_codes[:, 0:F])
+        wd_w = end_codes[:, F : F + 2 * N]
+
+        def quantise_wd(g):
+            nc.vector.quantize_mx(out=wd_w[:, half(g)].bitcast(FP8X4), scales=wd_s[:, half(g)], in_=wd_bf[g])
+
+        quantise_wd(0)
         quantise_z(0, half(0), z_words[:].bitcast(BF16))
         fetch_outer(last, 0, outer7[:, half(0)])
         quantise_z(0, half(1), z_words[:].bitcast(BF16))
+        quantise_wd(1)
         add_inner(last, half(0), jump7, outer7[:, half(0)])
         fetch_outer(last - 1, 1, outer6_late)
         fetch_outer(last, 1, outer7[:, half(1)])

@@ -24,7 +24,7 @@ QUARTER = 256
 BLOCKS = HALF // P
 SLICES = H // P
 PER_PASS = 4
-WB_CHUNKS = ((0, 128), (128, 384), (384, 512), (512, 1024))
+WB_CHUNKS = ((0, 256), (256, 512), (512, 1024))
 
 
 def tile_list_bone_face_features_kernel(
@@ -63,24 +63,26 @@ def tile_list_bone_face_features_kernel(
         ident = one("ident", [P, P], F32)
         ident_bf = one("ident_bf", [P, P], BF16)
         tab_w = one("tab_w", [P, T], U32, "table")
-        tab_s = one("tab_s", [P, T], U8)
+        tab_s = one("tab_s", [P, T], U8, "scales")
         v_w = tiles("v_w", 2, [P, HALF], U32)
-        v_s = tiles("v_s", 2, [P, HALF], U8)
+        picked_s = one("picked_s", [P, S], U8)
+        v_plane = one("v_plane", [P, S], U8)
+        v_s = [v_plane[:, half(h)] for h in range(2)]
         wa_w = one("wa_w", [P, 2 * H], U8)
         wc_w = one("wc_w", [P, H], U32)
         wa_s = one("wa_s", [P, H], U8)
         wc_s = one("wc_s", [P, H], U8)
         wb_last = one("wb_last", [P, 5 * HALF], F32)
-        wb_flat = [one("wb_raw%d" % i, [P, 4 * (c1 - c0)], F32)[:] for i, (c0, c1) in enumerate(WB_CHUNKS[:3])]
+        wb_flat = [one("wb_raw%d" % i, [P, 4 * (c1 - c0)], F32)[:] for i, (c0, c1) in enumerate(WB_CHUNKS[:2])]
         wb_flat.append(wb_last[:, HALF : 5 * HALF])
         wb_raw = [flat.rearrange("p (j c) -> p j c", j=4) for flat in wb_flat]
         w_bf = one("w_bf", [P, 4 * H], BF16)
-        wb_w = {i: one("wb_w%d" % i, [P, c1 - c0], U32) for i, (c0, c1) in enumerate(WB_CHUNKS) if i < 2}
+        wb_w = {i: one("wb_w%d" % i, [P, c1 - c0], U32) for i, (c0, c1) in enumerate(WB_CHUNKS) if i == 0}
         wb_s = one("wb_s", [P, H], U8)
         wd_s = one("wd_s", [P, 2 * N], U8)
         wgs_sb = one("wgs_sb", [P, S], F32, "behind3")
         wgs_dealt = [one("wgs_dealt%d" % t, [P, S], F32, "") for t in range(PER_PASS)]
-        pages = tiles("page", 2, [P, T2], F32)
+        pages = [one("page0", [P, T2], F32)]
         sum_ring = tiles("sum_ring", 3, [P, S], F32)
         outer_ring = tiles("outer_ring", 3, [P, F], F32)
         gate = one("gate", [P, S], F32)
@@ -111,7 +113,7 @@ def tile_list_bone_face_features_kernel(
         put_of[1] = wb_last[:, 0:S]
         split_sums = {1: (one("early_sum", [P, HALF], F32, "behind1")[:], summed[1][:, half(1)]),
                       2: (jump[0][:, half(0)], summed[2][:, half(1)])}
-        early_inner = wb_flat[0]
+        early_inner = wb_flat[0][:, half(0)]
         z_rows = one("z_rows", [P, F], BF16)
         staged = stiff_sb[0:4]
 
@@ -122,6 +124,7 @@ def tile_list_bone_face_features_kernel(
         nc.gpsimd.memset(tab_s[:, T // 2 : T].bitcast(I32), 0)
         nc.gpsimd.memset(wc_s[:].bitcast(I32), 0)
         nc.vector.memset(wa_s[:].bitcast(I32), 0)
+        nc.vector.memset(v_plane[:].bitcast(I32), 0)
         wb_rows = wb.rearrange("(p j) c -> p j c", j=4)
 
         def load_wb(i):
@@ -137,21 +140,24 @@ def tile_list_bone_face_features_kernel(
             nc.sync.dma_start(out=stiff_sb[s][:, :], in_=rows)
 
         nc.sync.dma_start(idx1[:], offs)
+        nc.sync.dma_start(out=tab_s[0:P:8, :].bitcast(I32), in_=tab_scales[0].bitcast(I32))
         load_wb(0)
-        load_scales(nc.sync, tab_s, tab_scales[0])
-        nc.sync.dma_start(idx2[:], offs2)
+        load_scales(nc.sync, wa_s, wa_scales[0])
         nc.sync.dma_start(out=tab_w[:].bitcast(I32), in_=tab_words[0].rearrange("p n t -> p (n t)").bitcast(I32))
         load_scales(nc.gpsimd, wc_s, wc_scales[0])
         wa_rows = wa_words[0].bitcast(I32)
         wc_rows = wc_words[0].rearrange("p n t -> p (n t)").bitcast(I32)
         nc.sync.dma_start(out=wa_w[:, 0:512].bitcast(I32), in_=wa_rows[:, 0:128])
-        load_scales(nc.sync, wa_s, wa_scales[0])
         nc.sync.dma_start(out=wc_w[:, 0:256].bitcast(I32), in_=wc_rows[:, 0:256])
-        load_wb(1)
+        nc.vector.tensor_copy(picked_s[:], tab_s[:].indirect(idx1[:]))
+        for q in range(4):
+            nc.scalar.dma_start(out=v_plane[32 * q : 32 * q + 4, :].bitcast(I32),
+                                in_=picked_s[32 * q : 32 * (q + 1) : 8, :].bitcast(I32))
+        nc.sync.dma_start(idx2[:], offs2)
         nc.sync.dma_start(out=wgs_sb[:, half(0)], in_=wgs[:, half(0)])
         nc.sync.dma_start(out=wgs_sb[:, half(1)], in_=wgs[:, half(1)])
+        load_wb(1)
         load_wb(2)
-        load_wb(3)
         nc.sync.dma_start(idx4[:], offs4)
         nc.sync.dma_start(out=wa_w[:, 512 : 2 * H].bitcast(I32), in_=wa_rows[:, 128 : H // 2])
         nc.sync.dma_start(out=wc_w[:, 256:H].bitcast(I32), in_=wc_rows[:, 256:H])
@@ -173,7 +179,6 @@ def tile_list_bone_face_features_kernel(
         make_identity(nc, ident[:])
         make_identity(nc, ident_bf[:])
         nc.vector.memset(pages[0][:], 0.0)
-        nc.gpsimd.memset(pages[1][:], 0.0)
 
         def interleave(dst, raw, copy):
             copy(out=dst.rearrange("p (c i t) -> p c t i", i=4, t=4), in_=raw.rearrange("p t (c i) -> p c t i", i=4))
@@ -184,7 +189,7 @@ def tile_list_bone_face_features_kernel(
                 interleave(w_bf[:, 4 * (c0 + a) : 4 * (c0 + a + P)], wb_raw[i][:, :, a : a + P], copy)
 
         def round_wb_dealt():
-            src = wb_raw[3].rearrange("p j (g t h i) -> p t g h j i", t=PER_PASS, h=2, i=4)
+            src = wb_raw[2].rearrange("p j (g t h i) -> p t g h j i", t=PER_PASS, h=2, i=4)
             for t in range(PER_PASS):
                 dst = w_bf[:, 4 * (K + t * P) : 4 * (K + (t + 1) * P)]
                 nc.scalar.copy(out=dst.rearrange("p (g h i j) -> p g h j i", h=2, i=4, j=4), in_=src[:, t])
@@ -314,16 +319,14 @@ def tile_list_bone_face_features_kernel(
                        (bank_s[0][:, low], bank_s[1][:, low], bank_c[0][:, high]),
                        (bank_b[1][:, low], bank_a[1][:, low], bank_c[1][:, low]),
                        (bank_b[0][:, low], bank_a[0][:, low], bank_c[1][:, high]))
-        first_gate = (put[1][:, first[0]], w_bf[:, 3 * HALF : 4 * HALF].bitcast(F32), put[1][:, first[3]], put[1][:, first[2]])
+        first_gate = (w_bf[:, 2 * HALF : 3 * HALF].bitcast(F32), w_bf[:, 3 * HALF : 4 * HALF].bitcast(F32),
+                      put[1][:, first[3]], put[1][:, first[2]])
         first_put = (put[1][:, first[1]], put[1][:, first[2]], put[0][:, half(1)])
         first_gated = [outer_ring[1][:, cols] for cols in first]
         second_sum = gated[1][:, QUARTER : QUARTER + HALF]
         first_sum = (outer_ring[2][:, first[0]], outer_ring[2][:, first[1]], second_sum[:, low], second_sum[:, high])
-        for c0 in (P, 2 * P):
-            nc.gpsimd.tensor_scalar(w_bf[:, 4 * c0 : 4 * (c0 + P)].rearrange("p (c t) -> p c t", t=4),
-                                    wb_raw[1][:, :, c0 - P : c0].rearrange("p t c -> p c t"), 1.0, 0.0, MULT, ADD)
-        for h in range(2):
-            nc.vector.tensor_copy(v_s[h][:], tab_s[:].indirect(entries(idx1, half(h))))
+        pages.append(one("page1", [P, T2], F32, "scales"))
+        nc.gpsimd.memset(pages[1][:], 0.0)
         for cols in first:
             h, c0 = divmod(cols.start, HALF)
             nc.vector.tensor_copy(v_w[h][:, c0 : c0 + QUARTER], tab_w[:].indirect(entries(idx1, cols)))
@@ -352,7 +355,6 @@ def tile_list_bone_face_features_kernel(
         first_gating(2)
         first_gating(3)
         first_summing(2)
-        quantise_wb(1)
         first_summing(3)
         for values, cols, dst in zip((first_sum[0], first_sum[1], second_sum), (first[0], first[1], half(1)), first_put):
             nc.gpsimd.tensor_tensor(dst, values, wgs_sb[:, cols], MULT)
@@ -360,15 +362,15 @@ def tile_list_bone_face_features_kernel(
             nc.vector.tensor_copy(pages[0][:].indirect(entries(idx2, half(h))), values)
         products(1)
         gate_and_sum(1)
-        round_wb(2, nc.scalar.copy)
+        round_wb(1, nc.scalar.copy)
         round_wb_dealt()
         weigh(1)
         for h in range(2):
             fetch_outer(0, h, outer[0][:, half(h)])
-        late_codes = one("late_codes", [P, P + K], U32, "behind1")
-        wb_w.update({2: late_codes[:, 0:P], 3: late_codes[:, P : P + K]})
+        late_codes = one("late_codes", [P, QUARTER + K], U32, "behind1")
+        wb_w.update({1: late_codes[:, 0:QUARTER], 2: late_codes[:, QUARTER : QUARTER + K]})
+        quantise_wb(1)
         quantise_wb(2)
-        quantise_wb(3)
         products(2)
         gate_and_sum(2)
         products(3)

@@ -63,9 +63,9 @@ def tile_list_bone_face_features_kernel(
         ident = one("ident", [P, P], F32)
         ident_bf = one("ident_bf", [P, P], BF16)
         tab_w = one("tab_w", [P, T], U32, "table")
-        tab_s = one("tab_s", [P, T], U8, "scales")
+        tab_s = one("tab_s", [P, T], U8)
         v_w = tiles("v_w", 2, [P, HALF], U32)
-        picked_s = one("picked_s", [P, S], U8)
+        picked_s = one("picked_s", [P, S], U8, "scales")
         v_plane = one("v_plane", [P, S], U8)
         v_s = [v_plane[:, half(h)] for h in range(2)]
         wa_w = one("wa_w", [P, 2 * H], U8)
@@ -131,9 +131,10 @@ def tile_list_bone_face_features_kernel(
             c0, c1 = WB_CHUNKS[i]
             nc.sync.dma_start(out=wb_raw[i], in_=wb_rows[:, :, c0:c1])
 
-        def load_scales(queue, plane, rows):
+        def load_scales(queue, plane, rows, cols):
             for q in range(4):
-                queue.dma_start(out=plane[32 * q : 32 * q + 4, :].bitcast(I32), in_=rows[4 * q : 4 * q + 4, :].bitcast(I32))
+                queue.dma_start(out=plane[32 * q : 32 * q + 4, cols].bitcast(I32),
+                                in_=rows[4 * q : 4 * q + 4, cols].bitcast(I32))
 
         def load_stiff(s):
             rows = stiff[block(s), :] if s < PER_PASS else dealt(stiff[K:H, :], s - PER_PASS)
@@ -142,9 +143,9 @@ def tile_list_bone_face_features_kernel(
         nc.sync.dma_start(idx1[:], offs)
         nc.sync.dma_start(out=tab_s[0:P:8, :].bitcast(I32), in_=tab_scales[0].bitcast(I32))
         load_wb(0)
-        load_scales(nc.sync, wa_s, wa_scales[0])
+        load_scales(nc.sync, wa_s, wa_scales[0], slice(0, QUARTER))
         nc.sync.dma_start(out=tab_w[:].bitcast(I32), in_=tab_words[0].rearrange("p n t -> p (n t)").bitcast(I32))
-        load_scales(nc.gpsimd, wc_s, wc_scales[0])
+        load_scales(nc.gpsimd, wc_s, wc_scales[0], slice(0, H))
         wa_rows = wa_words[0].bitcast(I32)
         wc_rows = wc_words[0].rearrange("p n t -> p (n t)").bitcast(I32)
         nc.sync.dma_start(out=wa_w[:, 0:512].bitcast(I32), in_=wa_rows[:, 0:128])
@@ -158,6 +159,7 @@ def tile_list_bone_face_features_kernel(
         nc.sync.dma_start(out=wgs_sb[:, half(1)], in_=wgs[:, half(1)])
         load_wb(1)
         load_wb(2)
+        load_scales(nc.sync, wa_s, wa_scales[0], slice(QUARTER, H))
         nc.sync.dma_start(idx4[:], offs4)
         nc.sync.dma_start(out=wa_w[:, 512 : 2 * H].bitcast(I32), in_=wa_rows[:, 128 : H // 2])
         nc.sync.dma_start(out=wc_w[:, 256:H].bitcast(I32), in_=wc_rows[:, 256:H])
@@ -200,8 +202,8 @@ def tile_list_bone_face_features_kernel(
                                   scales=wb_s[:, c0:c1], in_=w_bf[:, 4 * c0 : 4 * c1])
 
         def deal_columns(dst, src):
-            nc.scalar.copy(out=dst.bitcast(U32).rearrange("p (t g w) -> p t g w", t=PER_PASS, g=16),
-                           in_=src.bitcast(U32).rearrange("p (g t w) -> p t g w", t=PER_PASS, g=16))
+            nc.gpsimd.tensor_copy(out=dst.bitcast(U32).rearrange("p (t g w) -> p t g w", t=PER_PASS, g=16),
+                                  in_=src.bitcast(U32).rearrange("p (g t w) -> p t g w", t=PER_PASS, g=16))
 
         def weights(s):
             b = block(s % PER_PASS)

@@ -65,7 +65,7 @@ def tile_list_bone_face_features_kernel(
         tab_w = one("tab_w", [P, T], U32, "table")
         tab_s = one("tab_s", [P, T], U8)
         v_w = tiles("v_w", 2, [P, HALF], U32)
-        picked_s = one("picked_s", [P, S], U8, "scales")
+        picked_s = one("picked_s", [P, S], U8)
         v_plane = one("v_plane", [P, S], U8)
         v_s = [v_plane[:, half(h)] for h in range(2)]
         wa_w = one("wa_w", [P, 2 * H], U8)
@@ -76,8 +76,10 @@ def tile_list_bone_face_features_kernel(
         wb_flat = [one("wb_raw%d" % i, [P, 4 * (c1 - c0)], F32)[:] for i, (c0, c1) in enumerate(WB_CHUNKS[:2])]
         wb_flat.append(wb_last[:, HALF : 5 * HALF])
         wb_raw = [flat.rearrange("p (j c) -> p j c", j=4) for flat in wb_flat]
-        w_bf = one("w_bf", [P, 4 * H], BF16)
+        w_bf = one("w_bf", [P, 4 * K], BF16)
+        dealt_bf = one("dealt_bf", [P, 4 * K], BF16, "dealt")
         wb_w = {i: one("wb_w%d" % i, [P, c1 - c0], U32) for i, (c0, c1) in enumerate(WB_CHUNKS) if i == 0}
+        first_bf = one("first_bf", [P, 4 * QUARTER], BF16, "scales")
         wb_s = one("wb_s", [P, H], U8)
         wd_s = one("wd_s", [P, 2 * N], U8)
         wgs_sb = one("wgs_sb", [P, S], F32, "behind3")
@@ -90,7 +92,7 @@ def tile_list_bone_face_features_kernel(
         plain = one("plain", [P, S], F32)
         put = tiles("put", 2, [P, S], F32)
         gate_of = {n: gate[:] for n in range(1, SLICES)}
-        gate_of.update({2: one("second_gate", [P, S], F32, "behind2")[:]})
+        gate_of.update({2: one("second_gate", [P, S], F32)[:]})
         ends = one("ends", [P, 2 * S], F32)[:]
         stiff_sb = [t[:] for t in tiles("stiff_sb", SLICES - 3, [P, F], F32)] + [ends[:, S : 2 * S]]
         z_ends = one("z_t", [P, 2 * BLOCKS * HALF], BF16)
@@ -108,10 +110,11 @@ def tile_list_bone_face_features_kernel(
         inner = [sum_ring[(s + 1) % 3][:] for s in range(SLICES)]
         jump = [z_t[1].bitcast(F32)] + [resp[(s + 3) % 2][:] for s in range(1, SLICES - 3)]
         gated = {n: summed[n] for n in range(3, SLICES)}
-        gated.update({1: z_t[0].bitcast(F32), 2: w_bf[:, S : 3 * S].bitcast(F32)})
+        gated.update({1: z_t[0].bitcast(F32), 2: w_bf[:].bitcast(F32)})
+        outer[0], inner[0] = z_words[:, 0:S], z_words[:, S : 2 * S]
         put_of = [put[s % 2][:] for s in range(SLICES)]
         put_of[1] = wb_last[:, 0:S]
-        split_sums = {1: (one("early_sum", [P, HALF], F32, "behind1")[:], summed[1][:, half(1)]),
+        split_sums = {1: (one("early_sum", [P, HALF], F32, "behind1")[:], z_words[:, S - QUARTER : S + QUARTER]),
                       2: (jump[0][:, half(0)], summed[2][:, half(1)])}
         early_inner = wb_flat[0][:, half(0)]
         z_rows = one("z_rows", [P, F], BF16)
@@ -143,13 +146,13 @@ def tile_list_bone_face_features_kernel(
         nc.sync.dma_start(idx1[:], offs)
         nc.sync.dma_start(out=tab_s[0:P:8, :].bitcast(I32), in_=tab_scales[0].bitcast(I32))
         load_wb(0)
-        load_scales(nc.sync, wa_s, wa_scales[0], slice(0, QUARTER))
+        load_scales(nc.sync, wa_s, wa_scales[0], slice(0, K))
         nc.sync.dma_start(out=tab_w[:].bitcast(I32), in_=tab_words[0].rearrange("p n t -> p (n t)").bitcast(I32))
         load_scales(nc.gpsimd, wc_s, wc_scales[0], slice(0, H))
         wa_rows = wa_words[0].bitcast(I32)
         wc_rows = wc_words[0].rearrange("p n t -> p (n t)").bitcast(I32)
-        nc.sync.dma_start(out=wa_w[:, 0:512].bitcast(I32), in_=wa_rows[:, 0:128])
-        nc.sync.dma_start(out=wc_w[:, 0:256].bitcast(I32), in_=wc_rows[:, 0:256])
+        nc.sync.dma_start(out=wa_w[:, 0 : 2 * K].bitcast(I32), in_=wa_rows[:, 0 : K // 2])
+        nc.sync.dma_start(out=wc_w[:, 0:K].bitcast(I32), in_=wc_rows[:, 0:K])
         nc.vector.tensor_copy(picked_s[:], tab_s[:].indirect(idx1[:]))
         for q in range(4):
             nc.scalar.dma_start(out=v_plane[32 * q : 32 * q + 4, :].bitcast(I32),
@@ -159,10 +162,10 @@ def tile_list_bone_face_features_kernel(
         nc.sync.dma_start(out=wgs_sb[:, half(1)], in_=wgs[:, half(1)])
         load_wb(1)
         load_wb(2)
-        load_scales(nc.sync, wa_s, wa_scales[0], slice(QUARTER, H))
         nc.sync.dma_start(idx4[:], offs4)
-        nc.sync.dma_start(out=wa_w[:, 512 : 2 * H].bitcast(I32), in_=wa_rows[:, 128 : H // 2])
-        nc.sync.dma_start(out=wc_w[:, 256:H].bitcast(I32), in_=wc_rows[:, 256:H])
+        nc.sync.dma_start(out=wa_w[:, 2 * K : 2 * H].bitcast(I32), in_=wa_rows[:, K // 2 : H // 2])
+        nc.sync.dma_start(out=wc_w[:, K:H].bitcast(I32), in_=wc_rows[:, K:H])
+        load_scales(nc.sync, wa_s, wa_scales[0], slice(K, H))
         nc.sync.dma_start(idx3[:], offs3)
         wd_raw = one("wd_raw", [P, 2, 4, N], F32, "table")
         for s in range(SLICES - 2):
@@ -193,13 +196,13 @@ def tile_list_bone_face_features_kernel(
         def round_wb_dealt():
             src = wb_raw[2].rearrange("p j (g t h i) -> p t g h j i", t=PER_PASS, h=2, i=4)
             for t in range(PER_PASS):
-                dst = w_bf[:, 4 * (K + t * P) : 4 * (K + (t + 1) * P)]
+                dst = dealt_bf[:, half(t)]
                 nc.scalar.copy(out=dst.rearrange("p (g h i j) -> p g h j i", h=2, i=4, j=4), in_=src[:, t])
 
         def quantise_wb(i):
             c0, c1 = WB_CHUNKS[i]
             nc.vector.quantize_mx(out=wb_w[i][:, :].bitcast(FP8X4),
-                                  scales=wb_s[:, c0:c1], in_=w_bf[:, 4 * c0 : 4 * c1])
+                                  scales=wb_s[:, c0:c1], in_=w_bf[:, 4 * c0 : 4 * c1] if c0 < K else dealt_bf[:])
 
         def deal_columns(dst, src):
             nc.gpsimd.tensor_copy(out=dst.bitcast(U32).rearrange("p (t g w) -> p t g w", t=PER_PASS, g=16),
@@ -232,6 +235,7 @@ def tile_list_bone_face_features_kernel(
                 nc.scalar.copy(plain[:, half(h)], bank_c[h][:])
 
         def gate_and_sum(n):
+            bank_s = bank_a if n == 1 else banks[6:8]
             for h in range(2):
                 for i in range(BLOCKS):
                     turn(bank_s[h][:, block(i)], plain[:, block(BLOCKS * h + i)], i == 0, False)
@@ -313,8 +317,9 @@ def tile_list_bone_face_features_kernel(
                 nc.sync.dma_start(out=rows.rearrange("(a p) m -> p a m", a=per_bank),
                                   in_=stages[b][:, 0:used].rearrange("p (a m) -> p a m", a=per_bank))
 
-        round_wb(0, nc.vector.tensor_copy)
-        quantise_wb(0)
+        for a in range(2):
+            interleave(first_bf[:, half(a)], wb_raw[0][:, :, block(a)], nc.vector.tensor_copy)
+        nc.vector.quantize_mx(out=wb_w[0][:].bitcast(FP8X4), scales=wb_s[:, 0:QUARTER], in_=first_bf[:])
         first = [slice(k * QUARTER, (k + 1) * QUARTER) for k in range(4)]
         low, high = slice(0, QUARTER), slice(QUARTER, HALF)
         first_banks = ((bank_b[0][:, low], bank_a[0][:, low], bank_c[0][:, low]),
@@ -322,7 +327,7 @@ def tile_list_bone_face_features_kernel(
                        (bank_b[1][:, low], bank_a[1][:, low], bank_c[1][:, low]),
                        (bank_b[0][:, low], bank_a[0][:, low], bank_c[1][:, high]))
         first_gate = (w_bf[:, 2 * HALF : 3 * HALF].bitcast(F32), w_bf[:, 3 * HALF : 4 * HALF].bitcast(F32),
-                      put[1][:, first[3]], put[1][:, first[2]])
+                      put[1][:, first[2]], put[1][:, first[3]])
         first_put = (put[1][:, first[1]], put[1][:, first[2]], put[0][:, half(1)])
         first_gated = [outer_ring[1][:, cols] for cols in first]
         second_sum = gated[1][:, QUARTER : QUARTER + HALF]
@@ -351,10 +356,10 @@ def tile_list_bone_face_features_kernel(
             first_products(k)
         first_gating(0)
         first_products(3)
-        first_gating(1)
         first_summing(0)
-        first_summing(1)
+        first_gating(1)
         first_gating(2)
+        first_summing(1)
         first_gating(3)
         first_summing(2)
         first_summing(3)
@@ -367,16 +372,16 @@ def tile_list_bone_face_features_kernel(
         round_wb(1, nc.scalar.copy)
         round_wb_dealt()
         weigh(1)
-        for h in range(2):
-            fetch_outer(0, h, outer[0][:, half(h)])
+        fetch_outer(0, 0, outer[0][:, half(0)])
         late_codes = one("late_codes", [P, QUARTER + K], U32, "behind1")
         wb_w.update({1: late_codes[:, 0:QUARTER], 2: late_codes[:, QUARTER : QUARTER + K]})
         quantise_wb(1)
         quantise_wb(2)
+        fetch_outer(0, 1, outer[0][:, half(1)])
         products(2)
         gate_and_sum(2)
         products(3)
-        dealt_bytes = one("dealt_bytes", [P, 8 * K], U8, "behind2")
+        dealt_bytes = one("dealt_bytes", [P, 8 * K], U8, "dealt")
         dealt_weights = (dealt_bytes[:, 0 : 2 * K], dealt_bytes[:, 2 * K : 3 * K],
                          dealt_bytes[:, 4 * K : 8 * K].bitcast(U32), dealt_bytes[:, 3 * K : 4 * K])
         for dst, src in zip(dealt_weights, (wa_w[:, 2 * K : 2 * H], wa_s[:, K:H], wc_w[:, K:H], wc_s[:, K:H])):

@@ -111,10 +111,9 @@ def tile_list_bone_face_features_kernel(
         jump = [z_t[1].bitcast(F32)] + [resp[(s + 3) % 2][:] for s in range(1, SLICES - 3)]
         gated = {n: summed[n] for n in range(3, SLICES)}
         gated.update({1: z_t[0].bitcast(F32), 2: w_bf[:].bitcast(F32)})
-        outer[0], inner[0] = z_words[:, 0:S], z_words[:, S : 2 * S]
         put_of = [put[s % 2][:] for s in range(SLICES)]
         put_of[1] = wb_last[:, 0:S]
-        split_sums = {1: (one("early_sum", [P, HALF], F32, "behind1")[:], z_words[:, S - QUARTER : S + QUARTER]),
+        split_sums = {1: (one("early_sum", [P, HALF], F32, "behind1")[:], summed[1][:, half(1)]),
                       2: (jump[0][:, half(0)], summed[2][:, half(1)])}
         early_inner = wb_flat[0][:, half(0)]
         z_rows = one("z_rows", [P, F], BF16)
@@ -239,7 +238,7 @@ def tile_list_bone_face_features_kernel(
             for h in range(2):
                 for i in range(BLOCKS):
                     turn(bank_s[h][:, block(i)], plain[:, block(BLOCKS * h + i)], i == 0, False)
-            for cols in (half(0), half(1)) if n == 1 else (slice(0, S),):
+            for cols in (half(0), half(1)) if n in split_sums else (slice(0, S),):
                 nc.gpsimd.tensor_tensor(gated[n][:, cols], resp[n % 2][:, cols], gate_of[n][:, cols], MULT)
             for h in range(2):
                 for i in range(BLOCKS):
@@ -372,14 +371,15 @@ def tile_list_bone_face_features_kernel(
         round_wb(1, nc.scalar.copy)
         round_wb_dealt()
         weigh(1)
-        fetch_outer(0, 0, outer[0][:, half(0)])
+        for h in range(2):
+            fetch_outer(0, h, outer[0][:, half(h)])
         late_codes = one("late_codes", [P, QUARTER + K], U32, "behind1")
         wb_w.update({1: late_codes[:, 0:QUARTER], 2: late_codes[:, QUARTER : QUARTER + K]})
         quantise_wb(1)
         quantise_wb(2)
-        fetch_outer(0, 1, outer[0][:, half(1)])
         products(2)
         gate_and_sum(2)
+        weigh(2)
         products(3)
         dealt_bytes = one("dealt_bytes", [P, 8 * K], U8, "dealt")
         dealt_weights = (dealt_bytes[:, 0 : 2 * K], dealt_bytes[:, 2 * K : 3 * K],
@@ -387,7 +387,6 @@ def tile_list_bone_face_features_kernel(
         for dst, src in zip(dealt_weights, (wa_w[:, 2 * K : 2 * H], wa_s[:, K:H], wc_w[:, K:H], wc_s[:, K:H])):
             deal_columns(dst, src)
         gate_and_sum(3)
-        weigh(2)
 
         last = SLICES - 1
         wd_bf = [w_bf[:, 0 : 4 * N]]

@@ -24,6 +24,7 @@ QUARTER = 256
 BLOCKS = HALF // P
 SLICES = H // P
 PER_PASS = 4
+LAST = SLICES - 1
 WB_CHUNKS = ((0, 256), (256, 512), (512, 1024))
 
 
@@ -46,9 +47,13 @@ def tile_list_bone_face_features_kernel(
         def block(i):
             return slice(i * P, (i + 1) * P)
 
+        def quarter(q):
+            return slice(q * QUARTER, (q + 1) * QUARTER)
+
         def half(h):
             return slice(h * HALF, (h + 1) * HALF)
 
+        whole = slice(0, S)
         idx1 = lists.tile([P, S // 16], U16, name="idx1")
         idx2 = lists.tile([P, S // 16], U16, name="idx2")
         idx3 = lists.tile([P, F // 16], U16, name="idx3")
@@ -58,76 +63,66 @@ def tile_list_bone_face_features_kernel(
             return idx[:, cols.start // 16 : cols.stop // 16]
 
         banks = [ps.tile([P, HALF], F32, name="bank%d" % i) for i in range(8)]
-        bank_a, bank_b, bank_c, bank_s = banks[0:2], banks[2:4], banks[4:6], banks[6:8]
+        bank_b, bank_a = (banks[0], banks[4]), (banks[2], banks[6])
+        bank_c, bank_s = (banks[1], banks[3]), (banks[5], banks[7])
 
-        ident = one("ident", [P, P], F32)
         ident_bf = one("ident_bf", [P, P], BF16)
         tab_w = one("tab_w", [P, T], U32, "table")
-        tab_s = one("tab_s", [P, T], U8)
+        tab_s = one("tab_s", [P, T], U8, "after_scale_gather")
+        picked_s = one("picked_s", [P, S], U8, "after_moves")
         v_w = tiles("v_w", 2, [P, HALF], U32)
-        picked_s = one("picked_s", [P, S], U8)
-        v_plane = one("v_plane", [P, S], U8)
-        v_s = [v_plane[:, half(h)] for h in range(2)]
-        wa_w = one("wa_w", [P, 2 * H], U8)
-        wc_w = one("wc_w", [P, H], U32)
-        wa_s = one("wa_s", [P, H], U8)
-        wc_s = one("wc_s", [P, H], U8)
+        v_s = one("v_s", [P, S], U8)
+        wa_w = [one("wa_w0", [P, 2 * K], U8), one("wa_w1", [P, 2 * K], U8)]
+        wc_w = tiles("wc_w", 2, [P, K], U32)
+        planes = one("planes", [P, 2 * H], U8)
+        wa_s, wc_s = planes[:, 0:H], planes[:, H : 2 * H]
         wb_last = one("wb_last", [P, 5 * HALF], F32)
-        wb_flat = [one("wb_raw%d" % i, [P, 4 * (c1 - c0)], F32)[:] for i, (c0, c1) in enumerate(WB_CHUNKS[:2])]
-        wb_flat.append(wb_last[:, HALF : 5 * HALF])
-        wb_raw = [flat.rearrange("p (j c) -> p j c", j=4) for flat in wb_flat]
-        w_bf = one("w_bf", [P, 4 * K], BF16)
-        dealt_bf = one("dealt_bf", [P, 4 * K], BF16, "dealt")
-        wb_w = {i: one("wb_w%d" % i, [P, c1 - c0], U32) for i, (c0, c1) in enumerate(WB_CHUNKS) if i == 0}
-        first_bf = one("first_bf", [P, 4 * QUARTER], BF16, "scales")
+        wb_raw = [one("wb_raw0", [P, 4, QUARTER], F32, "after_rounding")[:], one("wb_raw1", [P, 4, QUARTER], F32)[:]]
+        wb_raw.append(wb_last[:, HALF : 5 * HALF].rearrange("p (j c) -> p j c", j=4))
+        wb_w = [one("wb_w0", [P, QUARTER], U32)]
         wb_s = one("wb_s", [P, H], U8)
         wd_s = one("wd_s", [P, 2 * N], U8)
-        wgs_sb = one("wgs_sb", [P, S], F32, "behind3")
-        wgs_dealt = [one("wgs_dealt%d" % t, [P, S], F32, "") for t in range(PER_PASS)]
+        wgs_sb = one("wgs_sb", [P, S], F32, "after_weigh3")
+        wgs_dealt = tiles("wgs_dealt", PER_PASS, [P, S], F32)
         pages = [one("page0", [P, T2], F32)]
-        sum_ring = tiles("sum_ring", 3, [P, S], F32)
-        outer_ring = tiles("outer_ring", 3, [P, F], F32)
+        work = one("work", [P, 3 * S], F32)
+        ring = (work[:, S : 2 * S], work[:, 0:S])
+        put = (one("put0", [P, S], F32)[:], wb_last[:, whole])
+        inner0 = one("inner0", [P, F], F32)
+        wb_bf = [one("wb_bf0", [P, 4 * QUARTER], BF16, "after_scale_gather")[:], inner0[:, half(1)].bitcast(BF16)]
+        dealt_bf = ring[0].bitcast(BF16)
+        sum1 = one("sum1", [P, HALF], F32, "after_weigh1")
         gate = one("gate", [P, S], F32)
-        resp = tiles("resp", 2, [P, S], F32)
+        gate2 = one("gate2", [P, S], F32, "after_gate2")
+        resp = one("resp", [P, S], F32)
         plain = one("plain", [P, S], F32)
-        put = tiles("put", 2, [P, S], F32)
-        gate_of = {n: gate[:] for n in range(1, SLICES)}
-        gate_of.update({2: one("second_gate", [P, S], F32)[:]})
-        ends = one("ends", [P, 2 * S], F32)[:]
-        stiff_sb = [t[:] for t in tiles("stiff_sb", SLICES - 3, [P, F], F32)] + [ends[:, S : 2 * S]]
-        z_ends = one("z_t", [P, 2 * BLOCKS * HALF], BF16)
-        z_t = [z_ends[:, h * BLOCKS * HALF : (h + 1) * BLOCKS * HALF] for h in range(2)]
-        z_pair = gate[:].bitcast(BF16)
-        z_last = one("z_last", [P, 4 * F], BF16)
-        stiff6 = one("stiff6", [P, F], F32, "behind6")[:, half(0)]
-        late = one("late", [P, 3 * HALF], F32)
+        resp3 = one("resp3", [P, S], F32)
+        gated = one("gated", [P, S], F32)
+        first_plain = one("first_plain", [P, HALF], F32)
+        stiff_sb = tiles("stiff_sb", SLICES - 2, [P, F], F32)
+        outer = [one("outer0", [P, F], F32), work[:, 2 * S : 3 * S]] + stiff_sb[0 : SLICES - 3]
+        stiff6 = one("stiff6", [P, HALF], F32, "after_stiff6")
+        jump6 = one("jump6", [P, HALF], F32)
+        end7 = one("end7", [P, F], F32)
+        late_stiff = one("late_stiff", [P, 2, HALF], F32)
+        z_rows = gate[:, half(1)].bitcast(BF16)
+        z_t = tiles("z_t", 2, [P, BLOCKS * HALF], BF16)
         z_words = one("z_words", [P, 2 * F], F32)
+        z_pair = gate[:].bitcast(BF16).rearrange("p (m e) -> p m e", e=2)
+        z_last = one("z_last", [P, 4 * F], BF16)
         z_w = {1: one("z_w1", [P, F], U32)}
         z_s = tiles("z_s", 2, [P, F], U8)
-
-        outer = [outer_ring[s % 3][:] for s in range(SLICES)]
-        summed = {n: sum_ring[n % 3][:] for n in range(1, SLICES)}
-        inner = [sum_ring[(s + 1) % 3][:] for s in range(SLICES)]
-        jump = [z_t[1].bitcast(F32)] + [resp[(s + 3) % 2][:] for s in range(1, SLICES - 3)]
-        gated = {n: summed[n] for n in range(3, SLICES)}
-        gated.update({1: z_t[0].bitcast(F32), 2: w_bf[:].bitcast(F32)})
-        put_of = [put[s % 2][:] for s in range(SLICES)]
-        put_of[1] = wb_last[:, 0:S]
-        split_sums = {1: (one("early_sum", [P, HALF], F32, "behind1")[:], summed[1][:, half(1)]),
-                      2: (jump[0][:, half(0)], summed[2][:, half(1)])}
-        early_inner = wb_flat[0][:, half(0)]
-        z_rows = one("z_rows", [P, F], BF16)
-        staged = stiff_sb[0:4]
 
         def dealt(rows, t):
             return rows.rearrange("(g t i) c -> t g i c", t=PER_PASS, i=8)[t]
 
-        nc.vector.memset(tab_s[:, 0 : T // 2].bitcast(I32), 0)
-        nc.gpsimd.memset(tab_s[:, T // 2 : T].bitcast(I32), 0)
-        nc.gpsimd.memset(wc_s[:].bitcast(I32), 0)
-        nc.vector.memset(wa_s[:].bitcast(I32), 0)
-        nc.vector.memset(v_plane[:].bitcast(I32), 0)
+        nc.vector.memset(tab_s[:].bitcast(I32), 0)
+        nc.vector.memset(planes[:].bitcast(I32), 0)
+        nc.vector.memset(v_s[:].bitcast(I32), 0)
+        nc.vector.memset(pages[0][:], 0.0)
         wb_rows = wb.rearrange("(p j) c -> p j c", j=4)
+        wa_rows = wa_words[0].bitcast(I32)
+        wc_rows = wc_words[0].rearrange("p n t -> p (n t)").bitcast(I32)
 
         def load_wb(i):
             c0, c1 = WB_CHUNKS[i]
@@ -138,37 +133,36 @@ def tile_list_bone_face_features_kernel(
                 queue.dma_start(out=plane[32 * q : 32 * q + 4, cols].bitcast(I32),
                                 in_=rows[4 * q : 4 * q + 4, cols].bitcast(I32))
 
-        def load_stiff(s):
-            rows = stiff[block(s), :] if s < PER_PASS else dealt(stiff[K:H, :], s - PER_PASS)
-            nc.sync.dma_start(out=stiff_sb[s][:, :], in_=rows)
+        def load_packed(c0, c1):
+            g, first = divmod(c0, K)
+            nc.sync.dma_start(out=wa_w[g][:].bitcast(I32)[:, first // 2 : (first + c1 - c0) // 2], in_=wa_rows[:, c0 // 2 : c1 // 2])
+            nc.sync.dma_start(out=wc_w[g][:].bitcast(I32)[:, first : first + c1 - c0], in_=wc_rows[:, c0:c1])
 
         nc.sync.dma_start(idx1[:], offs)
         nc.sync.dma_start(out=tab_s[0:P:8, :].bitcast(I32), in_=tab_scales[0].bitcast(I32))
         load_wb(0)
-        load_scales(nc.sync, wa_s, wa_scales[0], slice(0, K))
+        load_scales(nc.sync, wa_s, wa_scales[0], half(0))
         nc.sync.dma_start(out=tab_w[:].bitcast(I32), in_=tab_words[0].rearrange("p n t -> p (n t)").bitcast(I32))
         load_scales(nc.gpsimd, wc_s, wc_scales[0], slice(0, H))
-        wa_rows = wa_words[0].bitcast(I32)
-        wc_rows = wc_words[0].rearrange("p n t -> p (n t)").bitcast(I32)
-        nc.sync.dma_start(out=wa_w[:, 0 : 2 * K].bitcast(I32), in_=wa_rows[:, 0 : K // 2])
-        nc.sync.dma_start(out=wc_w[:, 0:K].bitcast(I32), in_=wc_rows[:, 0:K])
+        load_packed(*WB_CHUNKS[0])
         nc.vector.tensor_copy(picked_s[:], tab_s[:].indirect(idx1[:]))
         for q in range(4):
-            nc.scalar.dma_start(out=v_plane[32 * q : 32 * q + 4, :].bitcast(I32),
+            nc.scalar.dma_start(out=v_s[32 * q : 32 * q + 4, :].bitcast(I32),
                                 in_=picked_s[32 * q : 32 * (q + 1) : 8, :].bitcast(I32))
         nc.sync.dma_start(idx2[:], offs2)
-        nc.sync.dma_start(out=wgs_sb[:, half(0)], in_=wgs[:, half(0)])
-        nc.sync.dma_start(out=wgs_sb[:, half(1)], in_=wgs[:, half(1)])
+        for h in range(2):
+            nc.sync.dma_start(out=wgs_sb[:, half(h)], in_=wgs[:, half(h)])
         load_wb(1)
         load_wb(2)
         nc.sync.dma_start(idx4[:], offs4)
-        nc.sync.dma_start(out=wa_w[:, 2 * K : 2 * H].bitcast(I32), in_=wa_rows[:, K // 2 : H // 2])
-        nc.sync.dma_start(out=wc_w[:, K:H].bitcast(I32), in_=wc_rows[:, K:H])
-        load_scales(nc.sync, wa_s, wa_scales[0], slice(K, H))
         nc.sync.dma_start(idx3[:], offs3)
+        load_packed(*WB_CHUNKS[1])
+        load_packed(*WB_CHUNKS[2])
+        load_scales(nc.sync, wa_s, wa_scales[0], half(1))
         wd_raw = one("wd_raw", [P, 2, 4, N], F32, "table")
         for s in range(SLICES - 2):
-            load_stiff(s)
+            rows = stiff[block(s), :] if s < PER_PASS else dealt(stiff[K:H, :], s - PER_PASS)
+            nc.sync.dma_start(out=stiff_sb[s][:], in_=rows)
             if s < PER_PASS:
                 for a in range(4):
                     nc.sync.dma_start(out=wgs_dealt[s][32 * a : 32 * (a + 1), :], in_=dealt(wgs, s))
@@ -177,109 +171,122 @@ def tile_list_bone_face_features_kernel(
             if s == 1:
                 for t in range(PER_PASS):
                     nc.sync.dma_start(out=wd_raw[:, 1, t], in_=dealt(wd[K:H, :], t))
-        for dst, t, h in ((stiff6, 2, 0), (late[:, HALF:S], 2, 1), (late[:, 0:HALF], 3, 0), (late[:, S : 3 * HALF], 3, 1)):
+        for dst, t, h in ((stiff6[:], 2, 0), (end7[:, half(1)], 3, 0), (late_stiff[:, 0], 2, 1), (late_stiff[:, 1], 3, 1)):
             nc.sync.dma_start(out=dst, in_=dealt(stiff[K:H, half(h)], t))
 
-        make_identity(nc, ident[:])
-        make_identity(nc, ident_bf[:])
-        nc.vector.memset(pages[0][:], 0.0)
 
         def interleave(dst, raw, copy):
             copy(out=dst.rearrange("p (c i t) -> p c t i", i=4, t=4), in_=raw.rearrange("p t (c i) -> p c t i", i=4))
 
-        def round_wb(i, copy):
-            c0, c1 = WB_CHUNKS[i]
-            for a in range(0, c1 - c0, P):
-                interleave(w_bf[:, 4 * (c0 + a) : 4 * (c0 + a + P)], wb_raw[i][:, :, a : a + P], copy)
-
-        def round_wb_dealt():
-            src = wb_raw[2].rearrange("p j (g t h i) -> p t g h j i", t=PER_PASS, h=2, i=4)
-            for t in range(PER_PASS):
-                dst = dealt_bf[:, half(t)]
-                nc.scalar.copy(out=dst.rearrange("p (g h i j) -> p g h j i", h=2, i=4, j=4), in_=src[:, t])
-
-        def quantise_wb(i):
-            c0, c1 = WB_CHUNKS[i]
-            nc.vector.quantize_mx(out=wb_w[i][:, :].bitcast(FP8X4),
-                                  scales=wb_s[:, c0:c1], in_=w_bf[:, 4 * c0 : 4 * c1] if c0 < K else dealt_bf[:])
-
-        def deal_columns(dst, src):
-            nc.gpsimd.tensor_copy(out=dst.bitcast(U32).rearrange("p (t g w) -> p t g w", t=PER_PASS, g=16),
-                                  in_=src.bitcast(U32).rearrange("p (g t w) -> p t g w", t=PER_PASS, g=16))
+        def quantise(codes, scales, values):
+            nc.vector.quantize_mx(out=codes.bitcast(FP8X4), scales=scales, in_=values)
 
         def weights(s):
             b = block(s % PER_PASS)
             wide = slice(2 * b.start, 2 * b.stop)
-            a_w, a_s, c_w, c_s = (wa_w, wa_s, wc_w, wc_s) if s < PER_PASS else dealt_weights
+            a_w, a_s, c_w, c_s = (wa_w[0], wa_s, wc_w[0], wc_s) if s < PER_PASS else dealt_weights
             i = max(k for k, (c0, c1) in enumerate(WB_CHUNKS) if c0 <= s * P)
             c0 = s * P - WB_CHUNKS[i][0]
             return ((wb_w[i][:, c0 : c0 + P].bitcast(FP8X4), wb_s[:, block(s)]),
                     (a_w[:, wide].bitcast(FP4X4), a_s[:, b]),
                     (c_w[:, b].bitcast(FP8X4), c_s[:, b]))
 
-        def turn(out_ap, in_ap, start=True, stop=True, by=ident):
-            nc.tensor.matmul(out_ap, in_ap, by[:], start=start, stop=stop, is_transpose=True)
+        def turn(out_ap, in_ap, start=True, stop=True, by=None):
+            nc.tensor.matmul(out_ap, in_ap, (ident if by is None else by)[:], start=start, stop=stop, is_transpose=True)
+
+        def gate_of(n):
+            return gate2 if n == 2 else gate
+
+        def resp_of(n):
+            return resp3 if n == 3 else resp
+
+        def product(bank, h, codes, scales):
+            for i in range(BLOCKS):
+                nc.tensor.matmul_mx(out=bank[:, block(i)], lhsT=v_w[h][:, block(i)].bitcast(FP8X4),
+                                    lhsT_scale=v_s[:, block(BLOCKS * h + i)], rhs=codes, rhs_scale=scales,
+                                    start=True, stop=True)
+
+        def sum_banks(n):
+            return (bank_b, bank_s)[n % 2]
+
+        def gate_banks(n):
+            return (bank_c[0], bank_b[1]) if n == 3 else (bank_b, bank_s)[(n - 1) % 2]
+
+        def open_sum(n, h):
+            for i in range(BLOCKS):
+                turn(sum_banks(n)[h][:, block(i)], plain[:, block(BLOCKS * h + i)], i == 0, False)
+
+        def gated_products(n, h):
+            w_b, w_a, w_c = weights(n)
+            product(gate_banks(n)[h], h, *w_b)
+            product(bank_a[h], h, *w_a)
+            nc.scalar.activation(gate_of(n)[:, half(h)], gate_banks(n)[h][:], SIGMOID)
+            nc.scalar.copy(resp_of(n)[:, half(h)], bank_a[h][:])
+
+        def plain_product(n, h):
+            product(bank_a[h], h, *weights(n)[2])
+            nc.scalar.copy(plain[:, half(h)], bank_a[h][:])
+            open_sum(n, h)
 
         def products(n):
-            for three, (codes, scales) in zip((bank_b, bank_a, bank_c), weights(n)):
-                for h in range(2):
-                    for i in range(BLOCKS):
-                        nc.tensor.matmul_mx(out=three[h][:, block(i)], lhsT=v_w[h][:, block(i)].bitcast(FP8X4),
-                                            lhsT_scale=v_s[h][:, block(i)], rhs=codes, rhs_scale=scales,
-                                            start=True, stop=True)
             for h in range(2):
-                nc.scalar.activation(gate_of[n][:, half(h)], bank_b[h][:], SIGMOID)
-                nc.scalar.copy(resp[n % 2][:, half(h)], bank_a[h][:])
+                gated_products(n, h)
             for h in range(2):
-                nc.scalar.copy(plain[:, half(h)], bank_c[h][:])
+                plain_product(n, h)
 
-        def gate_and_sum(n):
-            bank_s = bank_a if n == 1 else banks[6:8]
-            for h in range(2):
-                for i in range(BLOCKS):
-                    turn(bank_s[h][:, block(i)], plain[:, block(BLOCKS * h + i)], i == 0, False)
-            for cols in (half(0), half(1)) if n in split_sums else (slice(0, S),):
-                nc.gpsimd.tensor_tensor(gated[n][:, cols], resp[n % 2][:, cols], gate_of[n][:, cols], MULT)
-            for h in range(2):
-                for i in range(BLOCKS):
-                    turn(bank_s[h][:, block(i)], gated[n][:, block(BLOCKS * h + i)], False, i == BLOCKS - 1)
-                nc.scalar.copy(split_sums[n][h] if n in split_sums else summed[n][:, half(h)], bank_s[h][:])
+        def sum_of(n, cols):
+            return sum1[:] if (n, cols) == (1, half(1)) else ring[n % 2][:, cols]
 
-        def weigh(n):
+        def inner_of(s, cols):
+            return (inner0 if s == 0 else ring[(s + 1) % 2])[:, cols]
+
+        def sum_up(n, h, values):
+            for i in range(BLOCKS):
+                turn(sum_banks(n)[h][:, block(i)], values[:, block(i)], False, i == BLOCKS - 1)
+            nc.scalar.copy(sum_of(n, half(h)), sum_banks(n)[h][:])
+
+        def gating(n):
+            nc.gpsimd.tensor_tensor(gated[:], resp_of(n)[:], gate_of(n)[:], MULT)
+            for h in range(2):
+                sum_up(n, h, gated[:, half(h)])
+
+        def weigh(n, cols):
             factor = wgs_sb if n < PER_PASS else wgs_dealt[n - PER_PASS]
-            if n in split_sums:
-                for h in range(2):
-                    nc.gpsimd.tensor_tensor(put_of[n][:, half(h)], split_sums[n][h], factor[:, half(h)], MULT)
-            else:
-                nc.gpsimd.tensor_tensor(put_of[n], summed[n], factor[:], MULT)
+            nc.gpsimd.tensor_tensor(put[n % 2][:, cols], sum_of(n, cols), factor[:, cols], MULT)
 
         def place(s, cols):
-            nc.vector.tensor_copy(pages[s % 2][:].indirect(entries(idx2, cols)), put_of[s][:, cols])
+            nc.vector.tensor_copy(pages[s % 2][:].indirect(entries(idx2, cols)), put[s % 2][:, cols])
 
         def fetch_outer(s, h, dst):
             nc.vector.tensor_scalar(dst, pages[s % 2][:].indirect(entries(idx4, half(h))), -1.0, 1.0, MULT, ADD)
 
+        def fetch_inner(s, cols):
+            nc.vector.tensor_copy(inner_of(s, cols), pages[s % 2][:].indirect(entries(idx3, cols)))
+
         def add_inner(s, cols, dst, outer_part):
             nc.vector.tensor_tensor(dst, pages[s % 2][:].indirect(entries(idx3, cols)), outer_part, ADD)
 
-        def fetch_inner(s, cols, dst):
-            nc.vector.tensor_copy(dst, pages[s % 2][:].indirect(entries(idx3, cols)))
+        def jump_of(s):
+            return ([ring[0], wgs_sb] + wgs_dealt)[s]
 
-        def stiffen(s, cols, values):
-            dst = z_rows[:] if s < PER_PASS else z_pair.rearrange("p (m e) -> p m e", e=2)[:, :, s - PER_PASS]
-            nc.gpsimd.tensor_tensor(dst[:, cols], values, stiff_sb[s][:, cols], MULT)
+        def add_picks(s, cols):
+            nc.gpsimd.tensor_tensor(jump_of(s)[:, cols], inner_of(s, cols), outer[s][:, cols], ADD)
+
+        def stiffen(s):
+            dst = z_rows if s < PER_PASS else z_pair[:, :, s - PER_PASS]
+            nc.gpsimd.tensor_tensor(dst, jump_of(s)[:, whole], stiff_sb[s][:], MULT)
 
         def turn_rows(s):
             for h in range(2):
-                turned = bank_s[h][:].bitcast(BF16)
+                turned = bank_c[h][:].bitcast(BF16)
                 for i in range(BLOCKS):
                     turn(turned[:, block(i)], z_rows[:, block(BLOCKS * h + i)], by=ident_bf)
-                dst = z_t[h].bitcast(F32).rearrange("p (b u w) -> p b u w", b=BLOCKS, u=2)[:, :, :, 32 * s : 32 * (s + 1)]
-                nc.scalar.copy(out=dst, in_=bank_s[h][:, 0:QUARTER].rearrange("p (b q u) -> p b u q", b=BLOCKS, u=2))
+                dst = z_t[h][:].bitcast(F32).rearrange("p (b u w) -> p b u w", b=BLOCKS, u=2)[:, :, :, 32 * s : 32 * (s + 1)]
+                nc.scalar.copy(out=dst, in_=bank_c[h][:, 0:QUARTER].rearrange("p (b q u) -> p b u q", b=BLOCKS, u=2))
 
         def turn_back():
             for h in range(2):
-                words = z_t[h].bitcast(F32)
+                words = z_t[h][:].bitcast(F32)
                 for pair in range(2):
                     bank = (bank_a, bank_b)[h][pair]
                     for i in range(BLOCKS):
@@ -288,13 +295,154 @@ def tile_list_bone_face_features_kernel(
                     nc.scalar.copy(out=z_words[:, first : first + HALF].rearrange("p (b m u) -> p b m u", b=2, u=2),
                                    in_=bank[:].rearrange("p (b u m) -> p b m u", b=2, u=2))
 
-        def quantise_z(g, cols, values):
-            nc.vector.quantize_mx(out=z_w[g][:, cols].bitcast(FP8X4), scales=z_s[g][:, cols],
-                                  in_=values[:, 4 * cols.start : 4 * cols.stop])
+        for a in range(2):
+            interleave(wb_bf[0][:, half(a)], wb_raw[0][:, :, block(a)], nc.vector.tensor_copy)
+        quantise(wb_w[0][:], wb_s[:, quarter(0)], wb_bf[0])
+        ident = one("ident", [P, P], F32, "after_rounding")
+        make_identity(nc, ident[:])
+        nc.gpsimd.tensor_copy(out=ident_bf[:], in_=ident[:])
+        pages.append(one("page1", [P, T2], F32, "after_moves"))
+        nc.gpsimd.memset(pages[1][:], 0.0)
+        first_gate = [inner0[:, quarter(q)] for q in (2, 3, 0, 1)]
+        first_gated = (ring[0][:, quarter(0)], ring[0][:, quarter(1)], ring[0][:, quarter(2)], first_plain[:, quarter(0)])
+        first_sum = (ring[0][:, quarter(2)], ring[0][:, quarter(3)], gate[:, quarter(0)], put[1][:, quarter(0)])
+
+        first_acc = [[banks[b][:, quarter(0)] for b in three] for three in ((0, 1, 3), (2, 5, 7), (4, 1, 6), (4, 5, 6))]
+
+        def first_product(q, k):
+            codes, scales = weights(0)[k]
+            nc.tensor.matmul_mx(out=first_acc[q][k], lhsT=codes, lhsT_scale=scales,
+                                rhs=v_w[q // 2][:, quarter(q % 2)].bitcast(FP8X4), rhs_scale=v_s[:, quarter(q)],
+                                start=True, stop=True)
+
+        def first_gate_product(q):
+            nc.vector.tensor_copy(v_w[q // 2][:, quarter(q % 2)], tab_w[:].indirect(entries(idx1, quarter(q))))
+            first_product(q, 0)
+            nc.scalar.activation(first_gate[q], first_acc[q][0], SIGMOID)
+
+        def first_other_products(q):
+            first_product(q, 1)
+            first_product(q, 2)
+            if q >= 2:
+                nc.scalar.copy(first_plain[:, quarter(q - 2)], first_acc[q][2])
+
+        def first_gating(q):
+            nc.vector.tensor_tensor(first_gated[q], first_acc[q][1], first_gate[q], MULT)
+
+        def first_summing(q):
+            if q < 2:
+                nc.vector.tensor_tensor(first_sum[q], first_acc[q][2], first_gated[q], ADD)
+            else:
+                nc.gpsimd.tensor_tensor(first_sum[q], first_plain[:, quarter(q - 2)], first_gated[q], ADD)
+            nc.gpsimd.tensor_tensor(put[0][:, quarter(q)], first_sum[q], wgs_sb[:, quarter(q)], MULT)
+
+        gated1 = work[:, 7 * QUARTER : 9 * QUARTER]
+
+        def gate_half(n, h, dst):
+            nc.gpsimd.tensor_tensor(dst, resp_of(n)[:, half(h)], gate_of(n)[:, half(h)], MULT)
+            sum_up(n, h, dst)
+
+        for q in range(2):
+            first_gate_product(q)
+            first_other_products(q)
+        first_gate_product(2)
+        for q in range(2):
+            first_gating(q)
+        gated_products(1, 0)
+        first_other_products(2)
+        first_gate_product(3)
+        first_other_products(3)
+        for q in range(2):
+            first_summing(q)
+        gated_products(1, 1)
+        place(0, quarter(0))
+        first_gating(2)
+        nc.gpsimd.tensor_tensor(gated1, resp[:, half(0)], gate[:, half(0)], MULT)
+        first_summing(2)
+        place(0, quarter(1))
+        first_gating(3)
+        for h in range(2):
+            plain_product(1, h)
+        sum_up(1, 0, gated1)
+        first_summing(3)
+        for q in range(2, 4):
+            place(0, quarter(q))
+
+        gate_half(1, 1, first_plain[:])
+        for a in range(2):
+            interleave(wb_bf[1][:, half(a)], wb_raw[1][:, :, block(a)], nc.scalar.copy)
+        src = wb_raw[2].rearrange("p j (g t h i) -> p t g h j i", t=PER_PASS, h=2, i=4)
+        for t in range(PER_PASS):
+            nc.scalar.copy(out=dealt_bf[:, half(t)].rearrange("p (g h i j) -> p g h j i", h=2, i=4, j=4), in_=src[:, t])
+        for h in range(2):
+            weigh(1, half(h))
+        for h in range(2):
+            fetch_outer(0, h, outer[0][:, half(h)])
+        fetch_inner(0, half(0))
+        late_codes = one("late_codes", [P, 3 * QUARTER], U32, "after_weigh1")
+        wb_w.extend((late_codes[:, 0:QUARTER], late_codes[:, QUARTER : 3 * QUARTER]))
+        quantise(wb_w[1], wb_s[:, quarter(1)], wb_bf[1])
+        quantise(wb_w[2], wb_s[:, K:H], dealt_bf)
+        products(2)
+        for h in range(2):
+            gate_half(2, h, gated[:, half(h)])
+        dealt_bytes = one("dealt_bytes", [P, 8 * K], U8, "after_gate2")
+        dealt_weights = (dealt_bytes[:, 0 : 2 * K], dealt_bytes[:, 2 * K : 3 * K],
+                         dealt_bytes[:, 4 * K : 8 * K].bitcast(U32), dealt_bytes[:, 3 * K : 4 * K])
+        gated_products(3, 0)
+        nc.gpsimd.tensor_tensor(resp[:, half(1)], resp3[:, half(0)], gate[:, half(0)], MULT)
+        for h in range(2):
+            weigh(2, half(h))
+        gated_products(3, 1)
+        for h in range(2):
+            plain_product(3, h)
+        sum_up(3, 0, resp[:, half(1)])
+        for dst, src in zip(dealt_weights, (wa_w[1][:], wa_s[:, K:H], wc_w[1][:], wc_s[:, K:H])):
+            nc.scalar.copy(out=dst.bitcast(U32).rearrange("p (t g w) -> p t g w", t=PER_PASS, g=16),
+                           in_=src.bitcast(U32).rearrange("p (g t w) -> p t g w", t=PER_PASS, g=16))
+
+        for s in range(1, LAST):
+            place(s, whole)
+            fetch_inner(s - 1, half(1) if s == 1 else whole)
+            for h in range(2 if s < LAST - 1 else 1):
+                fetch_outer(s, h, outer[s][:, half(h)])
+            add_picks(s - 1, whole)
+            if s == 1:
+                gate_half(3, 1, inner0[:, half(1)])
+            elif s + 2 < SLICES:
+                gating(s + 2)
+            stiffen(s - 1)
+            if s + 2 < SLICES:
+                weigh(s + 2, whole)
+            if s - 1 < PER_PASS:
+                turn_rows(s - 1)
+            if s + 3 < SLICES:
+                products(s + 3)
+            if s == 2:
+                wd_bf = one("wd_bf", [P, 2 * 4 * N], BF16, "after_weigh3")
+                for g in range(2):
+                    for c0 in range(0, N, P):
+                        first = 4 * (g * N + c0)
+                        interleave(wd_bf[:, first : first + 4 * P], wd_raw[:, g, :, c0 : c0 + P], nc.scalar.copy)
+            if s == PER_PASS:
+                turn_back()
+
+        slots = z_last[:].rearrange("p (m t) -> p m t", t=PER_PASS)
+        for h in range(2):
+            nc.scalar.copy(out=z_last[:].bitcast(F32).rearrange("p (m u) -> p m u", u=2)[:, half(h), 0],
+                           in_=gate[:, half(h)])
+        fetch_inner(LAST - 1, half(0))
+        place(LAST, whole)
+        nc.gpsimd.tensor_tensor(jump6[:], ring[LAST % 2][:, half(0)], outer[LAST - 1][:, half(0)], ADD)
+        nc.gpsimd.tensor_tensor(slots[:, half(0), 2], jump6[:], stiff6[:], MULT)
+        end_codes = one("end_codes", [P, F + 2 * N], U32, "after_stiff6")
+        z_w.setdefault(0, end_codes[:, 0:F])
+        wd_w = end_codes[:, F : F + 2 * N]
 
         pieces = [(half(0), (bank_a[0], bank_a[1], bank_b[0], bank_b[1]))]
         pieces.extend((block(BLOCKS + k), out_banks)
                       for k, out_banks in enumerate((bank_c[:1], bank_c[1:], bank_s[:1], (bank_s[1], bank_a[0]))))
+        stages = [t[:, half(h)] for h in range(2) for t in stiff_sb[0:4]] + [put[0][:, half(0)]]
 
         def last_products(g, cols, out_banks):
             width = cols.stop - cols.start
@@ -307,173 +455,42 @@ def tile_list_bone_face_features_kernel(
                                     rhs=z_w[g][:, cols].bitcast(FP8X4), rhs_scale=z_s[g][:, cols],
                                     start=g == 0 and a == 0, stop=g == 1 and a == per_bank - 1)
 
-        def store(cols, out_banks, stages, copies):
+        def finish(k, at, copies):
+            cols, out_banks = pieces[k]
+            quantise(z_w[1][:, cols], z_s[1][:, cols], z_last[:, 4 * cols.start : 4 * cols.stop])
+            last_products(1, cols, out_banks)
             per_bank = N // P // len(out_banks)
             used = per_bank * (cols.stop - cols.start)
             for b, bank in enumerate(out_banks):
-                copies[b](out=stages[b][:, 0:used], in_=bank[:, 0:used])
+                stage = stages[at + b][:, 0:used]
+                copies[b](out=stage, in_=bank[:, 0:used])
                 rows = out[b * per_bank * P : (b + 1) * per_bank * P, cols]
                 nc.sync.dma_start(out=rows.rearrange("(a p) m -> p a m", a=per_bank),
-                                  in_=stages[b][:, 0:used].rearrange("p (a m) -> p a m", a=per_bank))
+                                  in_=stage.rearrange("p (a m) -> p a m", a=per_bank))
 
-        for a in range(2):
-            interleave(first_bf[:, half(a)], wb_raw[0][:, :, block(a)], nc.vector.tensor_copy)
-        nc.vector.quantize_mx(out=wb_w[0][:].bitcast(FP8X4), scales=wb_s[:, 0:QUARTER], in_=first_bf[:])
-        first = [slice(k * QUARTER, (k + 1) * QUARTER) for k in range(4)]
-        low, high = slice(0, QUARTER), slice(QUARTER, HALF)
-        first_banks = ((bank_b[0][:, low], bank_a[0][:, low], bank_c[0][:, low]),
-                       (bank_s[0][:, low], bank_s[1][:, low], bank_c[0][:, high]),
-                       (bank_b[1][:, low], bank_a[1][:, low], bank_c[1][:, low]),
-                       (bank_b[0][:, low], bank_a[0][:, low], bank_c[1][:, high]))
-        first_gate = (w_bf[:, 2 * HALF : 3 * HALF].bitcast(F32), w_bf[:, 3 * HALF : 4 * HALF].bitcast(F32),
-                      put[1][:, first[2]], put[1][:, first[3]])
-        first_put = (put[1][:, first[1]], put[1][:, first[2]], put[0][:, half(1)])
-        first_gated = [outer_ring[1][:, cols] for cols in first]
-        second_sum = gated[1][:, QUARTER : QUARTER + HALF]
-        first_sum = (outer_ring[2][:, first[0]], outer_ring[2][:, first[1]], second_sum[:, low], second_sum[:, high])
-        pages.append(one("page1", [P, T2], F32, "scales"))
-        nc.gpsimd.memset(pages[1][:], 0.0)
-        for cols in first:
-            h, c0 = divmod(cols.start, HALF)
-            nc.vector.tensor_copy(v_w[h][:, c0 : c0 + QUARTER], tab_w[:].indirect(entries(idx1, cols)))
-
-        def first_products(k):
-            h, c0 = divmod(first[k].start, HALF)
-            here = slice(c0, c0 + QUARTER)
-            for acc, (codes, scales) in zip(first_banks[k], weights(0)):
-                nc.tensor.matmul_mx(out=acc, lhsT=codes, lhsT_scale=scales, rhs=v_w[h][:, here].bitcast(FP8X4),
-                                    rhs_scale=v_s[h][:, here], start=True, stop=True)
-            nc.scalar.activation(first_gate[k], first_banks[k][0], SIGMOID)
-
-        def first_gating(k):
-            nc.vector.tensor_tensor(first_gated[k], first_banks[k][1], first_gate[k], MULT)
-
-        def first_summing(k):
-            nc.vector.tensor_tensor(first_sum[k], first_banks[k][2], first_gated[k], ADD)
-
-        for k in range(3):
-            first_products(k)
-        first_gating(0)
-        first_products(3)
-        first_summing(0)
-        first_gating(1)
-        first_gating(2)
-        first_summing(1)
-        first_gating(3)
-        first_summing(2)
-        first_summing(3)
-        for values, cols, dst in zip((first_sum[0], first_sum[1], second_sum), (first[0], first[1], half(1)), first_put):
-            nc.gpsimd.tensor_tensor(dst, values, wgs_sb[:, cols], MULT)
-        for h, values in enumerate((put[1][:, QUARTER : QUARTER + HALF], first_put[2])):
-            nc.vector.tensor_copy(pages[0][:].indirect(entries(idx2, half(h))), values)
-        products(1)
-        gate_and_sum(1)
-        round_wb(1, nc.scalar.copy)
-        round_wb_dealt()
-        weigh(1)
-        for h in range(2):
-            fetch_outer(0, h, outer[0][:, half(h)])
-        late_codes = one("late_codes", [P, QUARTER + K], U32, "behind1")
-        wb_w.update({1: late_codes[:, 0:QUARTER], 2: late_codes[:, QUARTER : QUARTER + K]})
-        quantise_wb(1)
-        quantise_wb(2)
-        products(2)
-        gate_and_sum(2)
-        weigh(2)
-        products(3)
-        dealt_bytes = one("dealt_bytes", [P, 8 * K], U8, "dealt")
-        dealt_weights = (dealt_bytes[:, 0 : 2 * K], dealt_bytes[:, 2 * K : 3 * K],
-                         dealt_bytes[:, 4 * K : 8 * K].bitcast(U32), dealt_bytes[:, 3 * K : 4 * K])
-        for dst, src in zip(dealt_weights, (wa_w[:, 2 * K : 2 * H], wa_s[:, K:H], wc_w[:, K:H], wc_s[:, K:H])):
-            deal_columns(dst, src)
-        gate_and_sum(3)
-
-        last = SLICES - 1
-        wd_bf = [w_bf[:, 0 : 4 * N]]
-        for s in range(1, last):
-            place(s, slice(0, S))
-            if s < last - 1:
-                fetch_inner(s - 1, slice(0, F), inner[s - 1])
-            else:
-                fetch_inner(s - 1, half(1), inner[s - 1][:, half(1)])
-            for h in range(2 if s < last - 1 else 1):
-                fetch_outer(s, h, outer[s][:, half(h)])
-            if s == last - 2:
-                fetch_inner(s, half(0), early_inner)
-            if s < last - 1:
-                nc.gpsimd.tensor_tensor(jump[s - 1], inner[s - 1], outer[s - 1], ADD)
-                weigh(s + 2)
-                stiffen(s - 1, slice(0, F), jump[s - 1])
-            else:
-                for h, values in enumerate((early_inner, inner[s - 1][:, half(1)])):
-                    part = stiff_sb[s - 2 + h][:, half(0)]
-                    nc.gpsimd.tensor_tensor(part, values, outer[s - 1][:, half(h)], ADD)
-                    stiffen(s - 1, half(h), part)
-            if s + 3 < SLICES:
-                products(s + 3)
-                gate_and_sum(s + 3)
-            if s - 1 < PER_PASS:
-                turn_rows(s - 1)
-            if s == 1:
-                wd_bf.append(one("wd_bf", [P, 4 * N], BF16, "behind3")[:])
-            if s in (1, 2):
-                for c0 in range(0, N, P):
-                    interleave(wd_bf[s - 1][:, 4 * c0 : 4 * (c0 + P)], wd_raw[:, s - 1, :, c0 : c0 + P], nc.scalar.copy)
-            if s == PER_PASS + 1:
-                turn_back()
-
-        slots = z_last[:].rearrange("p (m t) -> p m t", t=PER_PASS)
-        for h in range(2):
-            nc.scalar.copy(out=z_last[:].bitcast(F32).rearrange("p (m u) -> p m u", u=2)[:, half(h), 0],
-                           in_=z_pair.bitcast(F32)[:, half(h)])
-        jump6, outer7 = ends[:, S + QUARTER : S + QUARTER + HALF], ends[:, S : 2 * S]
-        outer6_late = z_words[:, 0:HALF]
-        stiff7, jump7 = late[:, 0:HALF], ends[:, 0:HALF]
-        by_block = ends.rearrange("p (k m) -> p m k", m=P)
-        places = [(k % 2, 2 if k == 0 else (S + HALF) // P + k - 1) for k in range(BLOCKS)]
-        late_jumps = [by_block[:, :, a : b + 1 : b - a] for a, b in places]
-        late_stiff = late[:, HALF : 3 * HALF].rearrange("p (e m) -> p m e", e=2)
-        fetch_inner(last - 1, half(0), inner[last - 1][:, half(0)])
-        place(last, slice(0, S))
-        nc.gpsimd.tensor_tensor(jump6, inner[last - 1][:, half(0)], outer[last - 1][:, half(0)], ADD)
-        nc.gpsimd.tensor_tensor(slots[:, half(0), 2], jump6, stiff6, MULT)
-        end_codes = one("end_codes", [P, F + 2 * N], U32, "behind6")
-        z_w.setdefault(0, end_codes[:, 0:F])
-        wd_w = end_codes[:, F : F + 2 * N]
-
-        def quantise_wd(g):
-            nc.vector.quantize_mx(out=wd_w[:, half(g)].bitcast(FP8X4), scales=wd_s[:, half(g)], in_=wd_bf[g])
-
-        quantise_wd(0)
-        quantise_z(0, half(0), z_words[:].bitcast(BF16))
-        fetch_outer(last, 0, outer7[:, half(0)])
-        quantise_z(0, half(1), z_words[:].bitcast(BF16))
-        quantise_wd(1)
-        add_inner(last, half(0), jump7, outer7[:, half(0)])
-        fetch_outer(last - 1, 1, outer6_late)
-        fetch_outer(last, 1, outer7[:, half(1)])
-        for cols, out_banks in pieces[:-1]:
-            last_products(0, cols, out_banks)
-        nc.gpsimd.tensor_tensor(slots[:, half(0), 3], jump7, stiff7, MULT)
-        stages = [t[:, half(h)] for h in range(2) for t in staged] + [put[0][:, half(0)]]
+        late_outer = (z_words[:, half(0)], z_words[:, half(1)])
+        late_jump = [end7[:, half(k % 2)][:, 0:QUARTER].rearrange("p (e m) -> p e m", e=2) for k in range(BLOCKS)]
 
         def late_sum(e, k):
-            others = (outer6_late, outer7[:, half(1)])[e]
-            add_inner(last - 1 + e, pieces[k + 1][0], late_jumps[k][:, :, e], others[:, block(k)])
+            add_inner(LAST - 1 + e, pieces[k + 1][0], late_jump[k][:, e], late_outer[e][:, block(k)])
 
-        def finish(k, at, copies):
-            cols, out_banks = pieces[k]
-            quantise_z(1, cols, z_last[:])
-            last_products(1, cols, out_banks)
-            store(cols, out_banks, stages[at : at + len(out_banks)], copies)
-
+        quantise(wd_w, wd_s[:], wd_bf[:])
+        fetch_outer(LAST, 0, jump6[:])
+        quantise(z_w[0], z_s[0][:], z_words[:].bitcast(BF16))
+        add_inner(LAST, half(0), end7[:, half(0)], jump6[:])
+        for e in range(2):
+            fetch_outer(LAST - 1 + e, 1, late_outer[e])
+        for cols, out_banks in pieces[:-1]:
+            last_products(0, cols, out_banks)
+        nc.gpsimd.tensor_tensor(slots[:, half(0), 3], end7[:, half(0)], end7[:, half(1)], MULT)
         finish(0, 0, [nc.scalar.copy] * 4)
         last_products(0, *pieces[-1])
         late_sum(0, 0)
         late_sum(1, 0)
         late_sum(0, 1)
         for k in range(BLOCKS):
-            nc.vector.tensor_tensor(slots[:, pieces[k + 1][0], 2:4], late_jumps[k], late_stiff[:, block(k)], MULT)
+            nc.vector.tensor_tensor(slots[:, pieces[k + 1][0], 2:4], late_jump[k].rearrange("p e m -> p m e"),
+                                    late_stiff[:, :, block(k)].rearrange("p e m -> p m e"), MULT)
             if k + 1 < BLOCKS:
                 late_sum(1, k + 1)
             finish(k + 1, BLOCKS + k, [nc.scalar.copy, nc.vector.tensor_copy])

@@ -76,9 +76,9 @@ def tile_list_bone_face_features_kernel(
         wc_w = tiles("wc_w", 2, [P, K], U32)
         planes = one("planes", [P, 2 * H], U8)
         wa_s, wc_s = planes[:, 0:H], planes[:, H : 2 * H]
-        wb_last = one("wb_last", [P, 5 * HALF], F32)
+        wb_last = one("wb_last", [P, 4 * HALF], F32, "after_weigh1")
         wb_raw = [one("wb_raw0", [P, 4, QUARTER], F32, "after_rounding")[:], one("wb_raw1", [P, 4, QUARTER], F32)[:]]
-        wb_raw.append(wb_last[:, HALF : 5 * HALF].rearrange("p (j c) -> p j c", j=4))
+        wb_raw.append(wb_last[:].rearrange("p (j c) -> p j c", j=4))
         wb_w = [one("wb_w0", [P, QUARTER], U32)]
         wb_s = one("wb_s", [P, H], U8)
         wd_s = one("wd_s", [P, 2 * N], U8)
@@ -87,11 +87,11 @@ def tile_list_bone_face_features_kernel(
         pages = [one("page0", [P, T2], F32)]
         work = one("work", [P, 3 * S], F32)
         ring = (work[:, S : 2 * S], work[:, 0:S])
-        put = (one("put0", [P, S], F32)[:], wb_last[:, whole])
+        put = tiles("put", 2, [P, S], F32)
         inner0 = one("inner0", [P, F], F32)
-        wb_bf = [one("wb_bf0", [P, 4 * QUARTER], BF16, "after_scale_gather")[:], inner0[:, half(1)].bitcast(BF16)]
-        dealt_bf = ring[0].bitcast(BF16)
-        sum1 = one("sum1", [P, HALF], F32, "after_weigh1")
+        outer0 = one("outer0", [P, F], F32)
+        wb_bf = [one("wb_bf0", [P, 4 * QUARTER], BF16, "after_scale_gather")[:], outer0[:, QUARTER : 3 * QUARTER].bitcast(BF16)]
+        dealt_bf = inner0[:].bitcast(BF16)
         gate = one("gate", [P, S], F32)
         gate2 = one("gate2", [P, S], F32, "after_gate2")
         resp = one("resp", [P, S], F32)
@@ -100,7 +100,7 @@ def tile_list_bone_face_features_kernel(
         gated = one("gated", [P, S], F32)
         first_plain = one("first_plain", [P, HALF], F32)
         stiff_sb = tiles("stiff_sb", SLICES - 2, [P, F], F32)
-        outer = [one("outer0", [P, F], F32), work[:, 2 * S : 3 * S]] + stiff_sb[0 : SLICES - 3]
+        outer = [outer0, work[:, 2 * S : 3 * S]] + stiff_sb[0 : SLICES - 3]
         stiff6 = one("stiff6", [P, HALF], F32, "after_stiff6")
         jump6 = one("jump6", [P, HALF], F32)
         end7 = one("end7", [P, F], F32)
@@ -139,16 +139,16 @@ def tile_list_bone_face_features_kernel(
             nc.sync.dma_start(out=wc_w[g][:].bitcast(I32)[:, first : first + c1 - c0], in_=wc_rows[:, c0:c1])
 
         nc.sync.dma_start(idx1[:], offs)
-        nc.sync.dma_start(out=tab_s[0:P:8, :].bitcast(I32), in_=tab_scales[0].bitcast(I32))
+        nc.sync.dma_start(out=tab_s[4:P:8, :].bitcast(I32), in_=tab_scales[0].bitcast(I32))
         load_wb(0)
         load_scales(nc.sync, wa_s, wa_scales[0], half(0))
         nc.sync.dma_start(out=tab_w[:].bitcast(I32), in_=tab_words[0].rearrange("p n t -> p (n t)").bitcast(I32))
-        load_scales(nc.gpsimd, wc_s, wc_scales[0], slice(0, H))
+        load_scales(nc.gpsimd, wc_s, wc_scales[0], half(0))
         load_packed(*WB_CHUNKS[0])
         nc.vector.tensor_copy(picked_s[:], tab_s[:].indirect(idx1[:]))
         for q in range(4):
             nc.scalar.dma_start(out=v_s[32 * q : 32 * q + 4, :].bitcast(I32),
-                                in_=picked_s[32 * q : 32 * (q + 1) : 8, :].bitcast(I32))
+                                in_=picked_s[32 * q + 4 : 32 * (q + 1) : 8, :].bitcast(I32))
         nc.sync.dma_start(idx2[:], offs2)
         for h in range(2):
             nc.sync.dma_start(out=wgs_sb[:, half(h)], in_=wgs[:, half(h)])
@@ -158,7 +158,8 @@ def tile_list_bone_face_features_kernel(
         nc.sync.dma_start(idx3[:], offs3)
         load_packed(*WB_CHUNKS[1])
         load_packed(*WB_CHUNKS[2])
-        load_scales(nc.sync, wa_s, wa_scales[0], half(1))
+        for plane, rows in ((wa_s, wa_scales[0]), (wc_s, wc_scales[0])):
+            load_scales(nc.sync, plane, rows, half(1))
         wd_raw = one("wd_raw", [P, 2, 4, N], F32, "table")
         for s in range(SLICES - 2):
             rows = stiff[block(s), :] if s < PER_PASS else dealt(stiff[K:H, :], s - PER_PASS)
@@ -235,7 +236,7 @@ def tile_list_bone_face_features_kernel(
                 plain_product(n, h)
 
         def sum_of(n, cols):
-            return sum1[:] if (n, cols) == (1, half(1)) else ring[n % 2][:, cols]
+            return wb_last[:, half(0)] if (n, cols) == (1, half(1)) else ring[n % 2][:, cols]
 
         def inner_of(s, cols):
             return (inner0 if s == 0 else ring[(s + 1) % 2])[:, cols]
@@ -250,12 +251,15 @@ def tile_list_bone_face_features_kernel(
             for h in range(2):
                 sum_up(n, h, gated[:, half(h)])
 
+        def put_of(n):
+            return gate if n == 1 else put[n % 2]
+
         def weigh(n, cols):
             factor = wgs_sb if n < PER_PASS else wgs_dealt[n - PER_PASS]
-            nc.gpsimd.tensor_tensor(put[n % 2][:, cols], sum_of(n, cols), factor[:, cols], MULT)
+            nc.gpsimd.tensor_tensor(put_of(n)[:, cols], sum_of(n, cols), factor[:, cols], MULT)
 
         def place(s, cols):
-            nc.vector.tensor_copy(pages[s % 2][:].indirect(entries(idx2, cols)), put[s % 2][:, cols])
+            nc.vector.tensor_copy(pages[s % 2][:].indirect(entries(idx2, cols)), put_of(s)[:, cols])
 
         def fetch_outer(s, h, dst):
             nc.vector.tensor_scalar(dst, pages[s % 2][:].indirect(entries(idx4, half(h))), -1.0, 1.0, MULT, ADD)
@@ -303,11 +307,11 @@ def tile_list_bone_face_features_kernel(
         nc.gpsimd.tensor_copy(out=ident_bf[:], in_=ident[:])
         pages.append(one("page1", [P, T2], F32, "after_moves"))
         nc.gpsimd.memset(pages[1][:], 0.0)
-        first_gate = [inner0[:, quarter(q)] for q in (2, 3, 0, 1)]
+        first_gate = (outer0[:, quarter(1)], outer0[:, quarter(2)], inner0[:, quarter(2)], inner0[:, quarter(3)])
         first_gated = (ring[0][:, quarter(0)], ring[0][:, quarter(1)], ring[0][:, quarter(2)], first_plain[:, quarter(0)])
-        first_sum = (ring[0][:, quarter(2)], ring[0][:, quarter(3)], gate[:, quarter(0)], put[1][:, quarter(0)])
+        first_sum = (ring[0][:, quarter(2)], ring[0][:, quarter(3)], gate[:, quarter(0)], gate[:, quarter(2)])
 
-        first_acc = [[banks[b][:, quarter(0)] for b in three] for three in ((0, 1, 3), (2, 5, 7), (4, 1, 6), (4, 5, 6))]
+        first_acc = [[banks[b][:, quarter(0)] for b in three] for three in ((0, 1, 3), (2, 5, 7), (4, 1, 6), (4, 3, 6))]
 
         def first_product(q, k):
             codes, scales = weights(0)[k]
@@ -334,7 +338,10 @@ def tile_list_bone_face_features_kernel(
                 nc.vector.tensor_tensor(first_sum[q], first_acc[q][2], first_gated[q], ADD)
             else:
                 nc.gpsimd.tensor_tensor(first_sum[q], first_plain[:, quarter(q - 2)], first_gated[q], ADD)
-            nc.gpsimd.tensor_tensor(put[0][:, quarter(q)], first_sum[q], wgs_sb[:, quarter(q)], MULT)
+
+        def first_weighing(q):
+            engine = nc.vector if q == 0 else nc.gpsimd
+            engine.tensor_tensor(put[0][:, quarter(q)], first_sum[q], wgs_sb[:, quarter(q)], MULT)
 
         gated1 = work[:, 7 * QUARTER : 9 * QUARTER]
 
@@ -351,38 +358,41 @@ def tile_list_bone_face_features_kernel(
         gated_products(1, 0)
         first_other_products(2)
         first_gate_product(3)
-        first_other_products(3)
         for q in range(2):
             first_summing(q)
-        gated_products(1, 1)
+        first_other_products(3)
+        for q in range(2):
+            first_weighing(q)
+        plain_product(1, 0)
         place(0, quarter(0))
         first_gating(2)
-        nc.gpsimd.tensor_tensor(gated1, resp[:, half(0)], gate[:, half(0)], MULT)
+        gate_half(1, 0, gated1)
         first_summing(2)
-        place(0, quarter(1))
-        first_gating(3)
-        for h in range(2):
-            plain_product(1, h)
-        sum_up(1, 0, gated1)
-        first_summing(3)
-        for q in range(2, 4):
-            place(0, quarter(q))
-
-        gate_half(1, 1, first_plain[:])
+        first_weighing(2)
         for a in range(2):
             interleave(wb_bf[1][:, half(a)], wb_raw[1][:, :, block(a)], nc.scalar.copy)
+        gated_products(1, 1)
+        plain_product(1, 1)
+        place(0, quarter(1))
+        first_gating(3)
+        weigh(1, half(0))
         src = wb_raw[2].rearrange("p j (g t h i) -> p t g h j i", t=PER_PASS, h=2, i=4)
         for t in range(PER_PASS):
             nc.scalar.copy(out=dealt_bf[:, half(t)].rearrange("p (g h i j) -> p g h j i", h=2, i=4, j=4), in_=src[:, t])
-        for h in range(2):
-            weigh(1, half(h))
-        for h in range(2):
-            fetch_outer(0, h, outer[0][:, half(h)])
-        fetch_inner(0, half(0))
+        gate_half(1, 1, ring[1][:, half(0)])
+        first_summing(3)
+        first_weighing(3)
+        weigh(1, half(1))
+        place(0, quarter(2))
+        place(1, half(0))
+        place(0, quarter(3))
         late_codes = one("late_codes", [P, 3 * QUARTER], U32, "after_weigh1")
         wb_w.extend((late_codes[:, 0:QUARTER], late_codes[:, QUARTER : 3 * QUARTER]))
         quantise(wb_w[1], wb_s[:, quarter(1)], wb_bf[1])
         quantise(wb_w[2], wb_s[:, K:H], dealt_bf)
+        place(1, half(1))
+        for h in range(2):
+            fetch_outer(0, h, outer[0][:, half(h)])
         products(2)
         for h in range(2):
             gate_half(2, h, gated[:, half(h)])
@@ -402,8 +412,9 @@ def tile_list_bone_face_features_kernel(
                            in_=src.bitcast(U32).rearrange("p (g t w) -> p t g w", t=PER_PASS, g=16))
 
         for s in range(1, LAST):
-            place(s, whole)
-            fetch_inner(s - 1, half(1) if s == 1 else whole)
+            if s > 1:
+                place(s, whole)
+            fetch_inner(s - 1, whole)
             for h in range(2 if s < LAST - 1 else 1):
                 fetch_outer(s, h, outer[s][:, half(h)])
             add_picks(s - 1, whole)

@@ -16,6 +16,7 @@ FP8X4 = mybir.dt.float8_e4m3fn_x4
 FP4X4 = mybir.dt.float4_e2m1fn_x4
 MULT = mybir.AluOpType.mult
 ADD = mybir.AluOpType.add
+COPY = mybir.ActivationFunctionType.Copy
 SIGMOID = mybir.ActivationFunctionType.Sigmoid
 
 P = 128
@@ -63,8 +64,8 @@ def tile_list_bone_face_features_kernel(
             return idx[:, cols.start // 16 : cols.stop // 16]
 
         banks = [ps.tile([P, HALF], F32, name="bank%d" % i) for i in range(8)]
-        bank_b, bank_a = (banks[0], banks[4]), (banks[2], banks[6])
-        bank_c, bank_s = (banks[1], banks[3]), (banks[5], banks[7])
+        bank_b, bank_a = (banks[1], banks[2]), (banks[5], banks[6])
+        bank_c, bank_s = (banks[3], banks[4]), (banks[7], banks[0])
 
         ident_bf = one("ident_bf", [P, P], BF16)
         tab_w = one("tab_w", [P, T], U32, "table")
@@ -96,9 +97,8 @@ def tile_list_bone_face_features_kernel(
         gate2 = one("gate2", [P, S], F32, "after_gate2")
         resp = one("resp", [P, S], F32)
         plain = one("plain", [P, S], F32)
-        resp3 = one("resp3", [P, S], F32)
+        resp_odd = one("resp_odd", [P, S], F32)
         gated = one("gated", [P, S], F32)
-        first_plain = one("first_plain", [P, HALF], F32)
         stiff_sb = tiles("stiff_sb", SLICES - 2, [P, F], F32)
         outer = [outer0, work[:, 2 * S : 3 * S]] + stiff_sb[0 : SLICES - 3]
         stiff6 = one("stiff6", [P, HALF], F32, "after_stiff6")
@@ -139,16 +139,16 @@ def tile_list_bone_face_features_kernel(
             nc.sync.dma_start(out=wc_w[g][:].bitcast(I32)[:, first : first + c1 - c0], in_=wc_rows[:, c0:c1])
 
         nc.sync.dma_start(idx1[:], offs)
-        nc.sync.dma_start(out=tab_s[4:P:8, :].bitcast(I32), in_=tab_scales[0].bitcast(I32))
+        nc.sync.dma_start(out=tab_s[0:P:8, :].bitcast(I32), in_=tab_scales[0].bitcast(I32))
         load_wb(0)
         load_scales(nc.sync, wa_s, wa_scales[0], half(0))
         nc.sync.dma_start(out=tab_w[:].bitcast(I32), in_=tab_words[0].rearrange("p n t -> p (n t)").bitcast(I32))
-        load_scales(nc.gpsimd, wc_s, wc_scales[0], half(0))
+        load_scales(nc.gpsimd, wc_s, wc_scales[0], slice(0, H))
         load_packed(*WB_CHUNKS[0])
         nc.vector.tensor_copy(picked_s[:], tab_s[:].indirect(idx1[:]))
         for q in range(4):
             nc.scalar.dma_start(out=v_s[32 * q : 32 * q + 4, :].bitcast(I32),
-                                in_=picked_s[32 * q + 4 : 32 * (q + 1) : 8, :].bitcast(I32))
+                                in_=picked_s[32 * q : 32 * (q + 1) : 8, :].bitcast(I32))
         nc.sync.dma_start(idx2[:], offs2)
         for h in range(2):
             nc.sync.dma_start(out=wgs_sb[:, half(h)], in_=wgs[:, half(h)])
@@ -158,8 +158,7 @@ def tile_list_bone_face_features_kernel(
         nc.sync.dma_start(idx3[:], offs3)
         load_packed(*WB_CHUNKS[1])
         load_packed(*WB_CHUNKS[2])
-        for plane, rows in ((wa_s, wa_scales[0]), (wc_s, wc_scales[0])):
-            load_scales(nc.sync, plane, rows, half(1))
+        load_scales(nc.sync, wa_s, wa_scales[0], half(1))
         wd_raw = one("wd_raw", [P, 2, 4, N], F32, "table")
         for s in range(SLICES - 2):
             rows = stiff[block(s), :] if s < PER_PASS else dealt(stiff[K:H, :], s - PER_PASS)
@@ -199,7 +198,7 @@ def tile_list_bone_face_features_kernel(
             return gate2 if n == 2 else gate
 
         def resp_of(n):
-            return resp3 if n == 3 else resp
+            return resp if n == 1 else (resp, resp_odd)[n % 2]
 
         def product(bank, h, codes, scales):
             for i in range(BLOCKS):
@@ -251,15 +250,12 @@ def tile_list_bone_face_features_kernel(
             for h in range(2):
                 sum_up(n, h, gated[:, half(h)])
 
-        def put_of(n):
-            return gate if n == 1 else put[n % 2]
-
         def weigh(n, cols):
             factor = wgs_sb if n < PER_PASS else wgs_dealt[n - PER_PASS]
-            nc.gpsimd.tensor_tensor(put_of(n)[:, cols], sum_of(n, cols), factor[:, cols], MULT)
+            nc.gpsimd.tensor_tensor(put[n % 2][:, cols], sum_of(n, cols), factor[:, cols], MULT)
 
         def place(s, cols):
-            nc.vector.tensor_copy(pages[s % 2][:].indirect(entries(idx2, cols)), put_of(s)[:, cols])
+            nc.vector.tensor_copy(pages[s % 2][:].indirect(entries(idx2, cols)), put[s % 2][:, cols])
 
         def fetch_outer(s, h, dst):
             nc.vector.tensor_scalar(dst, pages[s % 2][:].indirect(entries(idx4, half(h))), -1.0, 1.0, MULT, ADD)
@@ -274,7 +270,7 @@ def tile_list_bone_face_features_kernel(
             return ([ring[0], wgs_sb] + wgs_dealt)[s]
 
         def add_picks(s, cols):
-            nc.gpsimd.tensor_tensor(jump_of(s)[:, cols], inner_of(s, cols), outer[s][:, cols], ADD)
+            nc.gpsimd.tensor_tensor(jump_of(s)[:, cols], inner_of(s, cols), (outer[0] if s == 0 else resp_of(s + 2))[:, cols], ADD)
 
         def stiffen(s):
             dst = z_rows if s < PER_PASS else z_pair[:, :, s - PER_PASS]
@@ -308,10 +304,11 @@ def tile_list_bone_face_features_kernel(
         pages.append(one("page1", [P, T2], F32, "after_moves"))
         nc.gpsimd.memset(pages[1][:], 0.0)
         first_gate = (outer0[:, quarter(1)], outer0[:, quarter(2)], inner0[:, quarter(2)], inner0[:, quarter(3)])
-        first_gated = (ring[0][:, quarter(0)], ring[0][:, quarter(1)], ring[0][:, quarter(2)], first_plain[:, quarter(0)])
-        first_sum = (ring[0][:, quarter(2)], ring[0][:, quarter(3)], gate[:, quarter(0)], gate[:, quarter(2)])
+        first_gated = (ring[0][:, quarter(0)], ring[0][:, quarter(1)], ring[1][:, quarter(2)], ring[0][:, quarter(2)])
+        first_sum = (ring[0][:, quarter(2)], ring[0][:, quarter(3)], ring[1][:, quarter(3)], put[1][:, quarter(0)])
+        first_put = [put[0][:, quarter(q)] for q in range(3)] + [resp[:, quarter(0)]]
 
-        first_acc = [[banks[b][:, quarter(0)] for b in three] for three in ((0, 1, 3), (2, 5, 7), (4, 1, 6), (4, 3, 6))]
+        first_acc = [[banks[b][:, quarter(0)] for b in three] for three in ((0, 1, 3), (2, 5, 7), (4, 6, 0), (2, 4, 3))]
 
         def first_product(q, k):
             codes, scales = weights(0)[k]
@@ -327,21 +324,18 @@ def tile_list_bone_face_features_kernel(
         def first_other_products(q):
             first_product(q, 1)
             first_product(q, 2)
-            if q >= 2:
-                nc.scalar.copy(first_plain[:, quarter(q - 2)], first_acc[q][2])
 
         def first_gating(q):
             nc.vector.tensor_tensor(first_gated[q], first_acc[q][1], first_gate[q], MULT)
 
         def first_summing(q):
-            if q < 2:
-                nc.vector.tensor_tensor(first_sum[q], first_acc[q][2], first_gated[q], ADD)
-            else:
-                nc.gpsimd.tensor_tensor(first_sum[q], first_plain[:, quarter(q - 2)], first_gated[q], ADD)
+            nc.vector.tensor_tensor(first_sum[q], first_acc[q][2], first_gated[q], ADD)
 
         def first_weighing(q):
-            engine = nc.vector if q == 0 else nc.gpsimd
-            engine.tensor_tensor(put[0][:, quarter(q)], first_sum[q], wgs_sb[:, quarter(q)], MULT)
+            nc.gpsimd.tensor_tensor(first_put[q], first_sum[q], wgs_sb[:, quarter(q)], MULT)
+
+        def first_place(q):
+            nc.vector.tensor_copy(pages[0][:].indirect(entries(idx2, quarter(q))), first_put[q])
 
         gated1 = work[:, 7 * QUARTER : 9 * QUARTER]
 
@@ -349,43 +343,40 @@ def tile_list_bone_face_features_kernel(
             nc.gpsimd.tensor_tensor(dst, resp_of(n)[:, half(h)], gate_of(n)[:, half(h)], MULT)
             sum_up(n, h, dst)
 
-        for q in range(2):
+        for q in range(3):
             first_gate_product(q)
             first_other_products(q)
-        first_gate_product(2)
+        first_gate_product(3)
         for q in range(2):
             first_gating(q)
         gated_products(1, 0)
-        first_other_products(2)
-        first_gate_product(3)
         for q in range(2):
             first_summing(q)
+        first_gating(2)
+        first_summing(2)
         first_other_products(3)
-        for q in range(2):
+        for q in range(3):
             first_weighing(q)
         plain_product(1, 0)
-        place(0, quarter(0))
-        first_gating(2)
         gate_half(1, 0, gated1)
-        first_summing(2)
-        first_weighing(2)
+        first_place(0)
+        first_gating(3)
+        gated_products(1, 1)
+        first_place(1)
+        first_summing(3)
+        plain_product(1, 1)
         for a in range(2):
             interleave(wb_bf[1][:, half(a)], wb_raw[1][:, :, block(a)], nc.scalar.copy)
-        gated_products(1, 1)
-        plain_product(1, 1)
-        place(0, quarter(1))
-        first_gating(3)
-        weigh(1, half(0))
         src = wb_raw[2].rearrange("p j (g t h i) -> p t g h j i", t=PER_PASS, h=2, i=4)
         for t in range(PER_PASS):
             nc.scalar.copy(out=dealt_bf[:, half(t)].rearrange("p (g h i j) -> p g h j i", h=2, i=4, j=4), in_=src[:, t])
-        gate_half(1, 1, ring[1][:, half(0)])
-        first_summing(3)
+        gate_half(1, 1, ring[1][:, half(1)])
         first_weighing(3)
-        weigh(1, half(1))
-        place(0, quarter(2))
+        for h in range(2):
+            weigh(1, half(h))
+        first_place(2)
+        first_place(3)
         place(1, half(0))
-        place(0, quarter(3))
         late_codes = one("late_codes", [P, 3 * QUARTER], U32, "after_weigh1")
         wb_w.extend((late_codes[:, 0:QUARTER], late_codes[:, QUARTER : 3 * QUARTER]))
         quantise(wb_w[1], wb_s[:, quarter(1)], wb_bf[1])
@@ -400,7 +391,7 @@ def tile_list_bone_face_features_kernel(
         dealt_weights = (dealt_bytes[:, 0 : 2 * K], dealt_bytes[:, 2 * K : 3 * K],
                          dealt_bytes[:, 4 * K : 8 * K].bitcast(U32), dealt_bytes[:, 3 * K : 4 * K])
         gated_products(3, 0)
-        nc.gpsimd.tensor_tensor(resp[:, half(1)], resp3[:, half(0)], gate[:, half(0)], MULT)
+        nc.gpsimd.tensor_tensor(resp[:, half(1)], resp_odd[:, half(0)], gate[:, half(0)], MULT)
         for h in range(2):
             weigh(2, half(h))
         gated_products(3, 1)
@@ -415,13 +406,17 @@ def tile_list_bone_face_features_kernel(
             if s > 1:
                 place(s, whole)
             fetch_inner(s - 1, whole)
-            for h in range(2 if s < LAST - 1 else 1):
-                fetch_outer(s, h, outer[s][:, half(h)])
+            if s < LAST - 1:
+                nc.vector.tensor_copy(outer[s][:, whole], pages[s % 2][:].indirect(idx4[:]))
+            else:
+                fetch_outer(s, 0, outer[s][:, half(0)])
             add_picks(s - 1, whole)
             if s == 1:
                 gate_half(3, 1, inner0[:, half(1)])
             elif s + 2 < SLICES:
                 gating(s + 2)
+            if s < LAST - 1:
+                nc.scalar.activation(resp_of(s + 2)[:], outer[s][:, whole], COPY, bias=1.0, scale=-1.0)
             stiffen(s - 1)
             if s + 2 < SLICES:
                 weigh(s + 2, whole)

@@ -139,7 +139,7 @@ def tile_list_bone_face_features_kernel(
             nc.sync.dma_start(out=wc_w[g][:].bitcast(I32)[:, first : first + c1 - c0], in_=wc_rows[:, c0:c1])
 
         nc.sync.dma_start(idx1[:], offs)
-        nc.sync.dma_start(out=tab_s[0:P:8, :].bitcast(I32), in_=tab_scales[0].bitcast(I32))
+        nc.scalar.dma_start(out=tab_s[0:P:8, :].bitcast(I32), in_=tab_scales[0].bitcast(I32))
         load_wb(0)
         load_scales(nc.sync, wa_s, wa_scales[0], half(0))
         nc.sync.dma_start(out=tab_w[:].bitcast(I32), in_=tab_words[0].rearrange("p n t -> p (n t)").bitcast(I32))

@@ -103,14 +103,15 @@ def tile_list_bone_face_features_kernel(
         outer = [outer0, work[:, 2 * S : 3 * S]] + stiff_sb[0 : SLICES - 3]
         stiff6 = one("stiff6", [P, HALF], F32, "after_stiff6")
         jump6 = one("jump6", [P, HALF], F32)
-        end7 = one("end7", [P, F], F32)
+        jump7 = one("jump7", [P, HALF], F32)
+        stiff7 = one("stiff7", [P, HALF], F32, "after_stiff7")
         late_stiff = one("late_stiff", [P, 2, HALF], F32)
         z_rows = gate[:, half(1)].bitcast(BF16)
         z_t = tiles("z_t", 2, [P, BLOCKS * HALF], BF16)
         z_words = one("z_words", [P, 2 * F], F32)
         z_pair = gate[:].bitcast(BF16).rearrange("p (m e) -> p m e", e=2)
         z_last = one("z_last", [P, 4 * F], BF16)
-        z_w = {1: one("z_w1", [P, F], U32)}
+        z_w1 = one("z_w1", [P, F], U32)
         z_s = tiles("z_s", 2, [P, F], U8)
 
         def dealt(rows, t):
@@ -171,7 +172,7 @@ def tile_list_bone_face_features_kernel(
             if s == 1:
                 for t in range(PER_PASS):
                     nc.sync.dma_start(out=wd_raw[:, 1, t], in_=dealt(wd[K:H, :], t))
-        for dst, t, h in ((stiff6[:], 2, 0), (end7[:, half(1)], 3, 0), (late_stiff[:, 0], 2, 1), (late_stiff[:, 1], 3, 1)):
+        for dst, t, h in ((stiff6[:], 2, 0), (stiff7[:], 3, 0), (late_stiff[:, 0], 2, 1), (late_stiff[:, 1], 3, 1)):
             nc.sync.dma_start(out=dst, in_=dealt(stiff[K:H, half(h)], t))
 
 
@@ -267,10 +268,10 @@ def tile_list_bone_face_features_kernel(
             nc.vector.tensor_tensor(dst, pages[s % 2][:].indirect(entries(idx3, cols)), outer_part, ADD)
 
         def jump_of(s):
-            return ([ring[0], wgs_sb] + wgs_dealt)[s]
+            return ([outer0, wgs_sb] + wgs_dealt)[s]
 
         def add_picks(s, cols):
-            nc.gpsimd.tensor_tensor(jump_of(s)[:, cols], inner_of(s, cols), (outer[0] if s == 0 else resp_of(s + 2))[:, cols], ADD)
+            nc.gpsimd.tensor_tensor(jump_of(s)[:, cols], inner_of(s, cols), (ring[0] if s == 0 else resp_of(s + 2))[:, cols], ADD)
 
         def stiffen(s):
             dst = z_rows if s < PER_PASS else z_pair[:, :, s - PER_PASS]
@@ -382,8 +383,7 @@ def tile_list_bone_face_features_kernel(
         quantise(wb_w[1], wb_s[:, quarter(1)], wb_bf[1])
         quantise(wb_w[2], wb_s[:, K:H], dealt_bf)
         place(1, half(1))
-        for h in range(2):
-            fetch_outer(0, h, outer[0][:, half(h)])
+        nc.vector.tensor_copy(outer[0][:], pages[0][:].indirect(idx4[:]))
         products(2)
         for h in range(2):
             gate_half(2, h, gated[:, half(h)])
@@ -394,6 +394,7 @@ def tile_list_bone_face_features_kernel(
         nc.gpsimd.tensor_tensor(resp[:, half(1)], resp_odd[:, half(0)], gate[:, half(0)], MULT)
         for h in range(2):
             weigh(2, half(h))
+        nc.scalar.activation(ring[0], outer0[:], COPY, bias=1.0, scale=-1.0)
         gated_products(3, 1)
         for h in range(2):
             plain_product(3, h)
@@ -441,9 +442,19 @@ def tile_list_bone_face_features_kernel(
         place(LAST, whole)
         nc.gpsimd.tensor_tensor(jump6[:], ring[LAST % 2][:, half(0)], outer[LAST - 1][:, half(0)], ADD)
         nc.gpsimd.tensor_tensor(slots[:, half(0), 2], jump6[:], stiff6[:], MULT)
-        end_codes = one("end_codes", [P, F + 2 * N], U32, "after_stiff6")
-        z_w.setdefault(0, end_codes[:, 0:F])
-        wd_w = end_codes[:, F : F + 2 * N]
+        end_codes = one("end_codes", [P, HALF + 2 * N], U32, "after_stiff6")
+        wd_w = end_codes[:, HALF : HALF + 2 * N]
+        z0_w = [end_codes[:, 0:HALF]]
+
+        def z_codes(g, cols):
+            if g == 1:
+                return z_w1[:, cols]
+            h = cols.start // HALF
+            return z0_w[h][:, cols.start - h * HALF : cols.stop - h * HALF]
+
+        def quantise_z(g, cols):
+            values = z_last[:] if g == 1 else z_words[:].bitcast(BF16)
+            quantise(z_codes(g, cols), z_s[g][:, cols], values[:, 4 * cols.start : 4 * cols.stop])
 
         pieces = [(half(0), (bank_a[0], bank_a[1], bank_b[0], bank_b[1]))]
         pieces.extend((block(BLOCKS + k), out_banks)
@@ -458,12 +469,12 @@ def tile_list_bone_face_features_kernel(
                 w_cols = slice(g * N + nb * P, g * N + (nb + 1) * P)
                 nc.tensor.matmul_mx(out=out_banks[nb // per_bank][:, a * width : (a + 1) * width],
                                     lhsT=wd_w[:, w_cols].bitcast(FP8X4), lhsT_scale=wd_s[:, w_cols],
-                                    rhs=z_w[g][:, cols].bitcast(FP8X4), rhs_scale=z_s[g][:, cols],
+                                    rhs=z_codes(g, cols).bitcast(FP8X4), rhs_scale=z_s[g][:, cols],
                                     start=g == 0 and a == 0, stop=g == 1 and a == per_bank - 1)
 
         def finish(k, at, copies):
             cols, out_banks = pieces[k]
-            quantise(z_w[1][:, cols], z_s[1][:, cols], z_last[:, 4 * cols.start : 4 * cols.stop])
+            quantise_z(1, cols)
             last_products(1, cols, out_banks)
             per_bank = N // P // len(out_banks)
             used = per_bank * (cols.stop - cols.start)
@@ -475,30 +486,38 @@ def tile_list_bone_face_features_kernel(
                                   in_=stage.rearrange("p (a m) -> p a m", a=per_bank))
 
         late_outer = (z_words[:, half(0)], z_words[:, half(1)])
-        late_jump = [end7[:, half(k % 2)][:, 0:QUARTER].rearrange("p (e m) -> p e m", e=2) for k in range(BLOCKS)]
+        late_jump = [jump7[:, quarter(k % 2)].rearrange("p (e m) -> p e m", e=2) for k in range(BLOCKS)]
 
         def late_sum(e, k):
             add_inner(LAST - 1 + e, pieces[k + 1][0], late_jump[k][:, e], late_outer[e][:, block(k)])
 
         quantise(wd_w, wd_s[:], wd_bf[:])
         fetch_outer(LAST, 0, jump6[:])
-        quantise(z_w[0], z_s[0][:], z_words[:].bitcast(BF16))
-        add_inner(LAST, half(0), end7[:, half(0)], jump6[:])
+        quantise_z(0, half(0))
+        add_inner(LAST, half(0), jump7[:], jump6[:])
         for e in range(2):
             fetch_outer(LAST - 1 + e, 1, late_outer[e])
-        for cols, out_banks in pieces[:-1]:
-            last_products(0, cols, out_banks)
-        nc.gpsimd.tensor_tensor(slots[:, half(0), 3], end7[:, half(0)], end7[:, half(1)], MULT)
+        last_products(0, *pieces[0])
+        nc.gpsimd.tensor_tensor(slots[:, half(0), 3], jump7[:], stiff7[:], MULT)
         finish(0, 0, [nc.scalar.copy] * 4)
-        last_products(0, *pieces[-1])
+        z0_w.append(one("z0_late", [P, HALF], U32, "after_stiff7")[:])
         late_sum(0, 0)
         late_sum(1, 0)
         late_sum(0, 1)
+
+        def late_first_pass(q):
+            quantise_z(0, quarter(q))
+            for piece in pieces[2 * q - 3 : 2 * q - 1]:
+                last_products(0, *piece)
+
+        late_first_pass(2)
         for k in range(BLOCKS):
             nc.vector.tensor_tensor(slots[:, pieces[k + 1][0], 2:4], late_jump[k].rearrange("p e m -> p m e"),
                                     late_stiff[:, :, block(k)].rearrange("p e m -> p m e"), MULT)
             if k + 1 < BLOCKS:
                 late_sum(1, k + 1)
             finish(k + 1, BLOCKS + k, [nc.scalar.copy, nc.vector.tensor_copy])
+            if k == 0:
+                late_first_pass(3)
             if k + 2 < BLOCKS:
                 late_sum(0, k + 2)

from contextlib import ExitStack

import concourse.mybir as mybir
from concourse.masks import make_identity

K, T, S, T2, F, H, N = 512, 4096, 1024, 2048, 1024, 1024, 512
FLOPS = 2 * (3 * K * H * S + H * N * F)

F32 = mybir.dt.float32
BF16 = mybir.dt.bfloat16
I32 = mybir.dt.int32
U32 = mybir.dt.uint32
U16 = mybir.dt.uint16
U8 = mybir.dt.uint8
FP8X4 = mybir.dt.float8_e4m3fn_x4
FP4X4 = mybir.dt.float4_e2m1fn_x4
MULT = mybir.AluOpType.mult
ADD = mybir.AluOpType.add
COPY = mybir.ActivationFunctionType.Copy
SIGMOID = mybir.ActivationFunctionType.Sigmoid

P = 128
HALF = 512
QUARTER = 256
BLOCKS = HALF // P
SLICES = H // P
PER_PASS = 4
LAST = SLICES - 1
WB_CHUNKS = ((0, 256), (256, 512), (512, 1024))


def tile_list_bone_face_features_kernel(
    tc, tab_words, tab_scales, wa_words, wa_scales, wb, wc_words, wc_scales,
    wgs, stiff, wd, offs, offs2, offs3, offs4, out,
):
    nc = tc.nc
    with ExitStack() as ctx:
        lists = ctx.enter_context(tc.tile_pool(name="lists", bufs=1))
        sb = ctx.enter_context(tc.tile_pool(name="sb", bufs=1))
        ps = ctx.enter_context(tc.psum_pool(name="ps", bufs=1))

        def one(name, shape, dtype, tag=""):
            return sb.tile(shape, dtype, name=name, align_bytes=64, tag=tag)

        def tiles(name, count, shape, dtype):
            return [one("%s%d" % (name, i), shape, dtype) for i in range(count)]

        def block(i):
            return slice(i * P, (i + 1) * P)

        def quarter(q):
            return slice(q * QUARTER, (q + 1) * QUARTER)

        def half(h):
            return slice(h * HALF, (h + 1) * HALF)

        whole = slice(0, S)
        idx1 = lists.tile([P, S // 16], U16, name="idx1")
        idx2 = lists.tile([P, S // 16], U16, name="idx2")
        idx3 = lists.tile([P, F // 16], U16, name="idx3")
        idx4 = lists.tile([P, F // 16], U16, name="idx4")

        def entries(idx, cols):
            return idx[:, cols.start // 16 : cols.stop // 16]

        banks = [ps.tile([P, HALF], F32, name="bank%d" % i) for i in range(8)]
        bank_b, bank_a = (banks[1], banks[2]), (banks[5], banks[6])
        bank_c, bank_s = (banks[3], banks[4]), (banks[7], banks[0])

        ident_bf = one("ident_bf", [P, P], BF16)
        tab_w = one("tab_w", [P, T], U32, "table")
        tab_s = one("tab_s", [P, T], U8, "after_scale_gather")
        picked_s = one("picked_s", [P, S], U8, "after_moves")
        v_w = tiles("v_w", 2, [P, HALF], U32)
        v_s = one("v_s", [P, S], U8)
        wa_w = [one("wa_w0", [P, 2 * K], U8), one("wa_w1", [P, 2 * K], U8)]
        wc_w = tiles("wc_w", 2, [P, K], U32)
        planes = one("planes", [P, 2 * H], U8)
        wa_s, wc_s = planes[:, 0:H], planes[:, H : 2 * H]
        wb_last = one("wb_last", [P, 4 * HALF], F32, "after_weigh1")
        wb_raw = [one("wb_raw0", [P, 4, QUARTER], F32, "after_rounding")[:], one("wb_raw1", [P, 4, QUARTER], F32)[:]]
        wb_raw.append(wb_last[:].rearrange("p (j c) -> p j c", j=4))
        wb_w = [one("wb_w0", [P, QUARTER], U32)]
        wb_s = one("wb_s", [P, H], U8)
        wd_s = one("wd_s", [P, 2 * N], U8)
        wgs_sb = one("wgs_sb", [P, S], F32, "after_weigh3")
        wgs_dealt = tiles("wgs_dealt", PER_PASS, [P, S], F32)
        pages = [one("page0", [P, T2], F32)]
        work = one("work", [P, 3 * S], F32)
        ring = (work[:, S : 2 * S], work[:, 0:S])
        put = tiles("put", 2, [P, S], F32)
        inner0 = one("inner0", [P, F], F32)
        outer0 = one("outer0", [P, F], F32)
        wb_bf = [one("wb_bf0", [P, 4 * QUARTER], BF16, "after_scale_gather")[:], outer0[:, QUARTER : 3 * QUARTER].bitcast(BF16)]
        dealt_bf = inner0[:].bitcast(BF16)
        gate = one("gate", [P, S], F32)
        gate2 = one("gate2", [P, S], F32, "after_gate2")
        resp = one("resp", [P, S], F32)
        plain = one("plain", [P, S], F32)
        resp_odd = one("resp_odd", [P, S], F32)
        gated = one("gated", [P, S], F32)
        stiff_sb = tiles("stiff_sb", SLICES - 2, [P, F], F32)
        outer = [outer0, work[:, 2 * S : 3 * S]] + stiff_sb[0 : SLICES - 3]
        stiff6 = one("stiff6", [P, HALF], F32, "after_stiff6")
        jump6 = one("jump6", [P, HALF], F32)
        jump7 = one("jump7", [P, HALF], F32)
        stiff7 = one("stiff7", [P, HALF], F32, "after_stiff7")
        late_stiff = one("late_stiff", [P, 2, HALF], F32)
        z_rows = gate[:, half(1)].bitcast(BF16)
        z_t = tiles("z_t", 2, [P, BLOCKS * HALF], BF16)
        z_words = one("z_words", [P, 2 * F], F32)
        z_pair = gate[:].bitcast(BF16).rearrange("p (m e) -> p m e", e=2)
        z_last = one("z_last", [P, 4 * F], BF16)
        z_w1 = one("z_w1", [P, F], U32)
        z_s = tiles("z_s", 2, [P, F], U8)

        def dealt(rows, t):
            return rows.rearrange("(g t i) c -> t g i c", t=PER_PASS, i=8)[t]

        nc.vector.memset(tab_s[:].bitcast(I32), 0)
        nc.vector.memset(planes[:].bitcast(I32), 0)
        nc.vector.memset(v_s[:].bitcast(I32), 0)
        nc.vector.memset(pages[0][:], 0.0)
        wb_rows = wb.rearrange("(p j) c -> p j c", j=4)
        wa_rows = wa_words[0].bitcast(I32)
        wc_rows = wc_words[0].rearrange("p n t -> p (n t)").bitcast(I32)

        def load_wb(i):
            c0, c1 = WB_CHUNKS[i]
            nc.sync.dma_start(out=wb_raw[i], in_=wb_rows[:, :, c0:c1])

        def load_scales(queue, plane, rows, cols):
            for q in range(4):
                queue.dma_start(out=plane[32 * q : 32 * q + 4, cols].bitcast(I32),
                                in_=rows[4 * q : 4 * q + 4, cols].bitcast(I32))

        def load_packed(c0, c1):
            g, first = divmod(c0, K)
            nc.sync.dma_start(out=wa_w[g][:].bitcast(I32)[:, first // 2 : (first + c1 - c0) // 2], in_=wa_rows[:, c0 // 2 : c1 // 2])
            nc.sync.dma_start(out=wc_w[g][:].bitcast(I32)[:, first : first + c1 - c0], in_=wc_rows[:, c0:c1])

        nc.sync.dma_start(idx1[:], offs)
        nc.scalar.dma_start(out=tab_s[0:P:8, :].bitcast(I32), in_=tab_scales[0].bitcast(I32))
        load_wb(0)
        load_scales(nc.sync, wa_s, wa_scales[0], half(0))
        nc.sync.dma_start(out=tab_w[:].bitcast(I32), in_=tab_words[0].rearrange("p n t -> p (n t)").bitcast(I32))
        load_scales(nc.gpsimd, wc_s, wc_scales[0], slice(0, H))
        load_packed(*WB_CHUNKS[0])
        nc.vector.tensor_copy(picked_s[:], tab_s[:].indirect(idx1[:]))
        for q in range(4):
            nc.scalar.dma_start(out=v_s[32 * q : 32 * q + 4, :].bitcast(I32),
                                in_=picked_s[32 * q : 32 * (q + 1) : 8, :].bitcast(I32))
        nc.sync.dma_start(idx2[:], offs2)
        for h in range(2):
            nc.sync.dma_start(out=wgs_sb[:, half(h)], in_=wgs[:, half(h)])
        load_wb(1)
        load_wb(2)
        nc.sync.dma_start(idx4[:], offs4)
        nc.sync.dma_start(idx3[:], offs3)
        load_packed(*WB_CHUNKS[1])
        load_packed(*WB_CHUNKS[2])
        load_scales(nc.sync, wa_s, wa_scales[0], half(1))
        wd_raw = one("wd_raw", [P, 2, 4, N], F32, "table")
        for s in range(SLICES - 2):
            rows = stiff[block(s), :] if s < PER_PASS else dealt(stiff[K:H, :], s - PER_PASS)
            nc.sync.dma_start(out=stiff_sb[s][:], in_=rows)
            if s < PER_PASS:
                for a in range(4):
                    nc.sync.dma_start(out=wgs_dealt[s][32 * a : 32 * (a + 1), :], in_=dealt(wgs, s))
            if s == 0:
                nc.sync.dma_start(out=wd_raw[:, 0], in_=wd[0:K, :].rearrange("(p j) c -> p j c", j=4))
            if s == 1:
                for t in range(PER_PASS):
                    nc.sync.dma_start(out=wd_raw[:, 1, t], in_=dealt(wd[K:H, :], t))
        for dst, t, h in ((stiff6[:], 2, 0), (stiff7[:], 3, 0), (late_stiff[:, 0], 2, 1), (late_stiff[:, 1], 3, 1)):
            nc.sync.dma_start(out=dst, in_=dealt(stiff[K:H, half(h)], t))


        def interleave(dst, raw, copy):
            copy(out=dst.rearrange("p (c i t) -> p c t i", i=4, t=4), in_=raw.rearrange("p t (c i) -> p c t i", i=4))

        def quantise(codes, scales, values):
            nc.vector.quantize_mx(out=codes.bitcast(FP8X4), scales=scales, in_=values)

        def weights(s):
            b = block(s % PER_PASS)
            wide = slice(2 * b.start, 2 * b.stop)
            a_w, a_s, c_w, c_s = (wa_w[0], wa_s, wc_w[0], wc_s) if s < PER_PASS else dealt_weights
            i = max(k for k, (c0, c1) in enumerate(WB_CHUNKS) if c0 <= s * P)
            c0 = s * P - WB_CHUNKS[i][0]
            return ((wb_w[i][:, c0 : c0 + P].bitcast(FP8X4), wb_s[:, block(s)]),
                    (a_w[:, wide].bitcast(FP4X4), a_s[:, b]),
                    (c_w[:, b].bitcast(FP8X4), c_s[:, b]))

        def turn(out_ap, in_ap, start=True, stop=True, by=None):
            nc.tensor.matmul(out_ap, in_ap, (ident if by is None else by)[:], start=start, stop=stop, is_transpose=True)

        def gate_of(n):
            return gate2 if n == 2 else gate

        def resp_of(n):
            return resp if n == 1 else (resp, resp_odd)[n % 2]

        def product(bank, h, codes, scales):
            for i in range(BLOCKS):
                nc.tensor.matmul_mx(out=bank[:, block(i)], lhsT=v_w[h][:, block(i)].bitcast(FP8X4),
                                    lhsT_scale=v_s[:, block(BLOCKS * h + i)], rhs=codes, rhs_scale=scales,
                                    start=True, stop=True)

        def sum_banks(n):
            return (bank_b, bank_s)[n % 2]

        def gate_banks(n):
            return (bank_c[0], bank_b[1]) if n == 3 else (bank_b, bank_s)[(n - 1) % 2]

        def open_sum(n, h):
            for i in range(BLOCKS):
                turn(sum_banks(n)[h][:, block(i)], plain[:, block(BLOCKS * h + i)], i == 0, False)

        def gated_products(n, h):
            w_b, w_a, w_c = weights(n)
            product(gate_banks(n)[h], h, *w_b)
            product(bank_a[h], h, *w_a)
            nc.scalar.activation(gate_of(n)[:, half(h)], gate_banks(n)[h][:], SIGMOID)
            nc.scalar.copy(resp_of(n)[:, half(h)], bank_a[h][:])

        def plain_product(n, h):
            product(bank_a[h], h, *weights(n)[2])
            nc.scalar.copy(plain[:, half(h)], bank_a[h][:])
            open_sum(n, h)

        def products(n):
            for h in range(2):
                gated_products(n, h)
            for h in range(2):
                plain_product(n, h)

        def sum_of(n, cols):
            return wb_last[:, half(0)] if (n, cols) == (1, half(1)) else ring[n % 2][:, cols]

        def inner_of(s, cols):
            return (inner0 if s == 0 else ring[(s + 1) % 2])[:, cols]

        def sum_up(n, h, values):
            for i in range(BLOCKS):
                turn(sum_banks(n)[h][:, block(i)], values[:, block(i)], False, i == BLOCKS - 1)
            nc.scalar.copy(sum_of(n, half(h)), sum_banks(n)[h][:])

        def gating(n):
            nc.gpsimd.tensor_tensor(gated[:], resp_of(n)[:], gate_of(n)[:], MULT)
            for h in range(2):
                sum_up(n, h, gated[:, half(h)])

        def weigh(n, cols):
            factor = wgs_sb if n < PER_PASS else wgs_dealt[n - PER_PASS]
            nc.gpsimd.tensor_tensor(put[n % 2][:, cols], sum_of(n, cols), factor[:, cols], MULT)

        def place(s, cols):
            nc.vector.tensor_copy(pages[s % 2][:].indirect(entries(idx2, cols)), put[s % 2][:, cols])

        def fetch_outer(s, h, dst):
            nc.vector.tensor_scalar(dst, pages[s % 2][:].indirect(entries(idx4, half(h))), -1.0, 1.0, MULT, ADD)

        def fetch_inner(s, cols):
            nc.vector.tensor_copy(inner_of(s, cols), pages[s % 2][:].indirect(entries(idx3, cols)))

        def add_inner(s, cols, dst, outer_part):
            nc.vector.tensor_tensor(dst, pages[s % 2][:].indirect(entries(idx3, cols)), outer_part, ADD)

        def jump_of(s):
            return ([outer0, wgs_sb] + wgs_dealt)[s]

        def add_picks(s, cols):
            nc.gpsimd.tensor_tensor(jump_of(s)[:, cols], inner_of(s, cols), (ring[0] if s == 0 else resp_of(s + 2))[:, cols], ADD)

        def stiffen(s):
            dst = z_rows if s < PER_PASS else z_pair[:, :, s - PER_PASS]
            nc.gpsimd.tensor_tensor(dst, jump_of(s)[:, whole], stiff_sb[s][:], MULT)

        def turn_rows(s):
            for h in range(2):
                turned = bank_c[h][:].bitcast(BF16)
                for i in range(BLOCKS):
                    turn(turned[:, block(i)], z_rows[:, block(BLOCKS * h + i)], by=ident_bf)
                dst = z_t[h][:].bitcast(F32).rearrange("p (b u w) -> p b u w", b=BLOCKS, u=2)[:, :, :, 32 * s : 32 * (s + 1)]
                nc.scalar.copy(out=dst, in_=bank_c[h][:, 0:QUARTER].rearrange("p (b q u) -> p b u q", b=BLOCKS, u=2))

        def turn_back():
            for h in range(2):
                words = z_t[h][:].bitcast(F32)
                for pair in range(2):
                    bank = (bank_a, bank_b)[h][pair]
                    for i in range(BLOCKS):
                        turn(bank[:, block(i)], words[:, block(BLOCKS * pair + i)])
                    first = 2 * (h * HALF + pair * QUARTER)
                    nc.scalar.copy(out=z_words[:, first : first + HALF].rearrange("p (b m u) -> p b m u", b=2, u=2),
                                   in_=bank[:].rearrange("p (b u m) -> p b m u", b=2, u=2))

        for a in range(2):
            interleave(wb_bf[0][:, half(a)], wb_raw[0][:, :, block(a)], nc.vector.tensor_copy)
        quantise(wb_w[0][:], wb_s[:, quarter(0)], wb_bf[0])
        ident = one("ident", [P, P], F32, "after_rounding")
        make_identity(nc, ident[:])
        nc.gpsimd.tensor_copy(out=ident_bf[:], in_=ident[:])
        pages.append(one("page1", [P, T2], F32, "after_moves"))
        nc.gpsimd.memset(pages[1][:], 0.0)
        first_gate = (outer0[:, quarter(1)], outer0[:, quarter(2)], inner0[:, quarter(2)], inner0[:, quarter(3)])
        first_gated = (ring[0][:, quarter(0)], ring[0][:, quarter(1)], ring[1][:, quarter(2)], ring[0][:, quarter(2)])
        first_sum = (ring[0][:, quarter(2)], ring[0][:, quarter(3)], ring[1][:, quarter(3)], put[1][:, quarter(0)])
        first_put = [put[0][:, quarter(q)] for q in range(3)] + [resp[:, quarter(0)]]

        first_acc = [[banks[b][:, quarter(0)] for b in three] for three in ((0, 1, 3), (2, 5, 7), (4, 6, 0), (2, 4, 3))]

        def first_product(q, k):
            codes, scales = weights(0)[k]
            nc.tensor.matmul_mx(out=first_acc[q][k], lhsT=codes, lhsT_scale=scales,
                                rhs=v_w[q // 2][:, quarter(q % 2)].bitcast(FP8X4), rhs_scale=v_s[:, quarter(q)],
                                start=True, stop=True)

        def first_gate_product(q):
            nc.vector.tensor_copy(v_w[q // 2][:, quarter(q % 2)], tab_w[:].indirect(entries(idx1, quarter(q))))
            first_product(q, 0)
            nc.scalar.activation(first_gate[q], first_acc[q][0], SIGMOID)

        def first_other_products(q):
            first_product(q, 1)
            first_product(q, 2)

        def first_gating(q):
            nc.vector.tensor_tensor(first_gated[q], first_acc[q][1], first_gate[q], MULT)

        def first_summing(q):
            nc.vector.tensor_tensor(first_sum[q], first_acc[q][2], first_gated[q], ADD)

        def first_weighing(q):
            nc.gpsimd.tensor_tensor(first_put[q], first_sum[q], wgs_sb[:, quarter(q)], MULT)

        def first_place(q):
            nc.vector.tensor_copy(pages[0][:].indirect(entries(idx2, quarter(q))), first_put[q])

        gated1 = work[:, 7 * QUARTER : 9 * QUARTER]

        def gate_half(n, h, dst):
            nc.gpsimd.tensor_tensor(dst, resp_of(n)[:, half(h)], gate_of(n)[:, half(h)], MULT)
            sum_up(n, h, dst)

        for q in range(3):
            first_gate_product(q)
            first_other_products(q)
        first_gate_product(3)
        for q in range(2):
            first_gating(q)
        gated_products(1, 0)
        for q in range(2):
            first_summing(q)
        first_gating(2)
        first_summing(2)
        first_other_products(3)
        for q in range(3):
            first_weighing(q)
        plain_product(1, 0)
        gate_half(1, 0, gated1)
        first_place(0)
        first_gating(3)
        gated_products(1, 1)
        first_place(1)
        first_summing(3)
        plain_product(1, 1)
        for a in range(2):
            interleave(wb_bf[1][:, half(a)], wb_raw[1][:, :, block(a)], nc.scalar.copy)
        src = wb_raw[2].rearrange("p j (g t h i) -> p t g h j i", t=PER_PASS, h=2, i=4)
        for t in range(PER_PASS):
            nc.scalar.copy(out=dealt_bf[:, half(t)].rearrange("p (g h i j) -> p g h j i", h=2, i=4, j=4), in_=src[:, t])
        gate_half(1, 1, ring[1][:, half(1)])
        first_weighing(3)
        for h in range(2):
            weigh(1, half(h))
        first_place(2)
        first_place(3)
        place(1, half(0))
        late_codes = one("late_codes", [P, 3 * QUARTER], U32, "after_weigh1")
        wb_w.extend((late_codes[:, 0:QUARTER], late_codes[:, QUARTER : 3 * QUARTER]))
        quantise(wb_w[1], wb_s[:, quarter(1)], wb_bf[1])
        quantise(wb_w[2], wb_s[:, K:H], dealt_bf)
        place(1, half(1))
        nc.vector.tensor_copy(outer[0][:], pages[0][:].indirect(idx4[:]))
        products(2)
        for h in range(2):
            gate_half(2, h, gated[:, half(h)])
        dealt_bytes = one("dealt_bytes", [P, 8 * K], U8, "after_gate2")
        dealt_weights = (dealt_bytes[:, 0 : 2 * K], dealt_bytes[:, 2 * K : 3 * K],
                         dealt_bytes[:, 4 * K : 8 * K].bitcast(U32), dealt_bytes[:, 3 * K : 4 * K])
        gated_products(3, 0)
        nc.gpsimd.tensor_tensor(resp[:, half(1)], resp_odd[:, half(0)], gate[:, half(0)], MULT)
        for h in range(2):
            weigh(2, half(h))
        nc.scalar.activation(ring[0], outer0[:], COPY, bias=1.0, scale=-1.0)
        gated_products(3, 1)
        for h in range(2):
            plain_product(3, h)
        sum_up(3, 0, resp[:, half(1)])
        for dst, src in zip(dealt_weights, (wa_w[1][:], wa_s[:, K:H], wc_w[1][:], wc_s[:, K:H])):
            nc.scalar.copy(out=dst.bitcast(U32).rearrange("p (t g w) -> p t g w", t=PER_PASS, g=16),
                           in_=src.bitcast(U32).rearrange("p (g t w) -> p t g w", t=PER_PASS, g=16))

        for s in range(1, LAST):
            if s > 1:
                place(s, whole)
            fetch_inner(s - 1, whole)
            if s < LAST - 1:
                nc.vector.tensor_copy(outer[s][:, whole], pages[s % 2][:].indirect(idx4[:]))
            else:
                fetch_outer(s, 0, outer[s][:, half(0)])
            add_picks(s - 1, whole)
            if s == 1:
                gate_half(3, 1, inner0[:, half(1)])
            elif s + 2 < SLICES:
                gating(s + 2)
            if s < LAST - 1:
                nc.scalar.activation(resp_of(s + 2)[:], outer[s][:, whole], COPY, bias=1.0, scale=-1.0)
            stiffen(s - 1)
            if s + 2 < SLICES:
                weigh(s + 2, whole)
            if s - 1 < PER_PASS:
                turn_rows(s - 1)
            if s + 3 < SLICES:
                products(s + 3)
            if s == 2:
                wd_bf = one("wd_bf", [P, 2 * 4 * N], BF16, "after_weigh3")
                for g in range(2):
                    for c0 in range(0, N, P):
                        first = 4 * (g * N + c0)
                        interleave(wd_bf[:, first : first + 4 * P], wd_raw[:, g, :, c0 : c0 + P], nc.scalar.copy)
            if s == PER_PASS:
                turn_back()

        slots = z_last[:].rearrange("p (m t) -> p m t", t=PER_PASS)
        for h in range(2):
            nc.scalar.copy(out=z_last[:].bitcast(F32).rearrange("p (m u) -> p m u", u=2)[:, half(h), 0],
                           in_=gate[:, half(h)])
        fetch_inner(LAST - 1, half(0))
        place(LAST, whole)
        nc.gpsimd.tensor_tensor(jump6[:], ring[LAST % 2][:, half(0)], outer[LAST - 1][:, half(0)], ADD)
        nc.gpsimd.tensor_tensor(slots[:, half(0), 2], jump6[:], stiff6[:], MULT)
        end_codes = one("end_codes", [P, HALF + 2 * N], U32, "after_stiff6")
        wd_w = end_codes[:, HALF : HALF + 2 * N]
        z0_w = [end_codes[:, 0:HALF]]

        def z_codes(g, cols):
            if g == 1:
                return z_w1[:, cols]
            h = cols.start // HALF
            return z0_w[h][:, cols.start - h * HALF : cols.stop - h * HALF]

        def quantise_z(g, cols):
            values = z_last[:] if g == 1 else z_words[:].bitcast(BF16)
            quantise(z_codes(g, cols), z_s[g][:, cols], values[:, 4 * cols.start : 4 * cols.stop])

        pieces = [(half(0), (bank_a[0], bank_a[1], bank_b[0], bank_b[1]))]
        pieces.extend((block(BLOCKS + k), out_banks)
                      for k, out_banks in enumerate((bank_c[:1], bank_c[1:], bank_s[:1], (bank_s[1], bank_a[0]))))
        stages = [t[:, half(h)] for h in range(2) for t in stiff_sb[0:4]] + [put[0][:, half(0)]]

        def last_products(g, cols, out_banks):
            width = cols.stop - cols.start
            per_bank = N // P // len(out_banks)
            for nb in range(N // P):
                a = nb % per_bank
                w_cols = slice(g * N + nb * P, g * N + (nb + 1) * P)
                nc.tensor.matmul_mx(out=out_banks[nb // per_bank][:, a * width : (a + 1) * width],
                                    lhsT=wd_w[:, w_cols].bitcast(FP8X4), lhsT_scale=wd_s[:, w_cols],
                                    rhs=z_codes(g, cols).bitcast(FP8X4), rhs_scale=z_s[g][:, cols],
                                    start=g == 0 and a == 0, stop=g == 1 and a == per_bank - 1)

        def finish(k, at, copies):
            cols, out_banks = pieces[k]
            quantise_z(1, cols)
            last_products(1, cols, out_banks)
            per_bank = N // P // len(out_banks)
            used = per_bank * (cols.stop - cols.start)
            for b, bank in enumerate(out_banks):
                stage = stages[at + b][:, 0:used]
                copies[b](out=stage, in_=bank[:, 0:used])
                rows = out[b * per_bank * P : (b + 1) * per_bank * P, cols]
                nc.sync.dma_start(out=rows.rearrange("(a p) m -> p a m", a=per_bank),
                                  in_=stage.rearrange("p (a m) -> p a m", a=per_bank))

        late_outer = (z_words[:, half(0)], z_words[:, half(1)])
        late_jump = [jump7[:, quarter(k % 2)].rearrange("p (e m) -> p e m", e=2) for k in range(BLOCKS)]

        def late_sum(e, k):
            add_inner(LAST - 1 + e, pieces[k + 1][0], late_jump[k][:, e], late_outer[e][:, block(k)])

        quantise(wd_w, wd_s[:], wd_bf[:])
        fetch_outer(LAST, 0, jump6[:])
        quantise_z(0, half(0))
        add_inner(LAST, half(0), jump7[:], jump6[:])
        for e in range(2):
            fetch_outer(LAST - 1 + e, 1, late_outer[e])
        last_products(0, *pieces[0])
        nc.gpsimd.tensor_tensor(slots[:, half(0), 3], jump7[:], stiff7[:], MULT)
        finish(0, 0, [nc.scalar.copy] * 4)
        z0_w.append(one("z0_late", [P, HALF], U32, "after_stiff7")[:])
        late_sum(0, 0)
        late_sum(1, 0)
        late_sum(0, 1)

        def late_first_pass(q):
            quantise_z(0, quarter(q))
            for piece in pieces[2 * q - 3 : 2 * q - 1]:
                last_products(0, *piece)

        late_first_pass(2)
        for k in range(BLOCKS):
            nc.vector.tensor_tensor(slots[:, pieces[k + 1][0], 2:4], late_jump[k].rearrange("p e m -> p m e"),
                                    late_stiff[:, :, block(k)].rearrange("p e m -> p m e"), MULT)
            if k + 1 < BLOCKS:
                late_sum(1, k + 1)
            finish(k + 1, BLOCKS + k, [nc.scalar.copy, nc.vector.tensor_copy])
            if k == 0:
                late_first_pass(3)
            if k + 2 < BLOCKS:
                late_sum(0, k + 2)
